import numpy as np, ml_dtypes
CORES = [10,34,74,98]
N = 4
BF = ml_dtypes.bfloat16
W, C, L, CAP, H, RO = 4096, 4, 256, 64, 2, 4
def ends(a):
    return np.arange(W).reshape(L, C, N)[:, a].reshape(-1)
def pairs(rng):
    o = np.argsort(rng.random((8, W)), axis=1); b = np.zeros((8, W), np.int64)
    np.put_along_axis(b, o, np.concatenate([o[:, W // 2:], o[:, :W // 2]], axis=1), 1)
    return b
def mix(rng, p, z):
    a, b = pairs(rng)[None, :, None], pairs(rng)[None, :, None]; u = rng.random((N, 8, 16, W), dtype=np.float32)
    return np.where(u < p, a, np.where(u < p + (1 - p) * 0.8, b, z))
def odds(rng):
    k = np.array([0.95, 0.75, 0.5, 0.3, 0.1])
    return np.where(rng.random((N, 8, 1, W)) < 0.25, rng.choice(k, (N, 8, 1, W)), rng.choice(k, (1, 8, 1, W)))
def anyone(rng):
    return rng.integers(0, W, (N, 8, 16, W))
def pack(m, x, t):
    return {"mt": np.ascontiguousarray(m.reshape(N, 128, W)).astype(np.int32), "xv": np.ascontiguousarray(x.reshape(N, 128, W)).astype(np.float32).astype(BF),
            "th": np.ascontiguousarray(t.reshape(N, 8, 1)).astype(np.int32)}
def put(o, v, i):
    e = int(np.nonzero(o == v)[0][0]); o[e] = o[i]; o[i] = v
def brim(rng, mg, h, less):
    mg[:] = rng.integers(0, W, mg.shape); k = np.arange(N); n = np.arange(8); j = np.arange(12)
    p = N * C * rng.permutation(L)[:, None] + k; w = N * C * rng.permutation(L)[:, None] + N + k; p2 = p + N * (2 % C)
    v = p[:CAP].reshape(-1); c = rng.permutation(w[:CAP].reshape(-1)); mg[:, :, v] = c; mg[:, :, c] = v
    if less: mg[:, :, int(c[-1])] = int(v[0])
    far = rng.permutation(p[CAP:CAP + 12].reshape(-1)).reshape(12, N)
    for r in range(N):
        q = (r + 1 + 1 % (N - 1)) % N; u, d = w[CAP:CAP + 12, r], far[:, r]; o = np.argsort(rng.random((16, 12)), axis=0)
        mg[r][:, u] = d; mg[r][:, d] = u; mg[q][:, d] = np.where(o < h - 16 + j % 4, u, (u + 1) % W)
        q = (r + 1 + 2 % (N - 1)) % N; z, y = p2[CAP + 12:CAP + 20, r], w[CAP + 12:CAP + 20, q]; o = np.argsort(rng.random((16, 8)), axis=0); e = n * N + (q + 1) % N
        mg[r][:, z] = y; mg[r][:, y] = z; mg[q][:, v[e]] = z
        mg[q][:, y] = np.where(o < np.where(n % 2 == 0, 16, h - 16 + n // 2), c[e], mg[q][:, y])
def setup_inputs(rng):
    return pack(mix(rng, odds(rng), anyone(rng)), rng.integers(0, 256, (N, 8, 16, W)), rng.integers(6, 33, (N, 8, 1)))
def setup_inputs_spread(rng):
    p = np.exp2(-5 * rng.random((N, 8, 1, W))); z = (W * rng.random((N, 8, 16, W)) ** 4).astype(np.int64)
    x = np.floor(np.exp2(8 * rng.random((N, 8, 1, W))) * rng.random((N, 8, 16, W))) * (rng.random((N, 8, 1, W)) > 0.0625)
    return pack(mix(rng, p, z), x, (33 * rng.random((N, 8, 1)) ** 2).astype(np.int64))
def setup_inputs_ends(rng):
    k = rng.integers(0, 4, (N, 8, 1, W)); m = np.where(k < 2, k, rng.integers(0, 2, (N, 8, 16, W))) * (W - 1)
    x = rng.integers(0, 2, (N, 8, 16, W)) * 255; k = rng.integers(0, 4, (N, 8, 1, W)); last = x[..., W - 1:].copy()
    x = np.where(k == 0, last, np.where(k == 1, 255 - last, x)); n = W // (10 * C)
    for g in range(8):
        pr = []; mg, xg = m[:, g], x[:, g]
        for a in range(C):
            o = rng.permutation(ends(a)); put(o, W - N * C + N * a + N - 1, n if a == C - 1 else 0)
            if a == C - 1: put(o, N * a, 2 * n)
            pr.append(o)
        for a in range(C):
            v, c, b = pr[a][:n], pr[a - 1][n:2 * n], pr[a - 1][2 * n:3 * n]; kind = rng.integers(0, 4, n); kind[0] = 0
            first = rng.random((N, 16, n)) < 0.5; first[:, 0, 0] = g % 2 == 1; first[:, 15] = ~first[:, 0]
            mg[:, :, v] = np.where(first, c, b); mg[:, :, c] = v; mg[:, :, b] = v
            xc = xg[:, :, c]
            xg[:, :, v] = np.where(kind == 1, 255 - xc, np.where(kind == 2, xg[:, :, v], xc)); xg[:, :, b] = np.where(kind == 3, 255 - xc, xc)
    t = 32 * rng.integers(0, 2, (N, 8, 1)); t[:, 0] = 0; t[:, 7] = 32
    return pack(m, x, t)
def setup_inputs_corners(rng):
    z = ends(0); m = np.where(rng.random((N, 8, 16, W), dtype=np.float32) < 0.6, z[rng.integers(0, len(z), (N, 8, 16, W))], anyone(rng))
    x = rng.choice(np.array([0, 1, 254, 255]), (N, 8, 16, W)); t = rng.choice(np.array([1, 2, 7, 16, 17, 31, 32]), (N, 8, 1)); off = int(rng.integers(0, 6))
    for g in range(8):
        w = rng.permutation(ends(1))
        for r in range(N):
            v = z[r::N]; c = w[r * L:r * L + L]; h = int(t[r, g, 0]); q = (r + 1) % N
            ok = np.zeros(L, bool); ok[rng.permutation(L)[:(0, 1, CAP - 1, CAP, CAP + 1, L)[(g + r + off) % 6]]] = True
            s = np.where(ok, rng.integers(h, 33, L), rng.integers(0, h, L)); s = np.where(rng.random(L) < 0.6, h - 1 + ok, s)
            own = rng.integers(np.maximum(s - 16, 0), np.minimum(s, 16) + 1); o = np.argsort(rng.random((2, 16, L)), axis=1)
            for b, e, n in ((r, 0, own), (q, 1, s - own)):
                y = m[b, g][:, c]; y = np.where(y == v, (v + N * C) % W, y); m[b, g][:, c] = np.where(o[e] < n, v, y)
            m[r, g][:, v] = c
    return pack(m, x, t)
def setup_inputs_crowd(rng):
    m = mix(rng, odds(rng), anyone(rng)); x = rng.integers(0, 256, (N, 8, 16, W)); t = rng.integers(6, 33, (N, 8, 1))
    for g, h in ((0, 0), (1, 0), (2, 0), (4, 32), (5, 30), (6, 1)):
        mg = m[:, g]; late = []; t[:, g] = h
        for a in range(C):
            v = ends(a); w = rng.permutation(ends((a + 1) % C)); f = w[:4 if g % 4 == 2 else 1]
            mg[:, :, v] = f[rng.integers(0, len(f), len(v))]
            if g % 4 == 1: mg[:, :, int(v[int(rng.integers(0, N * CAP))])] = int(w[9])
            if a < C - 1: late.append((f, np.append(v[-1:], rng.choice(v, len(f) - 1))))
        for f, v in late:
            mg[:, :, f] = v
            if g % 4 == 1: mg[:, 5, f] = (v + 1) % W
    for g in (3, 7):
        h = int(rng.integers(18, 28)); t[:, g] = h; brim(rng, m[:, g], h, g == 7)
    return pack(m, x, t)
def setup_inputs_ties(rng):
    m = mix(rng, rng.choice(np.array([0.4, 0.5, 0.6]), (1, 8, 1, W)), anyone(rng))
    x = rng.integers(0, 255, (N, 8, 16, 1)) + rng.integers(0, 2, (N, 8, 1, W)) * (np.arange(8) % 2).reshape(1, 8, 1, 1)
    return pack(m, x, rng.integers(8, 20, (N, 8, 1)))
def check_inputs(d):
    bad = []
    for k, lo, hi in (("mt", 0, W - 1), ("xv", 0, 255), ("th", 0, 32)):
        a = np.asarray(d[k]).astype(np.float64)
        if not (np.min(a) >= lo and np.max(a) <= hi and np.all(a == np.floor(a))): bad.append("range of " + k)
    return bad
def reference(mt, xv, th):
    M = mt.astype(np.int64).reshape(N, 8, 16, W); X = xv.astype(np.float32).astype(np.int64).reshape(N, 8, 16, W); T = th.astype(np.int64).reshape(N, 8, 1)
    pi = np.full((8, W), -1, np.int64); grp = np.arange(8).reshape(8, 1, 1); A = 0
    for t in range(RO):
        a = t % C; lanes, cand, has, cnt = [], [], [], []
        for r in range(N):
            v = N * C * np.arange(L) + N * a + r; alive = pi[:, v] < 0
            old = M[r][:, :, v]; m = old
            for h in range(H):
                p = pi[grp, m]; m = np.where(p >= 0, np.take_along_axis(M[r], np.maximum(p, 0), 2), m)
            M[r][:, :, v] = np.where(alive[:, None], m, old)
            ix = m.reshape(8, 1, 16 * L)
            n = np.sum(np.take_along_axis(M[r], ix, 2).reshape(8, 16, 16, L) == v, axis=1)
            D = np.sum(np.abs(np.take_along_axis(X[r], ix, 2).reshape(8, 16, 16, L) - X[r][:, :, v][:, :, None, :]), axis=1)
            may = alive[:, None] & (pi[grp, m] < 0) & (m // N % C != a)
            k = np.argmax(np.where(may, 4096 * n - D, -2 ** 20), axis=1)[:, None]
            lanes.append(v); has.append(np.any(may, axis=1)); cand.append(np.take_along_axis(m, k, 1)[:, 0]); cnt.append(np.take_along_axis(n, k, 1)[:, 0])
        yes = []
        for r in range(N):
            q = (r + 1 + t % (N - 1)) % N
            s = cnt[r] + np.sum(np.take_along_axis(M[q], cand[r][:, None, :], 2) == lanes[r], axis=1)
            y = has[r] & (s >= T[r] + (A & 3)); before = np.add.accumulate(y.astype(np.int64), axis=1) - y
            yes.append(y & (before < CAP))
        cc = np.concatenate(cand, axis=1); yy = np.concatenate(yes, axis=1); vv = np.concatenate(lanes)
        won = np.zeros((8, N * L), bool)
        for g in range(8):
            j = np.nonzero(yy[g])[0]; u, first = np.unique(cc[g, j], return_index=True); won[g, j[first]] = True
        for r in range(N):
            v = lanes[r]; lose = has[r] & ~won[:, r * L:r * L + L]; x = X[r][:, :, v]
            X[r][:, :, v] = np.where(lose[:, None], (x + np.take_along_axis(X[r], cand[r][:, None, :], 2)) >> 1, x)
        gg, jj = np.nonzero(won); pi[gg, vv[jj]] = cc[gg, jj]; pi[gg, cc[gg, jj]] = vv[jj]; A = int(np.sum(won))
    ym = np.stack([M[r].reshape(128, W)[:, r::N] for r in range(N)]); yx = np.stack([X[r].reshape(128, W)[:, r::N] for r in range(N)])
    return {"yp": np.stack([pi] * N).astype(np.float32), "ym": ym.astype(np.float32), "yx": yx.astype(np.float32).astype(BF)}

@@ -1,0 +1,580 @@
+from concourse.bass import DstId, RemoteDMATransfer
+from concourse.mybir import AluOpType as OP, AxisListType, ActivationFunctionType as AF
+
+W, RO, BIG, GW, SW = 4096, 4, 65536.0, 5120, 9216
+WHOLE = 12582912.0
+F32, BF, F16, I32, U16 = "float32", "bfloat16", "float16", "int32", "uint16"
+ACT_G1 = (1, 2, 3)
+ACT_G2 = ()
+WAIT_W = True
+SPLIT = 2
+TRIES, SLACK = 8000, 100.0
+PLAN = {}
+
+
+def _sb(n, d):
+    return ("sbuf", [128, n], d)
+
+
+SCRATCH = {
+    "Mi": _sb(W, I32), "Xb": _sb(W, BF), "Mf": _sb(GW, F32), "F": _sb(SW, F32), "Xs": _sb(SW, F32), "IO": _sb(GW, F32),
+    "VR": _sb(W, I32), "G": _sb(2048, F16), "Gf": _sb(2048, F32), "EQ": _sb(W, BF), "XG": _sb(2048, BF), "AB": _sb(2048, BF),
+    "D16": _sb(2048, F16), "D32": _sb(2048, F32), "SE": _sb(2048, BF), "SA": _sb(2048, BF), "YX": _sb(SW // 4, BF),
+    "s4": _sb(4, U16), "UO": _sb(4, U16), "XO": _sb(64, BF),
+    "FX32": _sb(512, F32), "FX16": _sb(512, F16), "I": _sb(128, BF), "NI": _sb(128, BF), "NL": _sb(128, BF), "NU": _sb(128, BF),
+    "ONE": _sb(128, BF), "I32": _sb(128, F32), "IR": _sb(256, F32),
+    "KH": _sb(128, F32), "KC": _sb(64, BF), "RS": _sb(256, F32), "RM": _sb(128, F32), "DMB": _sb(256, F32), "DM": _sb(256, F32),
+    "pidx": _sb(8, I32), "col": _sb(16, F32), "IOF": _sb(16, F32), "Q0": _sb(16, F32), "C2": _sb(4, F32), "Z16": _sb(16, F32),
+    "TH1": _sb(8, I32), "TH8": _sb(8, I32), "THF": _sb(8, F32),
+    "O0": _sb(256, U16), "OA": _sb(256, U16), "OB": _sb(256, U16), "M2": _sb(256, I32), "PEN": _sb(256, BF),
+    "LP": _sb(256, BF), "PT": _sb(256, F32), "P": _sb(256, F32), "NR": _sb(256, F32), "RP": _sb(256, F32), "CS": _sb(256, F16),
+    "O1": _sb(128, U16), "L1": _sb(128, U16), "LZ": _sb(128, U16),
+    "VV": _sb(256, F32), "E1": _sb(256, BF), "NF": _sb(16, F32), "PS": _sb(18, BF), "NP": _sb(16, F32), "QQ": _sb(16, F32),
+    "SN": _sb(16, F32), "SL": _sb(16, F32), "SO": _sb(16, U16), "CP": _sb(768, I32), "X2": _sb(128, I32), "MK": _sb(128, F32),
+    "SC": _sb(128, F32), "VC": _sb(4, F32), "OF": _sb(8, F32),
+    "BV": _sb(256, F32), "BC": _sb(256, F32), "MV": _sb(256, F32), "MC": _sb(256, F32), "VF": _sb(16, F32), "LO": _sb(256, F16),
+    "VO": _sb(16, U16), "CN": _sb(16, BF), "AI": _sb(4, I32),
+    "s1": _sb(16, F32), "s2": _sb(16, F32), "s3": _sb(16, F32), "SMO": _sb(16, U16), "SI": _sb(256, I32), "DL": _sb(256, F32), "AL": _sb(256, F32),
+    "pd0": ("psum", [128, 1024], F32), "pd1": ("psum", [128, 1024], F32), "pa": ("psum", [128, 512], F32),
+    "pb": ("psum", [128, 512], F32), "k0": ("psum", [128, 512], F32), "k1": ("psum", [128, 512], F32),
+}
+ALIAS = {"D0": ("RP", 128), "B": ("NR", 128), "J16": ("P", 256), "CL": ("SI", 256)}
+SEMAPHORES = (["cv", "cs", "cp", "cg", "sent", "lth", "lx", "oym", "oyx", "oyp"] + ["lm%d" % i for i in range(4)]
+              + ["a%d" % i for i in range(RO)] + ["e%d" % i for i in range(RO)] + ["b%d" % i for i in range(RO)])
+CYC, PEC, LAT, HOP1, HOP2 = 1.04, 0.52, 70.0, 3000.0, 3800.0
+
+
+def rank_program(g, core, T, topo):
+    r = T.rank_of(core)
+    if r is None:
+        return
+    N = len(T.cores)
+    ops = []
+    Q = {"v": g.vector, "s": g.scalar, "p": g.tensor, "g": g, "y": g.sync}
+    size = {F32: 4, I32: 4, BF: 2, F16: 2, U16: 2}
+
+    def R(name, lo=0, hi=None, step=None):
+        if name in ALIAS:
+            name, full = ALIAS[name]
+            hi = full if hi is None else hi
+        if hi is None:
+            hi = SCRATCH[name][1][1]
+        ap = T[name][:, lo:hi] if step is None else T[name][:, lo:hi:step]
+        n = hi - lo if step is None else (hi - lo + step - 1) // step
+        return {"ap": ap, "use": [(name, lo, hi)], "n": n, "ind": False, "name": name}
+
+    def IN(name, hi, off):
+        return {"ap": T[name][:, 0:hi].indirect(off["ap"]), "use": [(name, 0, hi)], "off": off["use"], "n": 16 * off["n"], "ind": True, "name": name}
+
+    def psum(x):
+        return SCRATCH[x["name"]][0] == "psum"
+
+    def op(eng, fn, outs, ins, cost, lat=0.0, sem=None, after=()):
+        wr, rd = [], []
+        for x in outs:
+            wr += x["use"]; rd += x.get("off", [])
+        for x in ins:
+            if isinstance(x, dict):
+                rd += x["use"] + x.get("off", [])
+        ops.append({"eng": eng, "fn": fn, "wr": wr, "rd": rd, "cost": cost, "lat": lat, "sem": sem, "after": list(after), "id": len(ops)})
+        return len(ops) - 1
+
+    def vcost(o, ins, two=False):
+        if o["ind"]:
+            return 50 + 3.8 * CYC * o["n"]
+        if ins[0]["ind"]:
+            return 50 + 1.56 * CYC * o["n"]
+        f = 0.5 if all(size[SCRATCH[x["name"]][2]] == 2 for x in [o] + ins) else 1.0
+        if two and not any(psum(x) for x in ins):
+            f *= 2
+        return 30 + CYC * max(64, f * o["n"])
+
+    def ap(x):
+        return x["ap"] if isinstance(x, dict) else x
+
+    def CP_(o, a):
+        return op("v", lambda: g.vector.tensor_copy(o["ap"], a["ap"]), [o], [a], vcost(o, [a]))
+
+    def TT(o, a, b, f):
+        return op("v", lambda: g.vector.tensor_tensor(o["ap"], a["ap"], b["ap"], f), [o], [a, b], vcost(o, [a, b], True))
+
+    def TS(o, a, s1, f1, s2=None, f2=None):
+        if f2 is None:
+            return op("v", lambda: g.vector.tensor_scalar(o["ap"], a["ap"], ap(s1), None, f1), [o], [a, s1], vcost(o, [a]))
+        return op("v", lambda: g.vector.tensor_scalar(o["ap"], a["ap"], ap(s1), ap(s2), f1, f2), [o], [a, s1, s2], vcost(o, [a]))
+
+    def SCAN(o, a, b, init, f0, f1):
+        return op("v", lambda: g.vector.tensor_tensor_scan(o["ap"], a["ap"], b["ap"], ap(init), f0, f1), [o], [a, b, init], vcost(o, [a, b]))
+
+    def TR(o, a):
+        return op("v", lambda: g.vector.transpose(o["ap"], a["ap"]), [o], [a], vcost(o, [a]))
+
+    def MS(o, val):
+        return op("v", lambda: g.vector.memset(o["ap"], val), [o], [], 30 + CYC * max(64, o["n"] * size[SCRATCH[o["name"]][2]] / 4))
+
+    def RED(o, a):
+        return op("v", lambda: g.vector.tensor_reduce(o["ap"], a["ap"], AxisListType.X, OP.add), [o], [a], 100)
+
+    def ACT(o, a, f, bias=0.0, scale=1.0):
+        c = 65 + 1.56 * CYC * o["n"] if a["ind"] else 40 + CYC * max(64, o["n"])
+        if o["ind"]:
+            return op("s", lambda: g.scalar.activation(o["ap"], a["ap"], f), [o], [a], 65 + 3.8 * CYC * o["n"])
+        return op("s", lambda: g.scalar.activation(o["ap"], a["ap"], f, bias=ap(bias), scale=ap(scale)), [o], [a, scale], c)
+
+    def MM(lst):
+        def fn():
+            for (o, l, x, s0, s1) in lst:
+                h = g.tensor.matmul(o["ap"], l["ap"], x["ap"], s0, s1)
+            return h
+        c = sum(PEC * max(64, x["n"]) * (4 if SCRATCH[x["name"]][2] == F32 else 1) for (o, l, x, s0, s1) in lst)
+        return op("p", fn, [m[0] for m in lst], [m[1] for m in lst] + [m[2] for m in lst], c + 40, lat=60)
+
+    def IOTA(o, pat, base, cm=0):
+        if SCRATCH[o["name"]][2] == I32:
+            return op("g", lambda: g.iota(o["ap"], pat, base, cm), [o], [], 130 + 2 * CYC * o["n"])
+        return op("g", lambda: g.iota(o["ap"], pat, base, cm, allow_small_or_imprecise_dtypes=True), [o], [], 130 + 2 * CYC * o["n"])
+
+    def DMA(q, out, in_, outs, ins, sem, lat):
+        return op(q, lambda: Q[q].dma_start(out, in_), outs, ins, 60, lat=lat, sem=(sem, 16))
+
+    def col(i):
+        return R("col", i, i + 1)
+
+    PM, PG, H0, H1, K15, THC, WC, AF_ = range(8)
+    lanes = lambda name, t, c0=0, c1=4: R(name, 1024 * c0 + 4 * t + r, 1024 * c1, 16)
+    voted = lambda t: (r - 1 - t % (N - 1)) % N
+    voter = lambda t: (r + 1 + t % (N - 1)) % N
+
+    j = DMA("y", T.Xb[:], T.xv[:], [R("Xb")], [], "lx", 7500)
+    for c in range(4):
+        k = DMA("y", T.Mi[:, 1024 * c:1024 * c + 1024], T.mt[:, 1024 * c:1024 * c + 1024], [R("Mi", 1024 * c, 1024 * c + 1024)], [], "lm%d" % c, 10200 + 2700 * c)
+        ops[k]["after"].append(j); j = k
+    IOTA(R("D0"), [[1, 128]], 0, -1)
+    IOTA(R("B"), [[1, 8], [0, 16]], 0)
+    IOTA(R("pidx", 0, 1), [[0, 1]], 0, 1)
+    IOTA(R("J16"), [[0, 16], [1, 16]], 0)
+    IOTA(R("IR"), [[1, 256]], 0)
+    op("g", lambda: g.dma_start(T.TH1[0:1, 0:8], T.th[:], allow_slow_non_contiguous=True), [R("TH1")], [], 1000, lat=3000, sem=("lth", 16))
+
+    def vrep(t, after=()):
+        for c in range(4):
+            j = IOTA(R("Mi" if t % 2 else "VR", 1024 * c, 1024 * c + 1024), [[16, 64], [0, 16]], 1024 * c + 4 * t + r)
+            ops[j]["after"] += list(after)
+    vrep(0)
+    op("g", lambda: g.partition_broadcast(T.TH8[:], T.TH1[0:1, 0:8], 128), [R("TH8")], [R("TH1")], 200)
+    for c in range(5):
+        IOTA(R("IO", 1024 * c, 1024 * c + 1024), [[1, 1024]], 1024 * c)
+    TS(R("pidx", 1, 2), R("pidx", 0, 1), 15, OP.bitwise_and); CP_(col(PM), R("pidx", 1, 2))
+    TS(R("pidx", 2, 3), R("pidx", 0, 1), 4, OP.arith_shift_right); CP_(col(PG), R("pidx", 2, 3))
+    TS(R("pidx", 3, 4), R("pidx", 0, 1), 16, OP.bitwise_and)
+    TS(col(H0), R("pidx", 3, 4), 0.0, OP.is_equal); TS(col(H1), R("pidx", 3, 4), 16.0, OP.is_equal)
+    TS(col(K15), col(PM), -1.0, OP.mult, 15.0, OP.add)
+    TS(R("I"), R("D0"), 0.0, OP.is_equal); TS(R("NI"), R("D0"), 0.0, OP.is_equal, -1.0, OP.mult); TS(R("I32"), R("D0"), 0.0, OP.is_equal)
+    TS(R("B"), R("B"), col(PG), OP.is_equal)
+    MS(R("ONE"), 1.0); MS(R("SE"), 0.0); MS(R("SA"), 0.0); MS(R("Z16"), 0.0); MS(R("PS"), 0.0)
+    for j in range(8):
+        TS(R("SE", 16 * j, 16 * j + 129 * 15 + 1, 129), R("ONE", 0, 16), R("B", 16 * j, 16 * j + 1), OP.mult, 65536.0, OP.mult)
+        TS(R("SA", 16 * j, 16 * j + 129 * 15 + 1, 129), R("ONE", 0, 16), R("B", 16 * j, 16 * j + 1), OP.mult, -16.0, OP.mult)
+    TS(R("KC"), R("ONE", 0, 64), col(K15), OP.mult)
+    TS(R("MK"), R("D0"), 0.0, OP.is_gt, -1.0, OP.mult); TT(R("NL"), R("MK"), R("B"), OP.mult)
+    TS(R("SC"), R("D0"), 0.0, OP.is_le, -1.0, OP.mult); TT(R("NU"), R("SC"), R("B"), OP.mult)
+    TS(R("KH"), R("J16", 0, 128), col(PM), OP.is_equal)
+    TS(R("RS"), R("J16"), 0.0, OP.is_equal, -1.0e9, OP.mult); TS(R("RM"), R("J16", 0, 128), 0.0, OP.not_equal)
+    TS(R("IOF"), R("IR", 0, 16), 16.0, OP.mult, col(PM), OP.add); TS(R("Q0"), R("IOF"), 256.0, OP.add)
+    TS(R("C2"), R("IOF", 0, 4), 16.0, OP.mult, 1.0e6 + W, OP.add)
+    for s in range(4):
+        TS(R("DMB", 64 * s, 64 * s + 64), R("IR", 0, 64), R("IOF", s, s + 1), OP.is_gt, R("C2", s, s + 1), OP.mult)
+    for h in range(2):
+        for q in range(2):
+            for nm in ("FX32", "FX16"):
+                TS(R(nm, 256 * h + 128 * q, 256 * h + 128 * q + 128), R("D0"), 16.0 * (q - h), OP.is_equal, col(H0 + h), OP.mult)
+    for k in range(16):
+        TS(R("D16", 128 * k, 128 * k + 128), R("I32"), R("KH", k, k + 1), OP.mult)
+        ACT(R("D32", 128 * k, 128 * k + 128), R("I32"), AF.Identity, scale=R("KH", k, k + 1))
+    TT(R("THF"), R("TH8"), R("B", 0, 128, 16), OP.mult); RED(col(THC), R("THF"))
+    TS(col(THC), col(THC), 1.0 / 1024, OP.add); TS(col(WC), col(THC), 256.0, OP.mult)
+    for c in range(2):
+        IOTA(R("Mf", W + 512 * c, W + 512 * c + 512), [[0, 512]], 0)
+    for c in range(8):
+        ACT(R("Xs", 512 * c, 512 * c + 512), R("Xb", 512 * c, 512 * c + 512), AF.Identity)
+        CP_(R("Mf", 512 * c, 512 * c + 512), R("Mi", 512 * c, 512 * c + 512))
+    for c in range(5):
+        ACT(R("F", 1024 * c, 1024 * c + 1024), R("IO", 1024 * c, 1024 * c + 1024), AF.Identity)
+
+    nsent = [0]
+    marks = []
+
+    def ch(name, c, w=64):
+        return R(name, w * c, w * c + w)
+
+    def follow(c, src, dst, by_act, last):
+        pm = R((("pa", "pb") if last else ("k0", "k1"))[c % 2], 0, 64)
+        b = 1024 * (c % 2)
+        if by_act:
+            ACT(R("Gf", b, b + 1024), IN("F", W, ch(src, c)), AF.Identity, bias=-2048.0)
+            MM([(pm, ch("D32", k, 128), R("Gf", b + k, b + 1024, 16), k == 0, k == 15) for k in range(16)])
+        else:
+            TS(R("G", b, b + 1024), IN("F", W, ch(src, c)), -2048.0, OP.add)
+            MM([(pm, ch("D16", k, 128), R("G", b + k, b + 1024, 16), k == 0, k == 15) for k in range(16)])
+        TS(ch(dst, c), pm, 2048.0, OP.add)
+        if last:
+            TS(ch("M2", c), pm, 2048.0, OP.add)
+            TR(ch("PT", c), pm)
+
+    def score(t, c):
+        b = 1024 * (c % 2); pd = "pd%d" % (c % 2)
+        m2 = lanes("Mi", 0, c, c + 1) if t == 0 else ch("M2", c)
+        TS(ch("CL", c), m2, 12, OP.bitwise_and)
+        TS(ch("PEN", c), ch("CL", c), 4.0 * t, OP.is_equal, -8388608.0, OP.mult)
+        ACT(R("XG", b, b + 1024), IN("Xb" if t == 0 else "Xs", W, ch("OB", c)), AF.Identity)
+        for hf in range(2):
+            ks = range(8 * hf, 8 * hf + 8)
+            MM([(ch(pd, k), R("NI"), lanes("Xb", t, c, c + 1), k == ks[0], False) for k in ks])
+            MM([(ch(pd, k), R("I"), R("XG", b + k, b + 1024, 16), False, k == ks[-1]) for k in ks])
+            ACT(R("AB", b + 512 * hf, b + 512 * hf + 512), ch(pd, hf, 512), AF.Abs)
+        TT(ch("EQ", c, 1024), IN("Mi" if t == 0 else "Mf", W, ch("OB", c)), ch("Mi" if t % 2 else "VR", c, 1024), OP.is_equal)
+        key = ch("k0" if c < SPLIT else "k1", c)
+        l0 = [(key, R("I"), R("KC"), c in (0, SPLIT), False), (key, R("I"), ch("PEN", c), False, False)]
+        if t:
+            l0.append((key, R("NI"), ch("LP", c), False, False))
+        l2 = [(key, ch("SA", k, 128), R("AB", b + 64 * k, b + 64 * k + 64), False, False) for k in range(16)]
+        MM(l2[:8] if c not in (0, SPLIT) else l0[:1] + l2[:8]); MM(l2[8:]); MM(l0[1:] if c in (0, SPLIT) else l0)
+        if c in (SPLIT - 1, 3):
+            for d in range(SPLIT if c == 3 else 0, c + 1):
+                MM([(ch("k0" if c < SPLIT else "k1", d), ch("SE", k, 128), R("EQ", 1024 * d + k, 1024 * d + 1024, 16), False, d == c and k == 15) for k in range(16)])
+
+    def choose(t, lo, hi):
+        m0 = 32 * t + lo // 8; m1 = m0 + (hi - lo) // 16; m2 = m1 + (hi - lo) // 16
+        TR(R("pa", lo, hi), R("k1" if lo else "k0", lo, hi))
+        SCAN(R("P", lo, hi), R("RS", lo, hi), R("pa", lo, hi), -2.0e9, OP.add, OP.max)
+        TT(R("pb", lo, hi), R("pa", lo, hi), R("P", lo, hi), OP.is_ge)
+        TT(R("NR", lo, hi), R("pa", lo, hi), R("P", lo, hi), OP.is_lt)
+        s0, s1 = lo // 16, hi // 16
+        MM([(R("pd0", s0 + h, s1, 2), ch("FX32", 2 * h + q, 128), R("P", lo + 15 + 16 * q, hi, 32), q == 0, q == 1) for h in range(2) for q in range(2)])
+        TT(R("RP", lo, hi), R("pb", lo, hi), R("PT", lo, hi), OP.mult)
+        SCAN(R("CS", lo, hi), R("NR", lo, hi), R("RP", lo, hi), 0.0, OP.mult, OP.add)
+        TS(R("O1", m1, m2), R("pd0", s0, s1), -1.0 / 256, OP.mult, col(WC), OP.add)
+        MM([(R("pd0", 512 + s0 + h, 512 + s1, 2), ch("FX16", 2 * h + q, 128), R("CS", lo + 15 + 16 * q, hi, 32), q == 0, q == 1) for h in range(2) for q in range(2)])
+        TS(R("O1", m0, m1), R("pd0", 512 + s0, 512 + s1), 2048.0, OP.add)
+        dst = T.cores[voter(t)]; rid, pid, _se = topo.addr(dst); sem = ("a%d" if lo else "e%d") % t
+        o1 = R("O1", m0, m2); l1 = R("L1", m0, m2)
+        s = op("g", lambda: g.remote_dma(l1["ap"], o1["ap"], T.sem[sem], T.sem.sent, pid, rid, topo.mask(core, dst)), [], [o1], 500, sem="remote")
+        nsent[0] += len(topo.engines(core, dst))
+        op(None, None, [l1], [], 0, lat=HOP1, sem=(sem, len(topo.engines(T.cores[voted(t)], core))), after=[s])
+
+    def vote(t, lo, hi):
+        m0 = 32 * t + lo // 8; m1 = m0 + (hi - lo) // 16; m2 = m1 + (hi - lo) // 16
+        s0, s1 = lo // 16, hi // 16
+        co = R("L1", m0, m1)
+        TT(R("E1", lo, hi), IN("Mi" if t == 0 else "Mf", W, co), R("VV", lo, hi), OP.is_equal)
+        TS(R("NF", s0, s1), R("L1", m1, m2), -255.0, OP.add, 256.0, OP.mult)
+        ACT(R("BC", lo, hi), IN("IO", W, co), AF.Identity, scale=512.0)
+        MM([(R("k0", s0, s1), ch("SE", k, 128), R("E1", lo + k, hi, 16), k == 0, k == 15) for k in range(16)])
+        TT(R("BV", lo, hi), R("BC", lo, hi), R("IR", lo, hi), OP.add)
+        TT(R("PS", s0 + 1, s1 + 1), R("k0", s0, s1), R("NF", s0, s1), OP.is_ge)
+        TT(R("NP", s0, s1), R("k0", s0, s1), R("NF", s0, s1), OP.is_lt)
+        MM([(R("k1", s0, s1), R("NL"), R("PS", s0 + 1, s1 + 1), True, False), (R("k1", s0, s1), R("NU"), R("PS", s0, s1), False, True)])
+        TT(R("QQ", s0, s1), R("NP", s0, s1), R("Q0", s0, s1), OP.mult)
+        SCAN(R("SN", s0, s1), R("k1", s0, s1), R("Z16", s0, s1), R("SN", s0 - 1, s0) if lo else 767.0, OP.add, OP.add)
+        TT(R("SL", s0, s1), R("SN", s0, s1), R("QQ", s0, s1), OP.subtract)
+        CP_(R("SO", s0, s1), R("SL", s0, s1))
+        CP_(IN("CP", 768, R("SO", s0, s1)), R("BV", lo, hi))
+
+    for t in range(RO):
+        rho = voted(t); base = 4 * t + rho
+        if t == 0:
+            for c in range(4):
+                CP_(ch("OB", c), lanes("Mi", 0, c, c + 1))
+                TS(ch("RP", c), lanes("Mi", 0, c, c + 1), -2048.0, OP.add)
+                TR(ch("PT", c), ch("RP", c))
+        else:
+            order = [(0, 0), (1, 0), (0, 1), (2, 0), (1, 1), (3, 0), (2, 1), (3, 1)]
+            for c, step in order:
+                if step == 0:
+                    follow(c, "O0", "OA", c in ACT_G1, False)
+                else:
+                    follow(c, "OA", "OB", c in ACT_G2, True)
+        TS(R("VV"), R("IR"), 16.0, OP.mult, float(base), OP.add)
+        TS(R("CP", 704, 768), R("IR", 0, 64), 8193.0, OP.mult, 512.0 * (W + base) + 256, OP.add)
+        TS(R("DM"), R("DMB"), base - 1.0e6, OP.add, 0.0, OP.max)
+        for c in range(4):
+            score(t, c)
+            if c == SPLIT - 1:
+                choose(t, 0, 64 * SPLIT)
+        choose(t, 64 * SPLIT, 256)
+        if t + 1 < RO:
+            CP_(R("O0"), lanes("Mf", t + 1))
+        vote(t, 0, 64 * SPLIT)
+        vote(t, 64 * SPLIT, 256)
+        TS(R("X2", 0, 64), R("CP", 704, 768), 9, OP.arith_shift_right)
+        TS(R("X2", 64, 128), R("CP", 704, 768), 511, OP.bitwise_and)
+        for hf in range(2):
+            TT(ch("MK", hf), ch("X2", hf), ch("KH", 0), OP.mult)
+            SCAN(ch("SC", hf), ch("RM", 0), ch("MK", hf), 0.0, OP.mult, OP.add)
+        for s4 in range(4):
+            TS(ch("NR", s4), R("X2", 0, 64), R("SC", 16 * s4 + 15, 16 * s4 + 16), OP.is_equal, 8192.0, OP.mult)
+        TS(R("VC"), R("SC", 79, 128, 16), 16.0, OP.mult, float(base), OP.add)
+        SCAN(R("P"), R("NR"), R("DM"), 0.0, OP.max, OP.min)
+        TT(R("OF", 0, 4), R("SC", 15, 64, 16), R("P", 63, 256, 64), OP.max)
+        TT(R("OF", 4, 8), R("VC"), R("P", 63, 256, 64), OP.max)
+        lz = lambda q, lo, hi, t=t: R("LZ", 32 * t + 8 * q + lo, 32 * t + 8 * q + hi)
+        CP_(lz(rho, 0, 8), R("OF"))
+        others = [T.cores[(r + d) % N] for d in range(1, N)]
+        others.sort(key=lambda x: topo.same_plane(topo.chip(core), topo.chip(x)))
+        msk = topo.mask(core, others[0])
+        for x in others:
+            msk &= topo.mask(core, x)
+        ne = bin(msk).count("1")
+        tr = RemoteDMATransfer(dst_ids=[DstId(rid=topo.addr(x)[0], pnc=topo.addr(x)[1]) for x in others], dma_engine_mask=msk,
+                               remote_sem=T.sem["b%d" % t], src=lz(rho, 0, 8)["ap"], dsts=[lz(rho, 0, 8)["ap"] for x in others])
+        s = op("g", lambda tr=tr: g.remote_dma_fused([tr], local_sem=T.sem.sent), [], [lz(rho, 0, 8)], 500, sem="remote")
+        nsent[0] += ne; marks.append(s)
+        op(None, None, [lz(q, 0, 8) for q in range(N) if q != rho], [], 0, lat=HOP2, sem=("b%d" % t, ne * (N - 1)), after=[s])
+        for s0, s1 in ((0, 4 * SPLIT), (4 * SPLIT, 16)):
+            TS(R("s1", s0, s1), R("O1", 32 * t + s0 + s1, 32 * t + 2 * s1), 12000.0, OP.is_lt)
+            CP_(R("s3", s0, s1), R("O1", 32 * t + 2 * s0, 32 * t + s0 + s1))
+        TS(R("s2"), R("IOF"), 16.0, OP.mult, float(4 * t + r), OP.add)
+        TT(R("s3"), R("s3"), R("s2"), OP.subtract); TT(R("s3"), R("s3"), R("s1"), OP.mult); TT(R("s3"), R("s3"), R("s2"), OP.add)
+        CP_(R("SMO"), R("s3"))
+        ACT(R("MC"), IN("Xs" if t else "Xb", W, R("SMO")), AF.Identity)
+        TT(R("DL"), R("MC"), lanes("Xs" if t else "Xb", t), OP.add)
+        TS(R("SI"), R("DL"), 0.5, OP.mult, -0.25, OP.add)
+        if t == 0:
+            CP_(R("YX", t, 1024, 4), R("SI"))
+        else:
+            TS(R("AL"), lanes("Xs", t), 256.0, OP.is_lt)
+            TT(R("DL"), R("SI"), lanes("Xb", t), OP.subtract); TT(R("DL"), R("DL"), R("AL"), OP.mult)
+            TT(R("YX", t, 1024, 4), R("DL"), lanes("Xb", t), OP.add)
+            TT(R("RP"), R("M2"), lanes("Mf", t), OP.subtract); TT(R("RP"), R("RP"), R("AL"), OP.mult)
+            TT(lanes("Mf", t), R("RP"), lanes("Mf", t), OP.add)
+        last = t == RO - 1
+        if not last:
+            CP_(lanes("Xs", t), R("SI"))
+            vrep(t + 1, [s])
+        else:
+            ACT(R("Gf", 0, 1024), R("Mf", r, W, 4), AF.Identity)
+            DMA("y", T.ym[:], T.Gf[:, 0:1024], [], [R("Gf", 0, 1024)], "oym", 4000)
+            for c in range(8):
+                ACT(ch("F", c, 512), ch("Xs", c, 512), AF.Identity, bias=WHOLE - BIG)
+                if c < 5:
+                    ACT(ch("F", c, 512), ch("F", c, 512), AF.Relu, bias=1.0 - WHOLE)
+                    ACT(ch("F", c, 512), ch("F", c, 512), AF.Identity, bias=-1.0)
+                else:
+                    TS(ch("F", c, 512), ch("F", c, 512), -WHOLE, OP.add, -1.0, OP.max)
+        add = 0.0 if last else BIG
+        val = "BV" if last else "MV"
+        for q in range(N - 1, -1, -1):
+            if not last:
+                ACT(ch("MV", q), IN("Mf", GW, lz(q, 4, 8)), AF.Identity, bias=q / 16.0)
+            ACT(ch("BV", q), IN("IO", GW, lz(q, 4, 8)), AF.Identity, bias=add)
+            TS(ch("VF", q, 4), lz(q, 4, 8), 1.0 / GW, OP.mult)
+        for q in range(N - 1, -1, -1):
+            CP_(IN("F", GW, lz(q, 0, 4)), ch(val, q))
+        for q in range(N):
+            if not last:
+                ACT(ch("MC", q), IN("Mf", GW, lz(q, 0, 4)), AF.Identity)
+            ACT(ch("BC", q), IN("IO", GW, lz(q, 0, 4)), AF.Identity, bias=add)
+        for q in range(1, N):
+            TT(ch("LO", q), IN("F", GW, lz(q, 0, 4)), ch(val, q), OP.not_equal)
+        MM([(R("pa", 0, 16), R("I32"), R("VF"), True, False)])
+        MM([(R("pa", 4, 16), ch("D16", k, 128), R("LO", 64 + k, 256, 16), False, k == 15) for k in range(16)])
+        vval = "BC" if last else "MC"
+        CP_(IN("F", GW, lz(0, 4, 8)), ch(vval, 0))
+        TS(R("VO"), R("pa", 0, 16), float(GW), OP.mult, 0.25, OP.add)
+        CP_(IN("F", SW, R("VO", 4, 16)), R(vval, 64, 256))
+        TS(R("s4"), lz(r, 4, 8), float(W - 1), OP.min)
+        ACT(R("XO"), IN("Xb", W, R("s4")), AF.Identity)
+        TS(R("UO"), R("pa", 4 * r, 4 * r + 4), GW / 4.0, OP.mult, 0.1 - r / 4.0, OP.add)
+        CP_(IN("YX", SW // 4, R("UO")), R("XO"))
+        if not last:
+            for q in range(N - 1, -1, -1):
+                ACT(IN("Xs", GW, lz(q, 0, 4)), ch("BV", q), AF.Silu)
+            ACT(R("LP"), lanes("Xs", t + 1), AF.Relu, bias=-255.0 * 128, scale=128.0)
+            ACT(IN("Xs", SW, R("VO")), R("BC"), AF.Silu)
+            TS(R("CN"), R("VO"), 4096.0, OP.is_lt)
+            MM([(R("pb", 0, 16), R("ONE"), R("CN"), True, True)])
+            RED(col(AF_), R("pb", 0, 16))
+            CP_(R("AI", 0, 1), col(AF_)); TS(R("AI", 1, 2), R("AI", 0, 1), 3, OP.bitwise_and)
+            TS(col(WC), R("AI", 1, 2), col(THC), OP.add, 256.0, OP.mult)
+        else:
+            DMA("y", T.yp[:], T.F[0:128:16, 0:W], [], [R("F", 0, W)], "oyp", 2800)
+            DMA("s", T.yx[:], T.YX[:, 0:1024], [], [R("YX", 0, 1024)], "oyx", 3400)
+
+    emit(g, T, Q, ops, nsent[0], marks)
+
+
+def emit(g, T, Q, ops, nsent, marks):
+    def meet(a, b, banks):
+        for (n, lo, hi) in a:
+            for (m, l2, h2) in b:
+                if n == m:
+                    if banks and SCRATCH[n][0] == "psum":
+                        if lo // 512 <= (h2 - 1) // 512 and l2 // 512 <= (hi - 1) // 512:
+                            return True
+                    elif not banks and lo < h2 and l2 < hi:
+                        return True
+        return False
+    by = {}
+    for o in ops:
+        o["dep"] = {}
+        names = set(x[0] for x in o["wr"] + o["rd"])
+        seen = set()
+        for nm in names:
+            seen.update(by.get(nm, []))
+            by.setdefault(nm, []).append(o["id"])
+        for j in seen:
+            e = ops[j]; same = e["eng"] == o["eng"] and e["sem"] is None and o["sem"] is None
+            raw = meet(e["wr"], o["rd"], False)
+            war = meet(e["rd"], o["wr"], False) or meet(e["wr"], o["wr"], False)
+            if same:
+                if raw or war or (o["eng"] == "p" and meet(e["wr"], o["wr"], True)):
+                    o["dep"][j] = o["eng"] != "p" and (raw or WAIT_W)
+            elif raw or war or meet(e["wr"] + e["rd"], o["wr"] + o["rd"], True):
+                o["dep"][j] = True
+        for j in o["after"]:
+            o["dep"][j] = False
+    n = len(ops)
+    succ = [[] for _ in range(n)]
+    for o in ops:
+        for j in o["dep"]:
+            succ[j].append(o["id"])
+
+    def gap(j, o):
+        return ops[j]["lat"] + LAT if o["dep"][j] or o["eng"] is None else 0.0
+    anc = [0] * n; gp = []; nxt = [[] for _ in range(n)]
+    for o in ops:
+        far = 0
+        for j in o["dep"]:
+            far |= anc[j]
+        gp.append([(j, ops[j]["cost"] + gap(j, o)) for j in o["dep"] if not far >> j & 1])
+        for j in o["dep"]:
+            far |= 1 << j
+        anc[o["id"]] = far
+        for j, w in gp[-1]:
+            nxt[j].append((o["id"], o["cost"] + gap(j, o)))
+
+    def place(seq, back):
+        busy = {}
+        st = [0.0] * n
+        for i in seq:
+            o = ops[i]
+            t0 = o["lat"] if back else 0.0
+            for j, w in (nxt[i] if back else gp[i]):
+                if st[j] + w > t0:
+                    t0 = st[j] + w
+            if o["eng"] is not None:
+                lst = busy.setdefault(o["eng"], [])
+                lo, hi = 0, len(lst)
+                while lo < hi:
+                    mid = (lo + hi) // 2
+                    if lst[mid][1] <= t0:
+                        lo = mid + 1
+                    else:
+                        hi = mid
+                while lo < len(lst) and t0 + o["cost"] > lst[lo][0]:
+                    t0 = max(t0, lst[lo][1]); lo += 1
+                lst.insert(lo, (t0, t0 + o["cost"]))
+            st[i] = t0
+        return st
+    up = [0.0] * n
+    for i in range(n - 1, -1, -1):
+        up[i] = ops[i]["cost"] + max([w - ops[k]["cost"] + up[k] for k, w in nxt[i]] + [ops[i]["lat"]]) + 1e-3
+    seq = sorted(range(n), key=lambda i: (-up[i], i))
+    best = None
+    rnd = [12345]
+
+    def rand():
+        rnd[0] = (rnd[0] * 1103515245 + 12345) % 2147483648
+        return rnd[0] / 2147483648
+
+    def moved(key, picks):
+        kk = list(key)
+        for i, d in picks:
+            kk[i] += d
+            todo = [i]
+            while todo:
+                x = todo.pop()
+                for j, w in (gp[x] if d < 0 else nxt[x]):
+                    if (kk[j] >= kk[x]) if d < 0 else (kk[j] <= kk[x]):
+                        kk[j] = kk[x] + (-1e-3 if d < 0 else 1e-3); todo.append(j)
+        for i in range(n):
+            for j, w in gp[i]:
+                if kk[j] >= kk[i]:
+                    kk[i] = kk[j] + 1e-3
+        return sorted(range(n), key=lambda i: (kk[i], i))
+    big = [i for i in range(n) if ops[i]["cost"] > 200]
+
+    def length(st):
+        return max(st[i] + ops[i]["cost"] + ops[i]["lat"] for i in range(n))
+    first = "key" not in PLAN
+    if not first:
+        seq = moved(PLAN["key"], [])
+    cur = place(seq, False)
+    best = (length(cur), cur)
+
+    def parts(st):
+        m = [0.0] + [st[i] for i in marks] + [length(st)]
+        return m, [m[k + 1] - m[k] for k in range(len(m) - 1)]
+    tries = TRIES if first else TRIES // 10
+    for it in range(tries):
+        slack = SLACK * (1.0 - it / tries)
+        m, old = parts(cur)
+        if it % 40 == 0:
+            bk = place(sorted(range(n), key=lambda i: (-(cur[i] + ops[i]["cost"]), -i)), True)
+            st = place(moved([-bk[i] - ops[i]["cost"] for i in range(n)], []), False)
+        else:
+            picks = [(big[int(rand() * len(big))], (rand() - 0.5) * 6000.0 * rand()) for _ in range(8)]
+            st = place(moved(cur, picks), False)
+            new = parts(st)[1]
+            good = [(i, d) for i, d in picks if any(m[k] <= cur[i] < m[k + 1] and new[k] <= old[k] + slack for k in range(len(old)))]
+            if not good:
+                continue
+            if len(good) < len(picks):
+                st = place(moved(cur, good), False)
+        span = length(st)
+        if span <= m[-1] + slack:
+            cur = st
+        if span < best[0]:
+            best = (span, st)
+    PLAN["key"] = best[1]; PLAN["span"] = best[0]
+    start = best[1]
+    end = [start[i] + ops[i]["cost"] for i in range(n)]
+    order = sorted(range(n), key=lambda i: (start[i], i))
+    cnt = {"v": 0, "s": 0, "p": 0, "g": 0}
+    for i in order:
+        o = ops[i]
+        o["inc"] = o["sem"] is None and any(ops[k]["dep"][i] for k in succ[i])
+        if o["sem"] is None:
+            cnt[o["eng"]] += o["inc"]
+            o["sig"] = ("c" + o["eng"], cnt[o["eng"]])
+        else:
+            o["sig"] = o["sem"]
+    known = {e: {} for e in Q}
+    for i in order:
+        o = ops[i]
+        if o["eng"] is None:
+            o["kn"] = {}
+            continue
+        kn = known[o["eng"]]
+        need = sorted((j for j, w in o["dep"].items() if w), key=lambda j: -end[j])
+        for j in need:
+            sm, val = ops[j]["sig"]
+            if kn.get(sm, 0) < val:
+                Q[o["eng"]].wait_ge(T.sem[sm], int(val)); kn[sm] = val
+                for s2, v2 in ops[j]["kn"].items():
+                    kn[s2] = max(kn.get(s2, 0), v2)
+        o["kn"] = dict(kn)
+        h = o["fn"]()
+        if o["sem"] is None:
+            if o["inc"]:
+                h.then_inc(T.sem[o["sig"][0]], 1)
+        elif o["sem"] != "remote":
+            h.then_inc(T.sem[o["sem"][0]], 16)
+    for e in cnt:
+        if cnt[e]:
+            g.wait_ge(T.sem["c" + e], int(cnt[e]))
+    for o in ops:
+        if o["sem"] not in (None, "remote"):
+            g.wait_ge(T.sem[o["sem"][0]], int(o["sem"][1]))
+    g.wait_ge(T.sem.sent, int(nsent))
+    return max(end[i] + ops[i]["lat"] for i in range(n))

@@ -1,13 +1,15 @@
 from concourse.bass import DstId, RemoteDMATransfer
 from concourse.mybir import AluOpType as OP, AxisListType, ActivationFunctionType as AF
 
-W, RO, BIG, GW, SW = 4096, 4, 65536.0, 5120, 9216
+W, RO, BIG, GW, SW = 4096, 4, 65536.0, 4624, 8720
+HI, UP = 8192.0, 32.0
 WHOLE = 12582912.0
 F32, BF, F16, I32, U16 = "float32", "bfloat16", "float16", "int32", "uint16"
-ACT_G1 = (1, 2, 3)
+ACT_G1 = (2, 3)
 ACT_G2 = ()
 WAIT_W = True
-SPLIT = 2
+SPLIT = 0
+LOAD = (6000.0, 2200.0)
 TRIES, SLACK = 8000, 100.0
 PLAN = {}
 
@@ -18,28 +20,29 @@ def _sb(n, d):
 
 SCRATCH = {
     "Mi": _sb(W, I32), "Xb": _sb(W, BF), "Mf": _sb(GW, F32), "F": _sb(SW, F32), "Xs": _sb(SW, F32), "IO": _sb(GW, F32),
-    "VR": _sb(W, I32), "G": _sb(2048, F16), "Gf": _sb(2048, F32), "EQ": _sb(W, BF), "XG": _sb(2048, BF), "AB": _sb(2048, BF),
-    "D16": _sb(2048, F16), "D32": _sb(2048, F32), "SE": _sb(2048, BF), "SA": _sb(2048, BF), "YX": _sb(SW // 4, BF),
+    "VR": _sb(W, I32), "G": _sb(2048, F16), "Gf": _sb(2048, F32), "EQ": _sb(2048, BF), "XG": _sb(2048, BF), "AB": _sb(2048, BF),
+    "D16": _sb(2048, F16), "D32": _sb(2048, F32), "SE": _sb(144, BF), "SA": _sb(144, BF), "YX": _sb(SW // 4, BF), "YM": _sb(1024, F32),
     "s4": _sb(4, U16), "UO": _sb(4, U16), "XO": _sb(64, BF),
-    "FX32": _sb(512, F32), "FX16": _sb(512, F16), "I": _sb(128, BF), "NI": _sb(128, BF), "NL": _sb(128, BF), "NU": _sb(128, BF),
-    "ONE": _sb(128, BF), "I32": _sb(128, F32), "IR": _sb(256, F32),
-    "KH": _sb(128, F32), "KC": _sb(64, BF), "RS": _sb(256, F32), "RM": _sb(128, F32), "DMB": _sb(256, F32), "DM": _sb(256, F32),
-    "pidx": _sb(8, I32), "col": _sb(16, F32), "IOF": _sb(16, F32), "Q0": _sb(16, F32), "C2": _sb(4, F32), "Z16": _sb(16, F32),
+    "FX32": _sb(512, F32), "I": _sb(128, BF), "NI": _sb(128, BF), "NL": _sb(128, BF), "NU": _sb(128, BF),
+    "ONE": _sb(128, BF), "I32": _sb(128, F32), "NI32": _sb(128, F32), "ONE32": _sb(128, F32), "SH": _sb(128, F32), "IR": _sb(256, F32),
+    "KH": _sb(128, F32), "KC": _sb(64, BF), "RS": _sb(256, F32), "RM": _sb(128, F32), "DM": _sb(256, F32),
+    "pidx": _sb(8, I32), "col": _sb(16, F32), "IOF": _sb(16, F32), "Q0": _sb(16, F32), "C2": _sb(4, F32), "Z16": _sb(16, F32), "DC": _sb(16, F32),
     "TH1": _sb(8, I32), "TH8": _sb(8, I32), "THF": _sb(8, F32),
-    "O0": _sb(256, U16), "OA": _sb(256, U16), "OB": _sb(256, U16), "M2": _sb(256, I32), "PEN": _sb(256, BF),
-    "LP": _sb(256, BF), "PT": _sb(256, F32), "P": _sb(256, F32), "NR": _sb(256, F32), "RP": _sb(256, F32), "CS": _sb(256, F16),
+    "O0": _sb(768, U16), "OA": _sb(256, U16), "OB": _sb(256, U16), "M2": _sb(256, F32), "PEN": _sb(256, BF),
+    "LP": _sb(256, BF), "PT": _sb(256, F32), "P": _sb(256, F32), "NR": _sb(256, F32), "U": _sb(256, F32),
     "O1": _sb(128, U16), "L1": _sb(128, U16), "LZ": _sb(128, U16),
-    "VV": _sb(256, F32), "E1": _sb(256, BF), "NF": _sb(16, F32), "PS": _sb(18, BF), "NP": _sb(16, F32), "QQ": _sb(16, F32),
-    "SN": _sb(16, F32), "SL": _sb(16, F32), "SO": _sb(16, U16), "CP": _sb(768, I32), "X2": _sb(128, I32), "MK": _sb(128, F32),
-    "SC": _sb(128, F32), "VC": _sb(4, F32), "OF": _sb(8, F32),
-    "BV": _sb(256, F32), "BC": _sb(256, F32), "MV": _sb(256, F32), "MC": _sb(256, F32), "VF": _sb(16, F32), "LO": _sb(256, F16),
-    "VO": _sb(16, U16), "CN": _sb(16, BF), "AI": _sb(4, I32),
-    "s1": _sb(16, F32), "s2": _sb(16, F32), "s3": _sb(16, F32), "SMO": _sb(16, U16), "SI": _sb(256, I32), "DL": _sb(256, F32), "AL": _sb(256, F32),
+    "VV": _sb(256, F32), "VU": _sb(256, F32), "E1": _sb(256, BF), "NF": _sb(16, F32), "PS": _sb(18, BF), "NP": _sb(16, F32), "QQ": _sb(16, F32),
+    "SN": _sb(16, F32), "SL": _sb(16, F32), "SO": _sb(16, U16), "CC": _sb(768, F32), "CV": _sb(768, F32), "MK": _sb(128, F32),
+    "SC": _sb(128, F32), "OF": _sb(8, F32), "N2": _sb(256, F32), "P2": _sb(256, F32),
+    "BV": _sb(256, F32), "BC": _sb(256, F32), "MV": _sb(256, F32), "MC": _sb(256, F32), "VF": _sb(32, F32), "LO": _sb(256, F16),
+    "VO": _sb(16, U16), "CN": _sb(16, F32), "AI": _sb(4, I32),
+    "s1": _sb(16, F32), "s3": _sb(16, F32), "SMO": _sb(16, U16), "CL": _sb(256, I32), "XC": _sb(256, F32), "SY": _sb(256, F32),
+    "X2": _sb(256, F32), "PB": _sb(256, F32),
     "pd0": ("psum", [128, 1024], F32), "pd1": ("psum", [128, 1024], F32), "pa": ("psum", [128, 512], F32),
     "pb": ("psum", [128, 512], F32), "k0": ("psum", [128, 512], F32), "k1": ("psum", [128, 512], F32),
 }
-ALIAS = {"D0": ("RP", 128), "B": ("NR", 128), "J16": ("P", 256), "CL": ("SI", 256)}
-SEMAPHORES = (["cv", "cs", "cp", "cg", "sent", "lth", "lx", "oym", "oyx", "oyp"] + ["lm%d" % i for i in range(4)]
+ALIAS = {"D0": ("U", 128), "B": ("NR", 128), "J16": ("P", 256)}
+SEMAPHORES = (["cv", "cs", "cp", "cg", "sent", "lth", "lx", "oym", "oyx", "oyp", "pi0", "pi1"] + ["lm%d" % i for i in range(4)]
               + ["a%d" % i for i in range(RO)] + ["e%d" % i for i in range(RO)] + ["b%d" % i for i in range(RO)])
 CYC, PEC, LAT, HOP1, HOP2 = 1.04, 0.52, 70.0, 3000.0, 3800.0
 
@@ -115,19 +118,23 @@ def rank_program(g, core, T, topo):
     def RED(o, a):
         return op("v", lambda: g.vector.tensor_reduce(o["ap"], a["ap"], AxisListType.X, OP.add), [o], [a], 100)
 
-    def ACT(o, a, f, bias=0.0, scale=1.0):
+    def ACT(o, a, f, bias=0.0, scale=1.0, acc=None):
         c = 65 + 1.56 * CYC * o["n"] if a["ind"] else 40 + CYC * max(64, o["n"])
         if o["ind"]:
             return op("s", lambda: g.scalar.activation(o["ap"], a["ap"], f), [o], [a], 65 + 3.8 * CYC * o["n"])
-        return op("s", lambda: g.scalar.activation(o["ap"], a["ap"], f, bias=ap(bias), scale=ap(scale)), [o], [a, scale], c)
+        if acc is not None:
+            return op("s", lambda: g.scalar.activation(o["ap"], a["ap"], f, bias=bias, scale=scale, accum_out=acc["ap"]), [o, acc], [a], c + 20)
+        return op("s", lambda: g.scalar.activation(o["ap"], a["ap"], f, bias=ap(bias), scale=ap(scale)), [o], [a, bias, scale], c)
 
-    def MM(lst):
+    def MM(lst, free=False):
         def fn():
             for (o, l, x, s0, s1) in lst:
                 h = g.tensor.matmul(o["ap"], l["ap"], x["ap"], s0, s1)
             return h
         c = sum(PEC * max(64, x["n"]) * (4 if SCRATCH[x["name"]][2] == F32 else 1) for (o, l, x, s0, s1) in lst)
-        return op("p", fn, [m[0] for m in lst], [m[1] for m in lst] + [m[2] for m in lst], c + 40, lat=60)
+        j = op("p", fn, [m[0] for m in lst], [m[1] for m in lst] + [m[2] for m in lst], c + 40, lat=60)
+        ops[j]["free"] = free
+        return j
 
     def IOTA(o, pat, base, cm=0):
         if SCRATCH[o["name"]][2] == I32:
@@ -145,9 +152,9 @@ def rank_program(g, core, T, topo):
     voted = lambda t: (r - 1 - t % (N - 1)) % N
     voter = lambda t: (r + 1 + t % (N - 1)) % N
 
-    j = DMA("y", T.Xb[:], T.xv[:], [R("Xb")], [], "lx", 7500)
+    j = DMA("y", T.Xb[:], T.xv[:], [R("Xb")], [], "lx", LOAD[0])
     for c in range(4):
-        k = DMA("y", T.Mi[:, 1024 * c:1024 * c + 1024], T.mt[:, 1024 * c:1024 * c + 1024], [R("Mi", 1024 * c, 1024 * c + 1024)], [], "lm%d" % c, 10200 + 2700 * c)
+        k = DMA("y", T.Mi[:, 1024 * c:1024 * c + 1024], T.mt[:, 1024 * c:1024 * c + 1024], [R("Mi", 1024 * c, 1024 * c + 1024)], [], "lm%d" % c, LOAD[0] + LOAD[1] * (c + 1))
         ops[k]["after"].append(j); j = k
     IOTA(R("D0"), [[1, 128]], 0, -1)
     IOTA(R("B"), [[1, 8], [0, 16]], 0)
@@ -156,14 +163,19 @@ def rank_program(g, core, T, topo):
     IOTA(R("IR"), [[1, 256]], 0)
     op("g", lambda: g.dma_start(T.TH1[0:1, 0:8], T.th[:], allow_slow_non_contiguous=True), [R("TH1")], [], 1000, lat=3000, sem=("lth", 16))
 
+    void = W + 260 + r
+
     def vrep(t, after=()):
-        for c in range(4):
-            j = IOTA(R("Mi" if t % 2 else "VR", 1024 * c, 1024 * c + 1024), [[16, 64], [0, 16]], 1024 * c + 4 * t + r)
+        js = [IOTA(R("VR", 1024 * c, 1024 * c + 1024), [[16, 64], [0, 16]], 1024 * c + 4 * t + r) for c in range(4)]
+        js.append(IOTA(R("VV"), [[16, 256]], 4 * t + voted(t)))
+        js.append(IOTA(R("VU"), [[16, 256]], 4 * t + voted(t) + int(UP)))
+        js += [IOTA(R(nm, 704, 768), [[4, 64]], void + int(UP)) for nm in ("CC", "CV")]
+        for j in js:
             ops[j]["after"] += list(after)
     vrep(0)
     op("g", lambda: g.partition_broadcast(T.TH8[:], T.TH1[0:1, 0:8], 128), [R("TH8")], [R("TH1")], 200)
-    for c in range(5):
-        IOTA(R("IO", 1024 * c, 1024 * c + 1024), [[1, 1024]], 1024 * c)
+    for c in range(4):
+        IOTA(R("IO", GW // 4 * c, GW // 4 * (c + 1)), [[1, GW // 4]], GW // 4 * c)
     TS(R("pidx", 1, 2), R("pidx", 0, 1), 15, OP.bitwise_and); CP_(col(PM), R("pidx", 1, 2))
     TS(R("pidx", 2, 3), R("pidx", 0, 1), 4, OP.arith_shift_right); CP_(col(PG), R("pidx", 2, 3))
     TS(R("pidx", 3, 4), R("pidx", 0, 1), 16, OP.bitwise_and)
@@ -172,34 +184,39 @@ def rank_program(g, core, T, topo):
     TS(R("I"), R("D0"), 0.0, OP.is_equal); TS(R("NI"), R("D0"), 0.0, OP.is_equal, -1.0, OP.mult); TS(R("I32"), R("D0"), 0.0, OP.is_equal)
     TS(R("B"), R("B"), col(PG), OP.is_equal)
     MS(R("ONE"), 1.0); MS(R("SE"), 0.0); MS(R("SA"), 0.0); MS(R("Z16"), 0.0); MS(R("PS"), 0.0)
-    for j in range(8):
-        TS(R("SE", 16 * j, 16 * j + 129 * 15 + 1, 129), R("ONE", 0, 16), R("B", 16 * j, 16 * j + 1), OP.mult, 65536.0, OP.mult)
-        TS(R("SA", 16 * j, 16 * j + 129 * 15 + 1, 129), R("ONE", 0, 16), R("B", 16 * j, 16 * j + 1), OP.mult, -16.0, OP.mult)
+    TS(R("SE", 15, 143, 16), R("B", 0, 128, 16), 65536.0, OP.mult); TS(R("SA", 15, 143, 16), R("B", 0, 128, 16), -16.0, OP.mult)
+    into = lambda name, k: R(name, 15 - k, 143 - k)
     TS(R("KC"), R("ONE", 0, 64), col(K15), OP.mult)
     TS(R("MK"), R("D0"), 0.0, OP.is_gt, -1.0, OP.mult); TT(R("NL"), R("MK"), R("B"), OP.mult)
     TS(R("SC"), R("D0"), 0.0, OP.is_le, -1.0, OP.mult); TT(R("NU"), R("SC"), R("B"), OP.mult)
     TS(R("KH"), R("J16", 0, 128), col(PM), OP.is_equal)
     TS(R("RS"), R("J16"), 0.0, OP.is_equal, -1.0e9, OP.mult); TS(R("RM"), R("J16", 0, 128), 0.0, OP.not_equal)
     TS(R("IOF"), R("IR", 0, 16), 16.0, OP.mult, col(PM), OP.add); TS(R("Q0"), R("IOF"), 256.0, OP.add)
-    TS(R("C2"), R("IOF", 0, 4), 16.0, OP.mult, 1.0e6 + W, OP.add)
+    TS(R("C2"), R("IOF", 0, 4), 4.0, OP.mult, void + UP, OP.add); TS(R("DC"), R("IOF"), float(W), OP.add)
     for s in range(4):
-        TS(R("DMB", 64 * s, 64 * s + 64), R("IR", 0, 64), R("IOF", s, s + 1), OP.is_gt, R("C2", s, s + 1), OP.mult)
+        TS(R("DM", 64 * s, 64 * s + 64), R("IR", 0, 64), R("IOF", s, s + 1), OP.is_gt, R("C2", s, s + 1), OP.mult)
     for h in range(2):
         for q in range(2):
-            for nm in ("FX32", "FX16"):
-                TS(R(nm, 256 * h + 128 * q, 256 * h + 128 * q + 128), R("D0"), 16.0 * (q - h), OP.is_equal, col(H0 + h), OP.mult)
+            TS(R("FX32", 256 * h + 128 * q, 256 * h + 128 * q + 128), R("D0"), 16.0 * (q - h), OP.is_equal, col(H0 + h), OP.mult)
+    TS(R("NI32"), R("I32"), -1.0, OP.mult); MS(R("ONE32"), 1.0)
+    TS(R("N2", 0, 128), R("D0"), 1.0, OP.is_equal); TS(R("N2", 128, 256), R("D0"), -15.0, OP.is_equal)
+    TT(R("P2", 0, 128), R("N2", 0, 128), R("I32"), OP.subtract); TT(R("P2", 0, 128), R("P2", 0, 128), R("N2", 128, 256), OP.subtract)
+    TT(R("P2", 0, 128), R("P2", 0, 128), R("RM"), OP.mult); TT(R("SH"), R("P2", 0, 128), R("N2", 128, 256), OP.add)
     for k in range(16):
         TS(R("D16", 128 * k, 128 * k + 128), R("I32"), R("KH", k, k + 1), OP.mult)
         ACT(R("D32", 128 * k, 128 * k + 128), R("I32"), AF.Identity, scale=R("KH", k, k + 1))
     TT(R("THF"), R("TH8"), R("B", 0, 128, 16), OP.mult); RED(col(THC), R("THF"))
     TS(col(THC), col(THC), 1.0 / 1024, OP.add); TS(col(WC), col(THC), 256.0, OP.mult)
-    for c in range(2):
-        IOTA(R("Mf", W + 512 * c, W + 512 * c + 512), [[0, 512]], 0)
+    MS(R("Mf", W, GW), 0.0)
     for c in range(8):
-        ACT(R("Xs", 512 * c, 512 * c + 512), R("Xb", 512 * c, 512 * c + 512), AF.Identity)
+        ACT(R("Xs", 512 * c, 512 * c + 512), R("Xb", 512 * c, 512 * c + 512), AF.Identity, bias=HI)
         CP_(R("Mf", 512 * c, 512 * c + 512), R("Mi", 512 * c, 512 * c + 512))
-    for c in range(5):
-        ACT(R("F", 1024 * c, 1024 * c + 1024), R("IO", 1024 * c, 1024 * c + 1024), AF.Identity)
+    for c in range(4):
+        ACT(R("F", GW // 4 * c, GW // 4 * (c + 1)), R("IO", GW // 4 * c, GW // 4 * (c + 1)), AF.Identity)
+    for t in range(1, RO):
+        CP_(R("O0", 256 * t - 256, 256 * t), lanes("Mi", t))
+    XA = R("Xs", W, W + 256)
+    ACT(XA, lanes("Xb", 0), AF.Identity, bias=HI)
 
     nsent = [0]
     marks = []
@@ -211,51 +228,58 @@ def rank_program(g, core, T, topo):
         pm = R((("pa", "pb") if last else ("k0", "k1"))[c % 2], 0, 64)
         b = 1024 * (c % 2)
         if by_act:
-            ACT(R("Gf", b, b + 1024), IN("F", W, ch(src, c)), AF.Identity, bias=-2048.0)
-            MM([(pm, ch("D32", k, 128), R("Gf", b + k, b + 1024, 16), k == 0, k == 15) for k in range(16)])
+            ACT(R("Gf", b, b + 1024), IN("F", W, src), AF.Identity, bias=-2048.0)
+            for k4 in range(0, 16, 4):
+                MM([(pm, ch("D32", k, 128), R("Gf", b + k, b + 1024, 16), k == 0, k == 15) for k in range(k4, k4 + 4)])
         else:
-            TS(R("G", b, b + 1024), IN("F", W, ch(src, c)), -2048.0, OP.add)
+            TS(R("G", b, b + 1024), IN("F", W, src), -2048.0, OP.add)
             MM([(pm, ch("D16", k, 128), R("G", b + k, b + 1024, 16), k == 0, k == 15) for k in range(16)])
         TS(ch(dst, c), pm, 2048.0, OP.add)
         if last:
-            TS(ch("M2", c), pm, 2048.0, OP.add)
-            TR(ch("PT", c), pm)
+            TS(ch("M2", c), pm, WHOLE + 2048, OP.add, -WHOLE, OP.add)
+            steps(c, ch("M2", c))
+
+    def steps(c, names):
+        pn = R(("pa", "pb")[c % 2], 64, 128)
+        MM([(pn, R("SH"), names, True, True)])
+        TR(ch("PT", c), pn)
 
     def score(t, c):
         b = 1024 * (c % 2); pd = "pd%d" % (c % 2)
-        m2 = lanes("Mi", 0, c, c + 1) if t == 0 else ch("M2", c)
-        TS(ch("CL", c), m2, 12, OP.bitwise_and)
-        TS(ch("PEN", c), ch("CL", c), 4.0 * t, OP.is_equal, -8388608.0, OP.mult)
-        ACT(R("XG", b, b + 1024), IN("Xb" if t == 0 else "Xs", W, ch("OB", c)), AF.Identity)
+        if t == 0:
+            TS(ch("CL", c), lanes("Mi", 0, c, c + 1), 12, OP.bitwise_and)
+            TS(ch("PEN", c), ch("CL", c), 0.0, OP.is_equal, -8388608.0, OP.mult)
+        ACT(R("XG", b, b + 1024), IN("Xs" if t else "Xb", W, ch("OB", c)), AF.Identity, bias=-HI if t else 0.0)
         for hf in range(2):
             ks = range(8 * hf, 8 * hf + 8)
             MM([(ch(pd, k), R("NI"), lanes("Xb", t, c, c + 1), k == ks[0], False) for k in ks])
             MM([(ch(pd, k), R("I"), R("XG", b + k, b + 1024, 16), False, k == ks[-1]) for k in ks])
             ACT(R("AB", b + 512 * hf, b + 512 * hf + 512), ch(pd, hf, 512), AF.Abs)
-        TT(ch("EQ", c, 1024), IN("Mi" if t == 0 else "Mf", W, ch("OB", c)), ch("Mi" if t % 2 else "VR", c, 1024), OP.is_equal)
-        key = ch("k0" if c < SPLIT else "k1", c)
-        l0 = [(key, R("I"), R("KC"), c in (0, SPLIT), False), (key, R("I"), ch("PEN", c), False, False)]
-        if t:
-            l0.append((key, R("NI"), ch("LP", c), False, False))
-        l2 = [(key, ch("SA", k, 128), R("AB", b + 64 * k, b + 64 * k + 64), False, False) for k in range(16)]
-        MM(l2[:8] if c not in (0, SPLIT) else l0[:1] + l2[:8]); MM(l2[8:]); MM(l0[1:] if c in (0, SPLIT) else l0)
-        if c in (SPLIT - 1, 3):
-            for d in range(SPLIT if c == 3 else 0, c + 1):
-                MM([(ch("k0" if c < SPLIT else "k1", d), ch("SE", k, 128), R("EQ", 1024 * d + k, 1024 * d + 1024, 16), False, d == c and k == 15) for k in range(16)])
+        TT(R("EQ", b, b + 1024), IN("Mi" if t == 0 else "Mf", W, ch("OB", c)), ch("VR", c, 1024), OP.is_equal)
+        bank = "k0" if c < SPLIT else "k1"
+        key = ch(bank, c); own = range(SPLIT) if c < SPLIT else range(SPLIT, 4)
+        if c == own[0]:
+            MM([(ch(bank, d), R("I"), R("KC"), d == c, False) for d in own])
+        for hf in range(2):
+            MM([(key, into("SA", k), R("AB", b + 64 * k, b + 64 * k + 64), False, False) for k in range(8 * hf, 8 * hf + 8)], True)
+            MM([(key, into("SE", k), R("EQ", b + k, b + 1024, 16), False, False) for k in range(8 * hf, 8 * hf + 8)], True)
+        MM([(key, R("NI"), ch("LP", c), False, c == own[-1]) if t else (key, R("I"), ch("PEN", c), False, c == own[-1])], c != own[-1])
 
     def choose(t, lo, hi):
         m0 = 32 * t + lo // 8; m1 = m0 + (hi - lo) // 16; m2 = m1 + (hi - lo) // 16
-        TR(R("pa", lo, hi), R("k1" if lo else "k0", lo, hi))
-        SCAN(R("P", lo, hi), R("RS", lo, hi), R("pa", lo, hi), -2.0e9, OP.add, OP.max)
-        TT(R("pb", lo, hi), R("pa", lo, hi), R("P", lo, hi), OP.is_ge)
-        TT(R("NR", lo, hi), R("pa", lo, hi), R("P", lo, hi), OP.is_lt)
+        kt = R("pa", 256 + lo, 256 + hi)
+        TR(kt, R("k1" if hi == 256 else "k0", lo, hi))
+        SCAN(R("P", lo, hi), R("RS", lo, hi), kt, -2.0e9, OP.add, OP.max)
+        TT(R("NR", lo, hi), kt, R("P", lo, hi), OP.is_lt)
         s0, s1 = lo // 16, hi // 16
-        MM([(R("pd0", s0 + h, s1, 2), ch("FX32", 2 * h + q, 128), R("P", lo + 15 + 16 * q, hi, 32), q == 0, q == 1) for h in range(2) for q in range(2)])
-        TT(R("RP", lo, hi), R("pb", lo, hi), R("PT", lo, hi), OP.mult)
-        SCAN(R("CS", lo, hi), R("NR", lo, hi), R("RP", lo, hi), 0.0, OP.mult, OP.add)
+        fx = lambda at, x, k, a, z: [(R("pd0", at + s0 + h, at + s1, 2), ch("FX32", 2 * h + q, 128), R(x, lo + k + 16 * q, hi, 32), a and h + q == 0, z and h + q == 2)
+                                     for h in range(2) for q in range(2)]
+        MM(fx(512, "PT", 0, True, False))
+        MM(fx(0, "P", 15, True, True))
+        SCAN(R("U", lo, hi), R("PT", lo, hi), R("NR", lo, hi), 0.0, OP.add, OP.mult)
         TS(R("O1", m1, m2), R("pd0", s0, s1), -1.0 / 256, OP.mult, col(WC), OP.add)
-        MM([(R("pd0", 512 + s0 + h, 512 + s1, 2), ch("FX16", 2 * h + q, 128), R("CS", lo + 15 + 16 * q, hi, 32), q == 0, q == 1) for h in range(2) for q in range(2)])
-        TS(R("O1", m0, m1), R("pd0", 512 + s0, 512 + s1), 2048.0, OP.add)
+        MM(fx(512, "U", 15, False, True))
+        CP_(R("O1", m0, m1), R("pd0", 512 + s0, 512 + s1))
         dst = T.cores[voter(t)]; rid, pid, _se = topo.addr(dst); sem = ("a%d" if lo else "e%d") % t
         o1 = R("O1", m0, m2); l1 = R("L1", m0, m2)
         s = op("g", lambda: g.remote_dma(l1["ap"], o1["ap"], T.sem[sem], T.sem.sent, pid, rid, topo.mask(core, dst)), [], [o1], 500, sem="remote")
@@ -268,9 +292,8 @@ def rank_program(g, core, T, topo):
         co = R("L1", m0, m1)
         TT(R("E1", lo, hi), IN("Mi" if t == 0 else "Mf", W, co), R("VV", lo, hi), OP.is_equal)
         TS(R("NF", s0, s1), R("L1", m1, m2), -255.0, OP.add, 256.0, OP.mult)
-        ACT(R("BC", lo, hi), IN("IO", W, co), AF.Identity, scale=512.0)
-        MM([(R("k0", s0, s1), ch("SE", k, 128), R("E1", lo + k, hi, 16), k == 0, k == 15) for k in range(16)])
-        TT(R("BV", lo, hi), R("BC", lo, hi), R("IR", lo, hi), OP.add)
+        ACT(R("BC", lo, hi), IN("IO", W, co), AF.Identity, bias=UP)
+        MM([(R("k0", s0, s1), into("SE", k), R("E1", lo + k, hi, 16), k == 0, k == 15) for k in range(16)])
         TT(R("PS", s0 + 1, s1 + 1), R("k0", s0, s1), R("NF", s0, s1), OP.is_ge)
         TT(R("NP", s0, s1), R("k0", s0, s1), R("NF", s0, s1), OP.is_lt)
         MM([(R("k1", s0, s1), R("NL"), R("PS", s0 + 1, s1 + 1), True, False), (R("k1", s0, s1), R("NU"), R("PS", s0, s1), False, True)])
@@ -278,47 +301,55 @@ def rank_program(g, core, T, topo):
         SCAN(R("SN", s0, s1), R("k1", s0, s1), R("Z16", s0, s1), R("SN", s0 - 1, s0) if lo else 767.0, OP.add, OP.add)
         TT(R("SL", s0, s1), R("SN", s0, s1), R("QQ", s0, s1), OP.subtract)
         CP_(R("SO", s0, s1), R("SL", s0, s1))
-        CP_(IN("CP", 768, R("SO", s0, s1)), R("BV", lo, hi))
+        CP_(IN("CC", 768, R("SO", s0, s1)), R("BC", lo, hi))
+        ACT(IN("CV", 768, R("SO", s0, s1)), R("VU", lo, hi), AF.Silu)
 
+    def yx(t, src, less):
+        ACT(R("X2"), lanes("Xb", t), AF.Identity, bias=256.0)
+        ACT(R("pb", 256, 512), src, AF.Abs, bias=-(less + HI + 256))
+        TT(R("X2"), R("pb", 256, 512), R("X2"), OP.min)
+        ACT(R("YX", t, 1024, 4), R("X2"), AF.Abs, bias=-256.0)
+
+    halves = [(0, 64 * SPLIT), (64 * SPLIT, 256)] if SPLIT else [(0, 256)]
     for t in range(RO):
-        rho = voted(t); base = 4 * t + rho
+        rho = voted(t)
+        last = t == RO - 1
         if t == 0:
             for c in range(4):
                 CP_(ch("OB", c), lanes("Mi", 0, c, c + 1))
-                TS(ch("RP", c), lanes("Mi", 0, c, c + 1), -2048.0, OP.add)
-                TR(ch("PT", c), ch("RP", c))
+                CP_(ch("M2", c), lanes("Mi", 0, c, c + 1))
+                steps(c, ch("M2", c))
         else:
             order = [(0, 0), (1, 0), (0, 1), (2, 0), (1, 1), (3, 0), (2, 1), (3, 1)]
             for c, step in order:
                 if step == 0:
-                    follow(c, "O0", "OA", c in ACT_G1, False)
+                    follow(c, ch("O0", 4 * t - 4 + c), "OA", c in ACT_G1, False)
                 else:
-                    follow(c, "OA", "OB", c in ACT_G2, True)
-        TS(R("VV"), R("IR"), 16.0, OP.mult, float(base), OP.add)
-        TS(R("CP", 704, 768), R("IR", 0, 64), 8193.0, OP.mult, 512.0 * (W + base) + 256, OP.add)
-        TS(R("DM"), R("DMB"), base - 1.0e6, OP.add, 0.0, OP.max)
+                    follow(c, ch("OA", c), "OB", c in ACT_G2, True)
+        if last:
+            DMA("y", T.PB[:], T.Xs[0:128:16, 0:W], [R("PB")], [R("Xs", 0, W)], "pi0", 2500)
+            ACT(R("PB"), R("PB"), AF.Abs); ACT(R("PB"), R("PB"), AF.Identity, bias=WHOLE - BIG)
+            ACT(R("PB"), R("PB"), AF.Relu, bias=1.0 - WHOLE); ACT(R("PB"), R("PB"), AF.Identity, bias=-1.0)
+            DMA("y", T.F[0:128:16, 0:W], T.PB[:], [R("F", 0, W)], [R("PB")], "pi1", 2500)
         for c in range(4):
             score(t, c)
             if c == SPLIT - 1:
-                choose(t, 0, 64 * SPLIT)
-        choose(t, 64 * SPLIT, 256)
-        if t + 1 < RO:
-            CP_(R("O0"), lanes("Mf", t + 1))
-        vote(t, 0, 64 * SPLIT)
-        vote(t, 64 * SPLIT, 256)
-        TS(R("X2", 0, 64), R("CP", 704, 768), 9, OP.arith_shift_right)
-        TS(R("X2", 64, 128), R("CP", 704, 768), 511, OP.bitwise_and)
-        for hf in range(2):
-            TT(ch("MK", hf), ch("X2", hf), ch("KH", 0), OP.mult)
+                choose(t, *halves[0])
+        choose(t, *halves[-1])
+        if t:
+            yx(t - 1, lanes("Xs", t - 1), 0.0)
+        for lo, hi in halves:
+            vote(t, lo, hi)
+        for hf, nm in enumerate(("CC", "CV")):
+            TT(ch("MK", hf), R(nm, 704, 768), ch("KH", 0), OP.mult)
             SCAN(ch("SC", hf), ch("RM", 0), ch("MK", hf), 0.0, OP.mult, OP.add)
         for s4 in range(4):
-            TS(ch("NR", s4), R("X2", 0, 64), R("SC", 16 * s4 + 15, 16 * s4 + 16), OP.is_equal, 8192.0, OP.mult)
-        TS(R("VC"), R("SC", 79, 128, 16), 16.0, OP.mult, float(base), OP.add)
-        SCAN(R("P"), R("NR"), R("DM"), 0.0, OP.max, OP.min)
-        TT(R("OF", 0, 4), R("SC", 15, 64, 16), R("P", 63, 256, 64), OP.max)
-        TT(R("OF", 4, 8), R("VC"), R("P", 63, 256, 64), OP.max)
+            TS(ch("N2", s4), R("CC", 704, 768), R("SC", 16 * s4 + 15, 16 * s4 + 16), OP.is_equal, 8192.0, OP.mult)
+        SCAN(R("P2"), R("N2"), R("DM"), 0.0, OP.max, OP.min)
+        TT(R("OF", 0, 4), R("SC", 15, 64, 16), R("P2", 63, 256, 64), OP.max)
+        TT(R("OF", 4, 8), R("SC", 79, 128, 16), R("P2", 63, 256, 64), OP.max)
         lz = lambda q, lo, hi, t=t: R("LZ", 32 * t + 8 * q + lo, 32 * t + 8 * q + hi)
-        CP_(lz(rho, 0, 8), R("OF"))
+        TS(lz(rho, 0, 8), R("OF"), -UP, OP.add)
         others = [T.cores[(r + d) % N] for d in range(1, N)]
         others.sort(key=lambda x: topo.same_plane(topo.chip(core), topo.chip(x)))
         msk = topo.mask(core, others[0])
@@ -330,44 +361,40 @@ def rank_program(g, core, T, topo):
         s = op("g", lambda tr=tr: g.remote_dma_fused([tr], local_sem=T.sem.sent), [], [lz(rho, 0, 8)], 500, sem="remote")
         nsent[0] += ne; marks.append(s)
         op(None, None, [lz(q, 0, 8) for q in range(N) if q != rho], [], 0, lat=HOP2, sem=("b%d" % t, ne * (N - 1)), after=[s])
-        for s0, s1 in ((0, 4 * SPLIT), (4 * SPLIT, 16)):
-            TS(R("s1", s0, s1), R("O1", 32 * t + s0 + s1, 32 * t + 2 * s1), 12000.0, OP.is_lt)
+        for lo, hi in halves:
+            s0, s1 = lo // 16, hi // 16
+            TS(R("s1", s0, s1), R("O1", 32 * t + s0 + s1, 32 * t + 2 * s1), 12000.0, OP.is_ge, 8192.0, OP.mult)
             CP_(R("s3", s0, s1), R("O1", 32 * t + 2 * s0, 32 * t + s0 + s1))
-        TS(R("s2"), R("IOF"), 16.0, OP.mult, float(4 * t + r), OP.add)
-        TT(R("s3"), R("s3"), R("s2"), OP.subtract); TT(R("s3"), R("s3"), R("s1"), OP.mult); TT(R("s3"), R("s3"), R("s2"), OP.add)
+        TT(R("s3"), R("s3"), R("s1"), OP.add); TT(R("s3"), R("s3"), R("DC"), OP.min)
         CP_(R("SMO"), R("s3"))
-        ACT(R("MC"), IN("Xs" if t else "Xb", W, R("SMO")), AF.Identity)
-        TT(R("DL"), R("MC"), lanes("Xs" if t else "Xb", t), OP.add)
-        TS(R("SI"), R("DL"), 0.5, OP.mult, -0.25, OP.add)
+        ACT(R("XC"), IN("Xs", W + 256, R("SMO")), AF.Identity, bias=-0.5)
+        MM([(R("pd1", 0, 256), R("I32"), XA, True, False)]); MM([(R("pd1", 0, 256), R("I32"), R("XC"), False, True)])
+        ACT(R("SY"), R("pd1", 0, 256), AF.Identity, bias=WHOLE, scale=0.5)
         if t == 0:
-            CP_(R("YX", t, 1024, 4), R("SI"))
+            ACT(R("YM", 0, 1024, 4), R("M2"), AF.Identity)
         else:
-            TS(R("AL"), lanes("Xs", t), 256.0, OP.is_lt)
-            TT(R("DL"), R("SI"), lanes("Xb", t), OP.subtract); TT(R("DL"), R("DL"), R("AL"), OP.mult)
-            TT(R("YX", t, 1024, 4), R("DL"), lanes("Xb", t), OP.add)
-            TT(R("RP"), R("M2"), lanes("Mf", t), OP.subtract); TT(R("RP"), R("RP"), R("AL"), OP.mult)
-            TT(lanes("Mf", t), R("RP"), lanes("Mf", t), OP.add)
-        last = t == RO - 1
+            MM([(R("pd1", 512, 768), R("NI32"), R("M2"), True, False), (R("pd1", 512, 768), R("I"), R("LP"), False, True)])
+            TT(R("NR"), R("pd1", 512, 768), lanes("Mf", t), OP.min)
+            ACT(R("YM", t, 1024, 4), R("NR"), AF.Abs)
         if not last:
-            CP_(lanes("Xs", t), R("SI"))
+            if t:
+                ACT(lanes("Mf", t), R("M2"), AF.Identity)
+            ACT(lanes("Xs", t), R("SY"), AF.Identity, bias=-WHOLE)
+            for x in range(N):
+                if t and x != r:
+                    ACT(R("Xs", 4 * t + x, W, 16), R("Xs", 4 * t + x, W, 16), AF.Abs)
+                ACT(R("Xs", 4 * t + 4 + x, W, 16), R("Xs", 4 * t + 4 + x, W, 16), AF.Identity, scale=-1.0)
             vrep(t + 1, [s])
         else:
-            ACT(R("Gf", 0, 1024), R("Mf", r, W, 4), AF.Identity)
-            DMA("y", T.ym[:], T.Gf[:, 0:1024], [], [R("Gf", 0, 1024)], "oym", 4000)
-            for c in range(8):
-                ACT(ch("F", c, 512), ch("Xs", c, 512), AF.Identity, bias=WHOLE - BIG)
-                if c < 5:
-                    ACT(ch("F", c, 512), ch("F", c, 512), AF.Relu, bias=1.0 - WHOLE)
-                    ACT(ch("F", c, 512), ch("F", c, 512), AF.Identity, bias=-1.0)
-                else:
-                    TS(ch("F", c, 512), ch("F", c, 512), -WHOLE, OP.add, -1.0, OP.max)
+            yx(t, R("SY"), WHOLE)
+            DMA("y", T.ym[:], T.YM[:], [], [R("YM")], "oym", 4000)
         add = 0.0 if last else BIG
         val = "BV" if last else "MV"
         for q in range(N - 1, -1, -1):
             if not last:
                 ACT(ch("MV", q), IN("Mf", GW, lz(q, 4, 8)), AF.Identity, bias=q / 16.0)
             ACT(ch("BV", q), IN("IO", GW, lz(q, 4, 8)), AF.Identity, bias=add)
-            TS(ch("VF", q, 4), lz(q, 4, 8), 1.0 / GW, OP.mult)
+        TS(R("VF"), lz(0, 0, 32), 1.0 / GW, OP.mult)
         for q in range(N - 1, -1, -1):
             CP_(IN("F", GW, lz(q, 0, 4)), ch(val, q))
         for q in range(N):
@@ -376,27 +403,27 @@ def rank_program(g, core, T, topo):
             ACT(ch("BC", q), IN("IO", GW, lz(q, 0, 4)), AF.Identity, bias=add)
         for q in range(1, N):
             TT(ch("LO", q), IN("F", GW, lz(q, 0, 4)), ch(val, q), OP.not_equal)
-        MM([(R("pa", 0, 16), R("I32"), R("VF"), True, False)])
+        MM([(R("pa", 4 * q, 4 * q + 4), R("I32"), R("VF", 8 * q + 4, 8 * q + 8), q == 0, False) for q in range(N)])
         MM([(R("pa", 4, 16), ch("D16", k, 128), R("LO", 64 + k, 256, 16), False, k == 15) for k in range(16)])
         vval = "BC" if last else "MC"
         CP_(IN("F", GW, lz(0, 4, 8)), ch(vval, 0))
         TS(R("VO"), R("pa", 0, 16), float(GW), OP.mult, 0.25, OP.add)
         CP_(IN("F", SW, R("VO", 4, 16)), R(vval, 64, 256))
-        TS(R("s4"), lz(r, 4, 8), float(W - 1), OP.min)
-        ACT(R("XO"), IN("Xb", W, R("s4")), AF.Identity)
-        TS(R("UO"), R("pa", 4 * r, 4 * r + 4), GW / 4.0, OP.mult, 0.1 - r / 4.0, OP.add)
-        CP_(IN("YX", SW // 4, R("UO")), R("XO"))
         if not last:
             for q in range(N - 1, -1, -1):
                 ACT(IN("Xs", GW, lz(q, 0, 4)), ch("BV", q), AF.Silu)
-            ACT(R("LP"), lanes("Xs", t + 1), AF.Relu, bias=-255.0 * 128, scale=128.0)
+            ACT(XA, lanes("Xs", t + 1), AF.Abs)
+            ACT(R("LP"), XA, AF.Relu, bias=-(HI + 255) * 128, scale=128.0)
             ACT(IN("Xs", SW, R("VO")), R("BC"), AF.Silu)
-            TS(R("CN"), R("VO"), 4096.0, OP.is_lt)
-            MM([(R("pb", 0, 16), R("ONE"), R("CN"), True, True)])
-            RED(col(AF_), R("pb", 0, 16))
-            CP_(R("AI", 0, 1), col(AF_)); TS(R("AI", 1, 2), R("AI", 0, 1), 3, OP.bitwise_and)
+            ACT(R("CN"), R("pa", 0, 16), AF.Sign, bias=(W - 0.5) / GW, scale=-1.0, acc=col(AF_))
+            MM([(R("pb", 0, 1), R("ONE32"), col(AF_), True, True)])
+            TS(R("AI", 0, 1), R("pb", 0, 1), 0.5, OP.mult, 1024.0, OP.add); TS(R("AI", 1, 2), R("AI", 0, 1), 3, OP.bitwise_and)
             TS(col(WC), R("AI", 1, 2), col(THC), OP.add, 256.0, OP.mult)
         else:
+            TS(R("s4"), lz(r, 4, 8), float(W - 1), OP.min)
+            ACT(R("XO"), IN("Xb", W, R("s4")), AF.Identity)
+            TS(R("UO"), R("pa", 4 * r, 4 * r + 4), GW / 4.0, OP.mult, 0.1 - r / 4.0, OP.add)
+            CP_(IN("YX", SW // 4, R("UO")), R("XO"))
             DMA("y", T.yp[:], T.F[0:128:16, 0:W], [], [R("F", 0, W)], "oyp", 2800)
             DMA("s", T.yx[:], T.YX[:, 0:1024], [], [R("YX", 0, 1024)], "oyx", 3400)
 
@@ -427,6 +454,8 @@ def emit(g, T, Q, ops, nsent, marks):
             raw = meet(e["wr"], o["rd"], False)
             war = meet(e["rd"], o["wr"], False) or meet(e["wr"], o["wr"], False)
             if same:
+                if e.get("free") and o.get("free"):
+                    continue
                 if raw or war or (o["eng"] == "p" and meet(e["wr"], o["wr"], True)):
                     o["dep"][j] = o["eng"] != "p" and (raw or WAIT_W)
             elif raw or war or meet(e["wr"] + e["rd"], o["wr"] + o["rd"], True):

@@ -1,16 +1,19 @@
 from concourse.bass import DstId, RemoteDMATransfer
 from concourse.mybir import AluOpType as OP, AxisListType, ActivationFunctionType as AF
 
-W, RO, BIG, GW, SW = 4096, 4, 65536.0, 4624, 8720
+W, RO, BIG, GW, SW = 4096, 4, 65536.0, 4624, 4880
 HI, UP = 8192.0, 32.0
 WHOLE = 12582912.0
 F32, BF, F16, I32, U16 = "float32", "bfloat16", "float16", "int32", "uint16"
-ACT_G1 = (2, 3)
-ACT_G2 = ()
+FOLLOW = [(1, 0, 64, "v", "pa"), (1, 64, 128, "v", "pb"), (2, 0, 64, "v", "pa"), (1, 128, 256, "s", "k0"),
+          (2, 64, 128, "v", "pb"), (2, 128, 192, "v", "pa"), (2, 192, 256, "v", "pb")]
 WAIT_W = True
 SPLIT = 0
+LOCAL = (2, 3)
+COPY = {2: "T1", 3: "T2"}
+COPY_NS = 25000.0
 LOAD = (6000.0, 2200.0)
-TRIES, SLACK = 8000, 100.0
+TRIES, SLACK = 200000, 2500.0
 PLAN = {}
 
 
@@ -19,9 +22,9 @@ def _sb(n, d):
 
 
 SCRATCH = {
-    "Mi": _sb(W, I32), "Xb": _sb(W, BF), "Mf": _sb(GW, F32), "F": _sb(SW, F32), "Xs": _sb(SW, F32), "IO": _sb(GW, F32),
-    "VR": _sb(W, I32), "G": _sb(2048, F16), "Gf": _sb(2048, F32), "EQ": _sb(2048, BF), "XG": _sb(2048, BF), "AB": _sb(2048, BF),
-    "D16": _sb(2048, F16), "D32": _sb(2048, F32), "SE": _sb(144, BF), "SA": _sb(144, BF), "YX": _sb(SW // 4, BF), "YM": _sb(1024, F32),
+    "Mi": _sb(W, I32), "Xb": _sb(W, BF), "Mf": _sb(GW, F32), "F": _sb(GW, F32), "Xs": _sb(SW, F32), "IO": _sb(GW, F32),
+    "VR": _sb(W, I32), "G": _sb(2048, F16), "Gf": _sb(3072, F32), "EQ": _sb(2048, BF), "XG": _sb(2048, BF), "AB": _sb(2048, BF),
+    "D16": _sb(2048, F16), "T16": _sb(128, F16), "I16": _sb(128, F16), "SE": _sb(144, BF), "SA": _sb(144, BF), "YX": _sb(SW // 4, BF), "YM": _sb(1024, F32),
     "s4": _sb(4, U16), "UO": _sb(4, U16), "XO": _sb(64, BF),
     "FX32": _sb(512, F32), "I": _sb(128, BF), "NI": _sb(128, BF), "NL": _sb(128, BF), "NU": _sb(128, BF),
     "ONE": _sb(128, BF), "I32": _sb(128, F32), "NI32": _sb(128, F32), "ONE32": _sb(128, F32), "SH": _sb(128, F32), "IR": _sb(256, F32),
@@ -37,20 +40,45 @@ SCRATCH = {
     "BV": _sb(256, F32), "BC": _sb(256, F32), "MV": _sb(256, F32), "MC": _sb(256, F32), "VF": _sb(32, F32), "LO": _sb(256, F16),
     "VO": _sb(16, U16), "CN": _sb(16, F32), "AI": _sb(4, I32),
     "s1": _sb(16, F32), "s3": _sb(16, F32), "SMO": _sb(16, U16), "CL": _sb(256, I32), "XC": _sb(256, F32), "SY": _sb(256, F32),
-    "X2": _sb(256, F32), "PB": _sb(256, F32),
+    "X2": _sb(256, F32), "PB": _sb(256, F32), "DU": _sb(16, F32), "VM": _sb(16, F32), "VL": _sb(16, U16), "LV": _sb(256, F32),
+    "T1": _sb(W, I32), "T2": _sb(W, I32), "N12": _sb(256, U16), "N13": _sb(256, U16), "N23": _sb(256, U16),
     "pd0": ("psum", [128, 1024], F32), "pd1": ("psum", [128, 1024], F32), "pa": ("psum", [128, 512], F32),
     "pb": ("psum", [128, 512], F32), "k0": ("psum", [128, 512], F32), "k1": ("psum", [128, 512], F32),
 }
 ALIAS = {"D0": ("U", 128), "B": ("NR", 128), "J16": ("P", 256)}
 SEMAPHORES = (["cv", "cs", "cp", "cg", "sent", "lth", "lx", "oym", "oyx", "oyp", "pi0", "pi1"] + ["lm%d" % i for i in range(4)]
+              + ["go", "c1", "c2", "c3", "N12", "N13", "N23", "sN12", "sN13", "sN23"] + ["h%d" % i for i in range(4)] + ["sh%d" % i for i in range(4)]
               + ["a%d" % i for i in range(RO)] + ["e%d" % i for i in range(RO)] + ["b%d" % i for i in range(RO)])
-CYC, PEC, LAT, HOP1, HOP2 = 1.04, 0.52, 70.0, 3000.0, 3800.0
+CYC, PEC, LAT, HOP1, HOP2 = 1.0, 0.5, 90.0, 1500.0, 1900.0
+VFIX, SFIX, GATH, SCAT = 50.0, 80.0, 1.56, 3.8
+
+
+def helpers(core, T, topo):
+    return [h for h in topo.cores_of(core) if topo.die(h) != topo.die(core) and all(topo.may_write(h, x) for x in T.cores)][:2]
+
+
+def helper_program(g, core, T, topo):
+    N = len(T.cores)
+    for q, own in enumerate(T.cores):
+        if LOCAL and core in helpers(own, T, topo):
+            half = helpers(own, T, topo).index(core); sent = 0
+            n = bin(topo.mask(own, core) & ~topo.mask(own, T.cores[(q + 1) % N])).count("1")
+            for t in LOCAL:
+                dst = T.cores[(q - 1 - t % (N - 1)) % N]; rid, pid, _se = topo.addr(dst)
+                if COPY[t] == "Mi":
+                    g.wait_ge(T.sem.go, 1)
+                for c in (2 * half, 2 * half + 1):
+                    g.wait_ge(T.sem["h%d" % c], n)
+                    g.remote_dma(T[COPY[t]][:, 1024 * c:1024 * c + 1024], T.Mi[:, 1024 * c:1024 * c + 1024], T.sem["c%d" % t], T.sem.sent,
+                                 pid, rid, topo.mask(core, dst))
+                    sent += len(topo.engines(core, dst))
+            g.wait_ge(T.sem.sent, sent)
 
 
 def rank_program(g, core, T, topo):
     r = T.rank_of(core)
     if r is None:
-        return
+        return helper_program(g, core, T, topo)
     N = len(T.cores)
     ops = []
     Q = {"v": g.vector, "s": g.scalar, "p": g.tensor, "g": g, "y": g.sync}
@@ -84,13 +112,13 @@ def rank_program(g, core, T, topo):
 
     def vcost(o, ins, two=False):
         if o["ind"]:
-            return 50 + 3.8 * CYC * o["n"]
+            return 50 + SCAT * CYC * o["n"]
         if ins[0]["ind"]:
-            return 50 + 1.56 * CYC * o["n"]
+            return 50 + GATH * CYC * o["n"]
         f = 0.5 if all(size[SCRATCH[x["name"]][2]] == 2 for x in [o] + ins) else 1.0
         if two and not any(psum(x) for x in ins):
             f *= 2
-        return 30 + CYC * max(64, f * o["n"])
+        return VFIX + CYC * max(64, f * o["n"])
 
     def ap(x):
         return x["ap"] if isinstance(x, dict) else x
@@ -113,15 +141,15 @@ def rank_program(g, core, T, topo):
         return op("v", lambda: g.vector.transpose(o["ap"], a["ap"]), [o], [a], vcost(o, [a]))
 
     def MS(o, val):
-        return op("v", lambda: g.vector.memset(o["ap"], val), [o], [], 30 + CYC * max(64, o["n"] * size[SCRATCH[o["name"]][2]] / 4))
+        return op("v", lambda: g.vector.memset(o["ap"], val), [o], [], VFIX + CYC * max(64, o["n"] * size[SCRATCH[o["name"]][2]] / 4))
 
     def RED(o, a):
         return op("v", lambda: g.vector.tensor_reduce(o["ap"], a["ap"], AxisListType.X, OP.add), [o], [a], 100)
 
     def ACT(o, a, f, bias=0.0, scale=1.0, acc=None):
-        c = 65 + 1.56 * CYC * o["n"] if a["ind"] else 40 + CYC * max(64, o["n"])
+        c = 65 + GATH * CYC * o["n"] if a["ind"] else SFIX + CYC * max(64, o["n"])
         if o["ind"]:
-            return op("s", lambda: g.scalar.activation(o["ap"], a["ap"], f), [o], [a], 65 + 3.8 * CYC * o["n"])
+            return op("s", lambda: g.scalar.activation(o["ap"], a["ap"], f), [o], [a], 65 + SCAT * CYC * o["n"])
         if acc is not None:
             return op("s", lambda: g.scalar.activation(o["ap"], a["ap"], f, bias=bias, scale=scale, accum_out=acc["ap"]), [o, acc], [a], c + 20)
         return op("s", lambda: g.scalar.activation(o["ap"], a["ap"], f, bias=ap(bias), scale=ap(scale)), [o], [a, bias, scale], c)
@@ -147,10 +175,12 @@ def rank_program(g, core, T, topo):
     def col(i):
         return R("col", i, i + 1)
 
-    PM, PG, H0, H1, K15, THC, WC, AF_ = range(8)
+    PM, PG, H0, H1, K15, THC, WC, AF_, THL = range(9)
     lanes = lambda name, t, c0=0, c1=4: R(name, 1024 * c0 + 4 * t + r, 1024 * c1, 16)
     voted = lambda t: (r - 1 - t % (N - 1)) % N
     voter = lambda t: (r + 1 + t % (N - 1)) % N
+    owner = lambda t: r if t in LOCAL else voted(t)
+    landed = lambda t: sum(2 * len(topo.engines(h, core)) for h in helpers(T.cores[voter(t)], T, topo))
 
     j = DMA("y", T.Xb[:], T.xv[:], [R("Xb")], [], "lx", LOAD[0])
     for c in range(4):
@@ -167,15 +197,18 @@ def rank_program(g, core, T, topo):
 
     def vrep(t, after=()):
         js = [IOTA(R("VR", 1024 * c, 1024 * c + 1024), [[16, 64], [0, 16]], 1024 * c + 4 * t + r) for c in range(4)]
-        js.append(IOTA(R("VV"), [[16, 256]], 4 * t + voted(t)))
-        js.append(IOTA(R("VU"), [[16, 256]], 4 * t + voted(t) + int(UP)))
+        js.append(IOTA(R("VV"), [[16, 256]], 4 * t + owner(t)))
+        js.append(IOTA(R("VU"), [[16, 256]], 4 * t + owner(t) + int(UP)))
         js += [IOTA(R(nm, 704, 768), [[4, 64]], void + int(UP)) for nm in ("CC", "CV")]
         for j in js:
             ops[j]["after"] += list(after)
-    vrep(0)
+    IOTA(R("IO", 0, GW // 8), [[1, GW // 8]], 0)
+    vrep(0, [o["id"] for o in ops if o["eng"] == "g"])
     op("g", lambda: g.partition_broadcast(T.TH8[:], T.TH1[0:1, 0:8], 128), [R("TH8")], [R("TH1")], 200)
-    for c in range(4):
-        IOTA(R("IO", GW // 4 * c, GW // 4 * (c + 1)), [[1, GW // 4]], GW // 4 * c)
+    for c in range(8):
+        ACT(R("F", GW // 8 * c, GW // 8 * (c + 1)), R("IO", 0, GW // 8), AF.Identity, bias=BIG + GW // 8 * c)
+        if c:
+            ACT(R("IO", GW // 8 * c, GW // 8 * (c + 1)), R("IO", 0, GW // 8), AF.Identity, bias=float(GW // 8 * c))
     TS(R("pidx", 1, 2), R("pidx", 0, 1), 15, OP.bitwise_and); CP_(col(PM), R("pidx", 1, 2))
     TS(R("pidx", 2, 3), R("pidx", 0, 1), 4, OP.arith_shift_right); CP_(col(PG), R("pidx", 2, 3))
     TS(R("pidx", 3, 4), R("pidx", 0, 1), 16, OP.bitwise_and)
@@ -204,44 +237,62 @@ def rank_program(g, core, T, topo):
     TT(R("P2", 0, 128), R("P2", 0, 128), R("RM"), OP.mult); TT(R("SH"), R("P2", 0, 128), R("N2", 128, 256), OP.add)
     for k in range(16):
         TS(R("D16", 128 * k, 128 * k + 128), R("I32"), R("KH", k, k + 1), OP.mult)
-        ACT(R("D32", 128 * k, 128 * k + 128), R("I32"), AF.Identity, scale=R("KH", k, k + 1))
+    CP_(R("I16"), R("I32"))
     TT(R("THF"), R("TH8"), R("B", 0, 128, 16), OP.mult); RED(col(THC), R("THF"))
-    TS(col(THC), col(THC), 1.0 / 1024, OP.add); TS(col(WC), col(THC), 256.0, OP.mult)
-    MS(R("Mf", W, GW), 0.0)
+    TS(col(THL), col(THC), -255.0 / 256, OP.add); TS(col(THC), col(THC), 1.0 / 1024, OP.add); TS(col(WC), col(THC), 256.0, OP.mult)
+    for q in range(N):
+        TS(R("DU", 4 * q, 4 * q + 4), R("IOF", 0, 4), 4.0 / 8192, OP.mult, (GW + q) / 8192.0, OP.add)
+    copies = []
+    if LOCAL:
+        for c in (0, 2, 1, 3):
+            h = helpers(core, T, topo)[c // 2]; rid, pid, _se = topo.addr(h)
+            msk = topo.mask(core, h) & ~topo.mask(core, T.cores[voter(0)]); x = R("Mi", 1024 * c, 1024 * c + 1024)
+            j = op("g", lambda x=x, c=c, a=(pid, rid, msk): g.remote_dma(x["ap"], x["ap"], T.sem["h%d" % c], T.sem["sh%d" % c], *a),
+                   [], [R("Mi")], 500, lat=5000, sem=("sh%d" % c, bin(msk).count("1")))
+            ops[j]["own"] = True; copies.append(j)
+        for k, u in enumerate(LOCAL):
+            if COPY[u] != "Mi":
+                op(None, None, [R(COPY[u])], [], 0, lat=COPY_NS * (k + 1), sem=("c%d" % u, landed(u)), after=[j])
+    MS(R("Mf", W, GW), 0.0); MS(R("LV", 0, 64), 0.0)
     for c in range(8):
         ACT(R("Xs", 512 * c, 512 * c + 512), R("Xb", 512 * c, 512 * c + 512), AF.Identity, bias=HI)
         CP_(R("Mf", 512 * c, 512 * c + 512), R("Mi", 512 * c, 512 * c + 512))
-    for c in range(4):
-        ACT(R("F", GW // 4 * c, GW // 4 * (c + 1)), R("IO", GW // 4 * c, GW // 4 * (c + 1)), AF.Identity)
     for t in range(1, RO):
         CP_(R("O0", 256 * t - 256, 256 * t), lanes("Mi", t))
     XA = R("Xs", W, W + 256)
     ACT(XA, lanes("Xb", 0), AF.Identity, bias=HI)
 
     nsent = [0]
-    marks = []
+    marks = []; alike = []
 
     def ch(name, c, w=64):
         return R(name, w * c, w * c + w)
 
-    def follow(c, src, dst, by_act, last):
-        pm = R((("pa", "pb") if last else ("k0", "k1"))[c % 2], 0, 64)
-        b = 1024 * (c % 2)
-        if by_act:
-            ACT(R("Gf", b, b + 1024), IN("F", W, src), AF.Identity, bias=-2048.0)
+    def follow(src, at, dst, lo, hi, by, bank):
+        n = hi - lo; pm = R(bank, 0, n)
+        if by == "s":
+            b = 16 * (lo - 64)
+            for x in range(lo, hi, 64):
+                y = min(x + 64, hi)
+                ACT(R("Gf", 16 * (x - 64), 16 * (y - 64)), IN("F", W, R(src, at + x, at + y)), AF.Identity, bias=-BIG - 2048)
+            part = lambda name, c0, c1, step=None: dict(R(name, c0, c1, step), ap=T[name][0:n, c0:c1:step or 1])
             for k4 in range(0, 16, 4):
-                MM([(pm, ch("D32", k, 128), R("Gf", b + k, b + 1024, 16), k == 0, k == 15) for k in range(k4, k4 + 4)])
+                MM([(part(bank, 128 + k, 256, 16), R("Gf", b + k, b + 16 * n, 16), R("I32", k, 128, 16), k == 0, k == 15) for k in range(k4, k4 + 4)])
+            CP_(part("T16", 0, 128), part(bank, 128, 256))
+            MM([(pm, part("T16", 0, 128), part("I16", 0, n), True, True)])
         else:
-            TS(R("G", b, b + 1024), IN("F", W, src), -2048.0, OP.add)
-            MM([(pm, ch("D16", k, 128), R("G", b + k, b + 1024, 16), k == 0, k == 15) for k in range(16)])
-        TS(ch(dst, c), pm, 2048.0, OP.add)
-        if last:
-            TS(ch("M2", c), pm, WHOLE + 2048, OP.add, -WHOLE, OP.add)
-            steps(c, ch("M2", c))
+            b = 16 * lo % 2048
+            TS(R("G", b, b + 16 * n), IN("F", W, R(src, at + lo, at + hi)), -BIG - 2048, OP.add)
+            MM([(pm, ch("D16", k, 128), R("G", b + k, b + 16 * n, 16), k == 0, k == 15) for k in range(16)])
+        TS(R(dst, lo, hi), pm, 2048.0, OP.add)
+        if dst == "OB":
+            TS(R("M2", lo, hi), pm, WHOLE + 2048, OP.add, -WHOLE, OP.add)
+            if hi % 64 == 0:
+                steps(hi // 64 - 1, bank)
 
-    def steps(c, names):
-        pn = R(("pa", "pb")[c % 2], 64, 128)
-        MM([(pn, R("SH"), names, True, True)])
+    def steps(c, bank):
+        pn = R(bank, 64, 128)
+        MM([(pn, R("SH"), ch("M2", c), True, True)])
         TR(ch("PT", c), pn)
 
     def score(t, c):
@@ -255,7 +306,9 @@ def rank_program(g, core, T, topo):
             MM([(ch(pd, k), R("NI"), lanes("Xb", t, c, c + 1), k == ks[0], False) for k in ks])
             MM([(ch(pd, k), R("I"), R("XG", b + k, b + 1024, 16), False, k == ks[-1]) for k in ks])
             ACT(R("AB", b + 512 * hf, b + 512 * hf + 512), ch(pd, hf, 512), AF.Abs)
-        TT(R("EQ", b, b + 1024), IN("Mi" if t == 0 else "Mf", W, ch("OB", c)), ch("VR", c, 1024), OP.is_equal)
+        j = TT(R("EQ", b, b + 1024), IN("Mi" if t == 0 else "Mf", W, ch("OB", c)), ch("VR", c, 1024), OP.is_equal)
+        if t == 0 and c == 3:
+            ops[j]["after"] += copies
         bank = "k0" if c < SPLIT else "k1"
         key = ch(bank, c); own = range(SPLIT) if c < SPLIT else range(SPLIT, 4)
         if c == own[0]:
@@ -275,11 +328,17 @@ def rank_program(g, core, T, topo):
         fx = lambda at, x, k, a, z: [(R("pd0", at + s0 + h, at + s1, 2), ch("FX32", 2 * h + q, 128), R(x, lo + k + 16 * q, hi, 32), a and h + q == 0, z and h + q == 2)
                                      for h in range(2) for q in range(2)]
         MM(fx(512, "PT", 0, True, False))
-        MM(fx(0, "P", 15, True, True))
+        MM(fx(0, "P", 15, True, t not in LOCAL))
+        if t in LOCAL:
+            MM([(dict(m[0], **R("pb", s0 + k // 2, s1, 2)),) + m[1:] for k, m in enumerate(fx(0, "P", 15, True, True))])
+            TS(R("s1", s0, s1), R("pb", s0, s1), -1.0e6, OP.is_lt, 8192.0, OP.mult)
         SCAN(R("U", lo, hi), R("PT", lo, hi), R("NR", lo, hi), 0.0, OP.add, OP.mult)
-        TS(R("O1", m1, m2), R("pd0", s0, s1), -1.0 / 256, OP.mult, col(WC), OP.add)
+        if t not in LOCAL:
+            TS(R("O1", m1, m2), R("pd0", s0, s1), -1.0 / 256, OP.mult, col(WC), OP.add)
         MM(fx(512, "U", 15, False, True))
         CP_(R("O1", m0, m1), R("pd0", 512 + s0, 512 + s1))
+        if t in LOCAL:
+            return
         dst = T.cores[voter(t)]; rid, pid, _se = topo.addr(dst); sem = ("a%d" if lo else "e%d") % t
         o1 = R("O1", m0, m2); l1 = R("L1", m0, m2)
         s = op("g", lambda: g.remote_dma(l1["ap"], o1["ap"], T.sem[sem], T.sem.sent, pid, rid, topo.mask(core, dst)), [], [o1], 500, sem="remote")
@@ -289,20 +348,29 @@ def rank_program(g, core, T, topo):
     def vote(t, lo, hi):
         m0 = 32 * t + lo // 8; m1 = m0 + (hi - lo) // 16; m2 = m1 + (hi - lo) // 16
         s0, s1 = lo // 16, hi // 16
-        co = R("L1", m0, m1)
-        TT(R("E1", lo, hi), IN("Mi" if t == 0 else "Mf", W, co), R("VV", lo, hi), OP.is_equal)
-        TS(R("NF", s0, s1), R("L1", m1, m2), -255.0, OP.add, 256.0, OP.mult)
-        ACT(R("BC", lo, hi), IN("IO", W, co), AF.Identity, bias=UP)
-        MM([(R("k0", s0, s1), into("SE", k), R("E1", lo + k, hi, 16), k == 0, k == 15) for k in range(16)])
-        TT(R("PS", s0 + 1, s1 + 1), R("k0", s0, s1), R("NF", s0, s1), OP.is_ge)
-        TT(R("NP", s0, s1), R("k0", s0, s1), R("NF", s0, s1), OP.is_lt)
+        if t in LOCAL:
+            co = R("O1", m0, m1); sums = R("pd0", s0, s1)
+            TT(R("E1", lo, hi), IN(COPY[t], W, co), R("VV", lo, hi), OP.is_equal)
+            ACT(R("BC", lo, hi), IN("IO", W, co), AF.Identity, bias=UP)
+            MM([(sums, into("SE", k), R("E1", lo + k, hi, 16), False, k == 15) for k in range(16)])
+            TS(R("PS", s0 + 1, s1 + 1), sums, col(WC), OP.is_ge)
+            TS(R("NP", s0, s1), sums, col(WC), OP.is_lt)
+        else:
+            co = R("L1", m0, m1)
+            TT(R("E1", lo, hi), IN("Mi" if t == 0 else "Mf", W, co), R("VV", lo, hi), OP.is_equal)
+            TS(R("NF", s0, s1), R("L1", m1, m2), -255.0, OP.add, 256.0, OP.mult)
+            ACT(R("BC", lo, hi), IN("IO", W, co), AF.Identity, bias=UP)
+            MM([(R("k0", s0, s1), into("SE", k), R("E1", lo + k, hi, 16), k == 0, k == 15) for k in range(16)])
+            TT(R("PS", s0 + 1, s1 + 1), R("k0", s0, s1), R("NF", s0, s1), OP.is_ge)
+            TT(R("NP", s0, s1), R("k0", s0, s1), R("NF", s0, s1), OP.is_lt)
         MM([(R("k1", s0, s1), R("NL"), R("PS", s0 + 1, s1 + 1), True, False), (R("k1", s0, s1), R("NU"), R("PS", s0, s1), False, True)])
         TT(R("QQ", s0, s1), R("NP", s0, s1), R("Q0", s0, s1), OP.mult)
         SCAN(R("SN", s0, s1), R("k1", s0, s1), R("Z16", s0, s1), R("SN", s0 - 1, s0) if lo else 767.0, OP.add, OP.add)
         TT(R("SL", s0, s1), R("SN", s0, s1), R("QQ", s0, s1), OP.subtract)
-        CP_(R("SO", s0, s1), R("SL", s0, s1))
+        j = CP_(R("SO", s0, s1), R("SL", s0, s1))
         CP_(IN("CC", 768, R("SO", s0, s1)), R("BC", lo, hi))
         ACT(IN("CV", 768, R("SO", s0, s1)), R("VU", lo, hi), AF.Silu)
+        return j
 
     def yx(t, src, less):
         ACT(R("X2"), lanes("Xb", t), AF.Identity, bias=256.0)
@@ -312,34 +380,48 @@ def rank_program(g, core, T, topo):
 
     halves = [(0, 64 * SPLIT), (64 * SPLIT, 256)] if SPLIT else [(0, 256)]
     for t in range(RO):
-        rho = voted(t)
+        rho = owner(t)
         last = t == RO - 1
         if t == 0:
             for c in range(4):
                 CP_(ch("OB", c), lanes("Mi", 0, c, c + 1))
                 CP_(ch("M2", c), lanes("Mi", 0, c, c + 1))
-                steps(c, ch("M2", c))
+                steps(c, ("pa", "pb")[c % 2])
         else:
-            order = [(0, 0), (1, 0), (0, 1), (2, 0), (1, 1), (3, 0), (2, 1), (3, 1)]
-            for c, step in order:
-                if step == 0:
-                    follow(c, ch("O0", 4 * t - 4 + c), "OA", c in ACT_G1, False)
+            alike.append([len(ops)])
+            for step, lo, hi, by, bank in FOLLOW:
+                if step == 1:
+                    follow("O0", 256 * t - 256, "OA", lo, hi, by, bank)
                 else:
-                    follow(c, ch("OA", c), "OB", c in ACT_G2, True)
+                    follow("OA", 0, "OB", lo, hi, by, bank)
+            alike[-1] = list(range(alike[-1][0], len(ops)))
+        if t in LOCAL:
+            for u in range(1, t):
+                CP_(R(COPY[t], 4 * u + voter(t), W, 16), R("N%d%d" % (u, t)))
         if last:
             DMA("y", T.PB[:], T.Xs[0:128:16, 0:W], [R("PB")], [R("Xs", 0, W)], "pi0", 2500)
             ACT(R("PB"), R("PB"), AF.Abs); ACT(R("PB"), R("PB"), AF.Identity, bias=WHOLE - BIG)
             ACT(R("PB"), R("PB"), AF.Relu, bias=1.0 - WHOLE); ACT(R("PB"), R("PB"), AF.Identity, bias=-1.0)
             DMA("y", T.F[0:128:16, 0:W], T.PB[:], [R("F", 0, W)], [R("PB")], "pi1", 2500)
+        j = len(ops)
         for c in range(4):
             score(t, c)
             if c == SPLIT - 1:
                 choose(t, *halves[0])
+        if t:
+            alike[-1] += list(range(j, len(ops)))
         choose(t, *halves[-1])
         if t:
             yx(t - 1, lanes("Xs", t - 1), 0.0)
         for lo, hi in halves:
-            vote(t, lo, hi)
+            s0, s1 = lo // 16, hi // 16
+            if t not in LOCAL:
+                TS(R("s1", s0, s1), R("O1", 32 * t + s0 + s1, 32 * t + 2 * s1), 12000.0, OP.is_ge, 8192.0, OP.mult)
+            CP_(R("s3", s0, s1), R("O1", 32 * t + 2 * s0, 32 * t + s0 + s1))
+        TT(R("s3"), R("s3"), R("s1"), OP.add); TT(R("s3"), R("s3"), R("DC"), OP.min)
+        smo = CP_(R("SMO"), R("s3"))
+        for lo, hi in halves:
+            ops[vote(t, lo, hi)]["after"].append(smo)
         for hf, nm in enumerate(("CC", "CV")):
             TT(ch("MK", hf), R(nm, 704, 768), ch("KH", 0), OP.mult)
             SCAN(ch("SC", hf), ch("RM", 0), ch("MK", hf), 0.0, OP.mult, OP.add)
@@ -361,12 +443,20 @@ def rank_program(g, core, T, topo):
         s = op("g", lambda tr=tr: g.remote_dma_fused([tr], local_sem=T.sem.sent), [], [lz(rho, 0, 8)], 500, sem="remote")
         nsent[0] += ne; marks.append(s)
         op(None, None, [lz(q, 0, 8) for q in range(N) if q != rho], [], 0, lat=HOP2, sem=("b%d" % t, ne * (N - 1)), after=[s])
-        for lo, hi in halves:
-            s0, s1 = lo // 16, hi // 16
-            TS(R("s1", s0, s1), R("O1", 32 * t + s0 + s1, 32 * t + 2 * s1), 12000.0, OP.is_ge, 8192.0, OP.mult)
-            CP_(R("s3", s0, s1), R("O1", 32 * t + 2 * s0, 32 * t + s0 + s1))
-        TT(R("s3"), R("s3"), R("s1"), OP.add); TT(R("s3"), R("s3"), R("DC"), OP.min)
-        CP_(R("SMO"), R("s3"))
+        for u in LOCAL:
+            if 0 < t < u:
+                slot = "N%d%d" % (t, u); dst = T.cores[voted(u)]; rid, pid, _se = topo.addr(dst); n = len(topo.engines(core, dst))
+                j = op("g", lambda slot=slot, a=(pid, rid, topo.mask(core, dst)): g.remote_dma(T[slot][:], T.OB[:], T.sem[slot], T.sem["s" + slot], *a),
+                       [], [R("OB"), lz(0, 0, 32)], 500, lat=3000, sem=("s" + slot, n))
+                ops[j]["own"] = True
+                op(None, None, [R(slot)], [], 0, lat=4000, sem=(slot, len(topo.engines(T.cores[voter(u)], core))), after=[j])
+        if t == 1 and COPY.get(RO - 1) == "Mi":
+            ops[s]["wait"] = [o["id"] for o in ops if o["eng"] is not None and any(x[0] == "Mi" for x in o["rd"])]
+            sig = [RemoteDMATransfer(dst_ids=[DstId(rid=topo.addr(h)[0], pnc=topo.addr(h)[1])], dma_engine_mask=1 << topo.engines(core, h)[-1 - k],
+                                     remote_sem=T.sem.go) for k, h in enumerate(helpers(core, T, topo))]
+            j = op("g", lambda: g.remote_dma_fused(sig, local_sem=T.sem.sent), [], [lz(0, 0, 32)], 500, sem="remote")
+            nsent[0] += len(sig)
+            op(None, None, [R("Mi")], [], 0, lat=COPY_NS, sem=("c%d" % (RO - 1), landed(RO - 1)), after=[j])
         ACT(R("XC"), IN("Xs", W + 256, R("SMO")), AF.Identity, bias=-0.5)
         MM([(R("pd1", 0, 256), R("I32"), XA, True, False)]); MM([(R("pd1", 0, 256), R("I32"), R("XC"), False, True)])
         ACT(R("SY"), R("pd1", 0, 256), AF.Identity, bias=WHOLE, scale=0.5)
@@ -392,45 +482,56 @@ def rank_program(g, core, T, topo):
         val = "BV" if last else "MV"
         for q in range(N - 1, -1, -1):
             if not last:
-                ACT(ch("MV", q), IN("Mf", GW, lz(q, 4, 8)), AF.Identity, bias=q / 16.0)
+                ACT(ch("MV", q), IN("Mf", GW, lz(q, 4, 8)), AF.Identity, bias=BIG + q / 16.0)
             ACT(ch("BV", q), IN("IO", GW, lz(q, 4, 8)), AF.Identity, bias=add)
-        TS(R("VF"), lz(0, 0, 32), 1.0 / GW, OP.mult)
+        TS(R("VF"), lz(0, 0, 32), 1.0 / 8192, OP.mult)
         for q in range(N - 1, -1, -1):
             CP_(IN("F", GW, lz(q, 0, 4)), ch(val, q))
         for q in range(N):
             if not last:
-                ACT(ch("MC", q), IN("Mf", GW, lz(q, 0, 4)), AF.Identity)
+                ACT(ch("MC", q), IN("Mf", GW, lz(q, 0, 4)), AF.Identity, bias=BIG)
             ACT(ch("BC", q), IN("IO", GW, lz(q, 0, 4)), AF.Identity, bias=add)
         for q in range(1, N):
             TT(ch("LO", q), IN("F", GW, lz(q, 0, 4)), ch(val, q), OP.not_equal)
-        MM([(R("pa", 4 * q, 4 * q + 4), R("I32"), R("VF", 8 * q + 4, 8 * q + 8), q == 0, False) for q in range(N)])
+        for bank in ("pb", "pa"):
+            MM([(R(bank, 4 * q, 4 * q + 4), R("I32"), R("VF", 8 * q + 4, 8 * q + 8), q == 0, bank == "pb" and q == N - 1) for q in range(N)])
+        TS(R("VL"), R("pb", 0, 16), 8192.0, OP.mult)
         MM([(R("pa", 4, 16), ch("D16", k, 128), R("LO", 64 + k, 256, 16), False, k == 15) for k in range(16)])
-        vval = "BC" if last else "MC"
-        CP_(IN("F", GW, lz(0, 4, 8)), ch(vval, 0))
-        TS(R("VO"), R("pa", 0, 16), float(GW), OP.mult, 0.25, OP.add)
-        CP_(IN("F", SW, R("VO", 4, 16)), R(vval, 64, 256))
+        vval = "BC" if last else "MC"; diff = R("k0", 64, 256)
+        MM([(diff, R("NI32"), R(vval, 64, 256), True, False)])
+        if last:
+            MM([(R("k0", 64, 192), R("NI"), R("ONE"), False, False), (R("k0", 192, 256), R("NI"), R("ONE", 0, 64), False, True)])
+        else:
+            MM([(diff, R("I32"), R("BV", 64, 256), False, True)])
+        TT(R("LV", 64, 256), diff, R("LO", 64, 256), OP.mult)
+        TT(IN("F", GW, R("VL")), R("LV"), R(vval), OP.add)
+        TT(R("VM"), R("pa", 0, 16), R("DU"), OP.min)
         if not last:
+            TS(R("VO"), R("VM"), 8192.0, OP.mult)
             for q in range(N - 1, -1, -1):
                 ACT(IN("Xs", GW, lz(q, 0, 4)), ch("BV", q), AF.Silu)
             ACT(XA, lanes("Xs", t + 1), AF.Abs)
             ACT(R("LP"), XA, AF.Relu, bias=-(HI + 255) * 128, scale=128.0)
             ACT(IN("Xs", SW, R("VO")), R("BC"), AF.Silu)
-            ACT(R("CN"), R("pa", 0, 16), AF.Sign, bias=(W - 0.5) / GW, scale=-1.0, acc=col(AF_))
+            ACT(R("CN"), R("VM"), AF.Sign, bias=(W - 0.5) / 8192, scale=-1.0, acc=col(AF_))
             MM([(R("pb", 0, 1), R("ONE32"), col(AF_), True, True)])
             TS(R("AI", 0, 1), R("pb", 0, 1), 0.5, OP.mult, 1024.0, OP.add); TS(R("AI", 1, 2), R("AI", 0, 1), 3, OP.bitwise_and)
-            TS(col(WC), R("AI", 1, 2), col(THC), OP.add, 256.0, OP.mult)
+            if t + 1 in LOCAL:
+                TS(col(WC), R("AI", 1, 2), col(THL), OP.add, 65536.0, OP.mult)
+            else:
+                TS(col(WC), R("AI", 1, 2), col(THC), OP.add, 256.0, OP.mult)
         else:
             TS(R("s4"), lz(r, 4, 8), float(W - 1), OP.min)
             ACT(R("XO"), IN("Xb", W, R("s4")), AF.Identity)
-            TS(R("UO"), R("pa", 4 * r, 4 * r + 4), GW / 4.0, OP.mult, 0.1 - r / 4.0, OP.add)
+            TS(R("UO"), R("VM", 4 * r, 4 * r + 4), 2048.0, OP.mult, 0.1 - r / 4.0, OP.add)
             CP_(IN("YX", SW // 4, R("UO")), R("XO"))
             DMA("y", T.yp[:], T.F[0:128:16, 0:W], [], [R("F", 0, W)], "oyp", 2800)
             DMA("s", T.yx[:], T.YX[:, 0:1024], [], [R("YX", 0, 1024)], "oyx", 3400)
 
-    emit(g, T, Q, ops, nsent[0], marks)
+    emit(g, T, Q, ops, nsent[0], marks, alike)
 
 
-def emit(g, T, Q, ops, nsent, marks):
+def emit(g, T, Q, ops, nsent, marks, alike):
     def meet(a, b, banks):
         for (n, lo, hi) in a:
             for (m, l2, h2) in b:
@@ -462,6 +563,8 @@ def emit(g, T, Q, ops, nsent, marks):
                 o["dep"][j] = True
         for j in o["after"]:
             o["dep"][j] = False
+        for j in o.get("wait", []):
+            o["dep"][j] = True
     n = len(ops)
     succ = [[] for _ in range(n)]
     for o in ops:
@@ -508,63 +611,107 @@ def emit(g, T, Q, ops, nsent, marks):
     up = [0.0] * n
     for i in range(n - 1, -1, -1):
         up[i] = ops[i]["cost"] + max([w - ops[k]["cost"] + up[k] for k, w in nxt[i]] + [ops[i]["lat"]]) + 1e-3
-    seq = sorted(range(n), key=lambda i: (-up[i], i))
-    best = None
     rnd = [12345]
 
     def rand():
         rnd[0] = (rnd[0] * 1103515245 + 12345) % 2147483648
         return rnd[0] / 2147483648
 
-    def moved(key, picks):
+    def by_key(key):
         kk = list(key)
-        for i, d in picks:
-            kk[i] += d
-            todo = [i]
-            while todo:
-                x = todo.pop()
-                for j, w in (gp[x] if d < 0 else nxt[x]):
-                    if (kk[j] >= kk[x]) if d < 0 else (kk[j] <= kk[x]):
-                        kk[j] = kk[x] + (-1e-3 if d < 0 else 1e-3); todo.append(j)
         for i in range(n):
             for j, w in gp[i]:
                 if kk[j] >= kk[i]:
                     kk[i] = kk[j] + 1e-3
         return sorted(range(n), key=lambda i: (kk[i], i))
-    big = [i for i in range(n) if ops[i]["cost"] > 200]
+    cost = [o["cost"] for o in ops]; tail = [o["cost"] + o["lat"] for o in ops]; eng = [o["eng"] for o in ops]
 
-    def length(st):
-        return max(st[i] + ops[i]["cost"] + ops[i]["lat"] for i in range(n))
-    first = "key" not in PLAN
-    if not first:
-        seq = moved(PLAN["key"], [])
-    cur = place(seq, False)
-    best = (length(cur), cur)
+    def run(seq, base=None, last=None):
+        st, prev = ([0.0] * n, {}) if base is None else (list(base[0]), dict(base[1]))
+        by = {}
+        for i in seq:
+            t0 = 0.0; b = -1
+            for j, w in gp[i]:
+                if st[j] + w > t0:
+                    t0 = st[j] + w; b = j
+            e = eng[i]
+            if e is not None:
+                p = prev.get(e)
+                if p is not None and st[p] + cost[p] > t0:
+                    t0 = st[p] + cost[p]; b = -2 - p
+                prev[e] = i
+            st[i] = t0; by[i] = b
+        z = max(seq, key=lambda i: st[i] + tail[i]) if last is None else last
+        return st[z] + tail[z], st, by, z, prev
 
-    def parts(st):
-        m = [0.0] + [st[i] for i in marks] + [length(st)]
-        return m, [m[k + 1] - m[k] for k in range(len(m) - 1)]
-    tries = TRIES if first else TRIES // 10
-    for it in range(tries):
-        slack = SLACK * (1.0 - it / tries)
-        m, old = parts(cur)
-        if it % 40 == 0:
-            bk = place(sorted(range(n), key=lambda i: (-(cur[i] + ops[i]["cost"]), -i)), True)
-            st = place(moved([-bk[i] - ops[i]["cost"] for i in range(n)], []), False)
-        else:
-            picks = [(big[int(rand() * len(big))], (rand() - 0.5) * 6000.0 * rand()) for _ in range(8)]
-            st = place(moved(cur, picks), False)
-            new = parts(st)[1]
-            good = [(i, d) for i, d in picks if any(m[k] <= cur[i] < m[k + 1] and new[k] <= old[k] + slack for k in range(len(old)))]
-            if not good:
+    def better(seq, tries, slack, base=None, last=None):
+        now = run(seq, base, last); best = (now, seq); m = len(seq)
+        for it in range(tries):
+            span, st, by, z = now[:4]
+            pairs = []
+            while z in by:
+                b = by[z]
+                if b <= -2:
+                    b = -2 - b
+                    if b in by:
+                        pairs.append((b, z))
+                z = b
+            if not pairs:
+                break
+            u, v = pairs[int(rand() * len(pairs))]
+            if anc[v] >> u & 1:
                 continue
-            if len(good) < len(picks):
-                st = place(moved(cur, good), False)
-        span = length(st)
-        if span <= m[-1] + slack:
-            cur = st
-        if span < best[0]:
-            best = (span, st)
+            a, z = seq.index(u), seq.index(v)
+            ahead = rand() < 0.5
+            for more in range(int(rand() * rand() * 6)):
+                k = a - 1 if ahead else z + 1
+                while 0 <= k < m and eng[seq[k]] != eng[v]:
+                    k += -1 if ahead else 1
+                if not 0 <= k < m or (anc[v] >> seq[k] & 1 if ahead else anc[seq[k]] >> u & 1):
+                    break
+                a, z = (k, z) if ahead else (a, k)
+            mid = seq[a:z + 1]
+            if ahead:
+                mid = [i for i in mid if i == v or anc[v] >> i & 1] + [i for i in mid if not (i == v or anc[v] >> i & 1)]
+            else:
+                mid = [i for i in mid if not (i == u or anc[i] >> u & 1)] + [i for i in mid if i == u or anc[i] >> u & 1]
+            new = seq[:a] + mid + seq[z + 1:]
+            res = run(new, base, last)
+            if res[0] <= span + slack * (1.0 - it / tries) * rand():
+                now = res; seq = new
+                if it % 8 == 0:
+                    seq = sorted(seq, key=lambda i: res[1][i])
+                if res[0] < best[0][0]:
+                    best = (res, seq)
+        return best[1]
+
+    def tight(seq):
+        st = place(seq, False)
+        return sorted(seq, key=lambda i: st[i])
+    if "key" not in PLAN:
+        cur = place(sorted(range(n), key=lambda i: (-up[i], i)), False)
+        for it in range(6):
+            bk = place(sorted(range(n), key=lambda i: (-(cur[i] + cost[i]), -i)), True)
+            cur = place(by_key([-bk[i] - cost[i] for i in range(n)]), False)
+        seq = by_key(cur)
+        for turn in range(2):
+            for k in range(len(marks)):
+                a = seq.index(marks[k - 1]) + 1 if k else 0; z = seq.index(marks[k]) + 1
+                head = run(seq[:a]) if a else None
+                mid = better(seq[a:z], TRIES // 8, SLACK / (1 + 2 * turn), head and (head[1], head[4]), marks[k])
+                seq = tight(seq[:a] + mid + seq[z:])
+            st = run(seq)[1]
+            b = min(alike, key=lambda x: st[x[-1]] - st[x[0]])
+            for x in alike:
+                key = list(st)
+                for i, j in zip(x, b):
+                    key[i] = st[x[0]] + st[j] - st[b[0]]
+                new = better(tight(by_key(key)), TRIES // 100, SLACK / 10)
+                if run(new)[0] < run(seq)[0]:
+                    seq = new; st = run(seq)[1]
+    else:
+        seq = by_key(PLAN["key"])
+    best = run(better(seq, TRIES // 20, SLACK / 10))
     PLAN["key"] = best[1]; PLAN["span"] = best[0]
     start = best[1]
     end = [start[i] + ops[i]["cost"] for i in range(n)]
@@ -597,7 +744,7 @@ def emit(g, T, Q, ops, nsent, marks):
         if o["sem"] is None:
             if o["inc"]:
                 h.then_inc(T.sem[o["sig"][0]], 1)
-        elif o["sem"] != "remote":
+        elif o["sem"] != "remote" and not o.get("own"):
             h.then_inc(T.sem[o["sem"][0]], 16)
     for e in cnt:
         if cnt[e]:

@@ -8,12 +8,14 @@ F32, BF, F16, I32, U16 = "float32", "bfloat16", "float16", "int32", "uint16"
 FOLLOW = [(1, 0, 64, "v", "pa"), (1, 64, 128, "v", "pb"), (2, 0, 64, "v", "pa"), (1, 128, 256, "s", "k0"),
           (2, 64, 128, "v", "pb"), (2, 128, 192, "v", "pa"), (2, 192, 256, "v", "pb")]
 WAIT_W = True
-SPLIT = 0
-LOCAL = (2, 3)
-COPY = {2: "T1", 3: "T2"}
+SPLIT = 3
+VSPLIT = False
+T_BY, A_BY, M_BY = "s", "s", "s"
+LOCAL = (1, 2, 3)
+COPY = {1: "T1", 2: "T2", 3: "Mi"}
 COPY_NS = 25000.0
-LOAD = (6000.0, 2200.0)
-TRIES, SLACK = 200000, 2500.0
+LOAD = (5000.0, 1900.0)
+TRIES, SLACK = 190000, 2500.0
 PLAN = {}
 
 
@@ -23,16 +25,16 @@ def _sb(n, d):
 
 SCRATCH = {
     "Mi": _sb(W, I32), "Xb": _sb(W, BF), "Mf": _sb(GW, F32), "F": _sb(GW, F32), "Xs": _sb(SW, F32), "IO": _sb(GW, F32),
-    "VR": _sb(W, I32), "G": _sb(2048, F16), "Gf": _sb(3072, F32), "EQ": _sb(2048, BF), "XG": _sb(2048, BF), "AB": _sb(2048, BF),
-    "D16": _sb(2048, F16), "T16": _sb(128, F16), "I16": _sb(128, F16), "SE": _sb(144, BF), "SA": _sb(144, BF), "YX": _sb(SW // 4, BF), "YM": _sb(1024, F32),
-    "s4": _sb(4, U16), "UO": _sb(4, U16), "XO": _sb(64, BF),
+    "VR": _sb(W, I32), "G": _sb(2048, F16), "Gf": _sb(2048, F32), "EQ": _sb(2048, BF), "XG": _sb(2048, BF), "AB": _sb(2048, BF),
+    "D16": _sb(2048, BF), "T16": _sb(128, F16), "T32": _sb(128, F32), "I16": _sb(128, F16), "SE": _sb(144, BF), "SA": _sb(144, BF), "YX": _sb(SW // 4, BF), "YM": _sb(1024, F32),
+    "s4": _sb(4, U16), "UO": _sb(4, U16), "XO": _sb(128, BF),
     "FX32": _sb(512, F32), "I": _sb(128, BF), "NI": _sb(128, BF), "NL": _sb(128, BF), "NU": _sb(128, BF),
     "ONE": _sb(128, BF), "I32": _sb(128, F32), "NI32": _sb(128, F32), "ONE32": _sb(128, F32), "SH": _sb(128, F32), "IR": _sb(256, F32),
     "KH": _sb(128, F32), "KC": _sb(64, BF), "RS": _sb(256, F32), "RM": _sb(128, F32), "DM": _sb(256, F32),
     "pidx": _sb(8, I32), "col": _sb(16, F32), "IOF": _sb(16, F32), "Q0": _sb(16, F32), "C2": _sb(4, F32), "Z16": _sb(16, F32), "DC": _sb(16, F32),
     "TH1": _sb(8, I32), "TH8": _sb(8, I32), "THF": _sb(8, F32),
     "O0": _sb(768, U16), "OA": _sb(256, U16), "OB": _sb(256, U16), "M2": _sb(256, F32), "PEN": _sb(256, BF),
-    "LP": _sb(256, BF), "PT": _sb(256, F32), "P": _sb(256, F32), "NR": _sb(256, F32), "U": _sb(256, F32),
+    "LP": _sb(256, BF), "PT": _sb(512, F32), "P": _sb(512, F32), "NR": _sb(256, F32), "U": _sb(128, F32),
     "O1": _sb(128, U16), "L1": _sb(128, U16), "LZ": _sb(128, U16),
     "VV": _sb(256, F32), "VU": _sb(256, F32), "E1": _sb(256, BF), "NF": _sb(16, F32), "PS": _sb(18, BF), "NP": _sb(16, F32), "QQ": _sb(16, F32),
     "SN": _sb(16, F32), "SL": _sb(16, F32), "SO": _sb(16, U16), "CC": _sb(768, F32), "CV": _sb(768, F32), "MK": _sb(128, F32),
@@ -40,21 +42,30 @@ SCRATCH = {
     "BV": _sb(256, F32), "BC": _sb(256, F32), "MV": _sb(256, F32), "MC": _sb(256, F32), "VF": _sb(32, F32), "LO": _sb(256, F16),
     "VO": _sb(16, U16), "CN": _sb(16, F32), "AI": _sb(4, I32),
     "s1": _sb(16, F32), "s3": _sb(16, F32), "SMO": _sb(16, U16), "CL": _sb(256, I32), "XC": _sb(256, F32), "SY": _sb(256, F32),
-    "X2": _sb(256, F32), "PB": _sb(256, F32), "DU": _sb(16, F32), "VM": _sb(16, F32), "VL": _sb(16, U16), "LV": _sb(256, F32),
+    "X2": _sb(256, F32), "PB": _sb(256, F32), "DU": _sb(16, F32), "VM": _sb(16, F32), "WH": _sb(64, BF), "VL": _sb(16, U16), "LV": _sb(256, F32),
     "T1": _sb(W, I32), "T2": _sb(W, I32), "N12": _sb(256, U16), "N13": _sb(256, U16), "N23": _sb(256, U16),
     "pd0": ("psum", [128, 1024], F32), "pd1": ("psum", [128, 1024], F32), "pa": ("psum", [128, 512], F32),
     "pb": ("psum", [128, 512], F32), "k0": ("psum", [128, 512], F32), "k1": ("psum", [128, 512], F32),
 }
 ALIAS = {"D0": ("U", 128), "B": ("NR", 128), "J16": ("P", 256)}
 SEMAPHORES = (["cv", "cs", "cp", "cg", "sent", "lth", "lx", "oym", "oyx", "oyp", "pi0", "pi1"] + ["lm%d" % i for i in range(4)]
-              + ["go", "c1", "c2", "c3", "N12", "N13", "N23", "sN12", "sN13", "sN23"] + ["h%d" % i for i in range(4)] + ["sh%d" % i for i in range(4)]
+              + ["go", "sn0", "sn1", "c1", "c2", "c3", "N12", "N13", "N23", "sN12", "sN13", "sN23"] + ["h%d" % i for i in range(4)] + ["sh%d" % i for i in range(4)]
               + ["a%d" % i for i in range(RO)] + ["e%d" % i for i in range(RO)] + ["b%d" % i for i in range(RO)])
-CYC, PEC, LAT, HOP1, HOP2 = 1.0, 0.5, 90.0, 1500.0, 1900.0
-VFIX, SFIX, GATH, SCAT = 50.0, 80.0, 1.56, 3.8
+COSTS = [(1.0, 0.5, 90.0, 1500.0, 1900.0, 50.0, 80.0, 1.56, 3.8), (0.83, 0.45, 120.0, 1200.0, 1600.0, 60.0, 110.0, 1.56, 3.8)]
 
 
 def helpers(core, T, topo):
     return [h for h in topo.cores_of(core) if topo.die(h) != topo.die(core) and all(topo.may_write(h, x) for x in T.cores)][:2]
+
+
+def near(core, q, T, topo):
+    dst = T.cores[(q - 2) % len(T.cores)]
+    return [h for h in topo.cores_of(core) if h != core and topo.die(h) == topo.die(core) and topo.may_write(h, dst)][:2]
+
+
+def quarter_mask(core, helper, c, T, topo):
+    other = [x for x in T.cores if x != core][0]
+    return topo.mask(core, helper) & ~(topo.mask(core, other) if c % 2 else 0)
 
 
 def helper_program(g, core, T, topo):
@@ -62,23 +73,33 @@ def helper_program(g, core, T, topo):
     for q, own in enumerate(T.cores):
         if LOCAL and core in helpers(own, T, topo):
             half = helpers(own, T, topo).index(core); sent = 0
-            n = bin(topo.mask(own, core) & ~topo.mask(own, T.cores[(q + 1) % N])).count("1")
             for t in LOCAL:
                 dst = T.cores[(q - 1 - t % (N - 1)) % N]; rid, pid, _se = topo.addr(dst)
                 if COPY[t] == "Mi":
                     g.wait_ge(T.sem.go, 1)
-                for c in (2 * half, 2 * half + 1):
-                    g.wait_ge(T.sem["h%d" % c], n)
+                for c in (2 * half, 2 * half + 1)[:1 if t == 1 else 2]:
+                    g.wait_ge(T.sem["h%d" % c], bin(quarter_mask(own, core, c, T, topo)).count("1"))
                     g.remote_dma(T[COPY[t]][:, 1024 * c:1024 * c + 1024], T.Mi[:, 1024 * c:1024 * c + 1024], T.sem["c%d" % t], T.sem.sent,
                                  pid, rid, topo.mask(core, dst))
                     sent += len(topo.engines(core, dst))
             g.wait_ge(T.sem.sent, sent)
+        if 1 in LOCAL and core in near(own, q, T, topo):
+            c = 2 * near(own, q, T, topo).index(core) + 1; dst = T.cores[(q - 2) % N]; rid, pid, _se = topo.addr(dst)
+            g.wait_ge(T.sem["h%d" % c], bin(quarter_mask(own, core, c, T, topo)).count("1")); g.wait_ge(T.sem.go, 1)
+            g.remote_dma(T[COPY[1]][:, 1024 * c:1024 * c + 1024], T.Mi[:, 1024 * c:1024 * c + 1024], T.sem.c1, T.sem.sent, pid, rid, topo.mask(core, dst))
+            g.wait_ge(T.sem.sent, len(topo.engines(core, dst)))
 
 
 def rank_program(g, core, T, topo):
     r = T.rank_of(core)
     if r is None:
         return helper_program(g, core, T, topo)
+    plans = [calls(g, core, T, topo, r, costs) for costs in COSTS]
+    emit(g, T, *plans[0], [p[1] for p in plans])
+
+
+def calls(g, core, T, topo, r, costs):
+    CYC, PEC, LAT, HOP1, HOP2, VFIX, SFIX, GATH, SCAT = costs
     N = len(T.cores)
     ops = []
     Q = {"v": g.vector, "s": g.scalar, "p": g.tensor, "g": g, "y": g.sync}
@@ -175,7 +196,7 @@ def rank_program(g, core, T, topo):
     def col(i):
         return R("col", i, i + 1)
 
-    PM, PG, H0, H1, K15, THC, WC, AF_, THL = range(9)
+    PM, PG, H0, H1, K15, THC, WC, AF_, THL, THM, A1, A2 = range(12)
     lanes = lambda name, t, c0=0, c1=4: R(name, 1024 * c0 + 4 * t + r, 1024 * c1, 16)
     voted = lambda t: (r - 1 - t % (N - 1)) % N
     voter = lambda t: (r + 1 + t % (N - 1)) % N
@@ -235,10 +256,16 @@ def rank_program(g, core, T, topo):
     TS(R("N2", 0, 128), R("D0"), 1.0, OP.is_equal); TS(R("N2", 128, 256), R("D0"), -15.0, OP.is_equal)
     TT(R("P2", 0, 128), R("N2", 0, 128), R("I32"), OP.subtract); TT(R("P2", 0, 128), R("P2", 0, 128), R("N2", 128, 256), OP.subtract)
     TT(R("P2", 0, 128), R("P2", 0, 128), R("RM"), OP.mult); TT(R("SH"), R("P2", 0, 128), R("N2", 128, 256), OP.add)
-    for k in range(16):
-        TS(R("D16", 128 * k, 128 * k + 128), R("I32"), R("KH", k, k + 1), OP.mult)
+    MS(R("D16"), 1.0)
+
+    def masks(after):
+        for c in range(2):
+            x = R("D16", 1024 * c, 1024 * c + 1024)
+            op("g", lambda x=x, c=c: g.affine_select(x["ap"], x["ap"], [[-1024, 8], [16, 8], [1025, 16]], OP.is_equal, 0.0, -8192 * c, -1),
+               [x], [x], 170 + 2 * CYC * 1024, after=after)
     CP_(R("I16"), R("I32"))
     TT(R("THF"), R("TH8"), R("B", 0, 128, 16), OP.mult); RED(col(THC), R("THF"))
+    TS(col(THM), col(THC), 1024 - 255.0 / 256, OP.add, 65536.0, OP.mult)
     TS(col(THL), col(THC), -255.0 / 256, OP.add); TS(col(THC), col(THC), 1.0 / 1024, OP.add); TS(col(WC), col(THC), 256.0, OP.mult)
     for q in range(N):
         TS(R("DU", 4 * q, 4 * q + 4), R("IOF", 0, 4), 4.0 / 8192, OP.mult, (GW + q) / 8192.0, OP.add)
@@ -246,14 +273,20 @@ def rank_program(g, core, T, topo):
     if LOCAL:
         for c in (0, 2, 1, 3):
             h = helpers(core, T, topo)[c // 2]; rid, pid, _se = topo.addr(h)
-            msk = topo.mask(core, h) & ~topo.mask(core, T.cores[voter(0)]); x = R("Mi", 1024 * c, 1024 * c + 1024)
+            msk = quarter_mask(core, h, c, T, topo); x = R("Mi", 1024 * c, 1024 * c + 1024)
             j = op("g", lambda x=x, c=c, a=(pid, rid, msk): g.remote_dma(x["ap"], x["ap"], T.sem["h%d" % c], T.sem["sh%d" % c], *a),
                    [], [R("Mi")], 500, lat=5000, sem=("sh%d" % c, bin(msk).count("1")))
             ops[j]["own"] = True; copies.append(j)
+        for k, h in enumerate(near(core, r, T, topo) if 1 in LOCAL else []):
+            c = 2 * k + 1; rid, pid, _se = topo.addr(h); msk = quarter_mask(core, h, c, T, topo); x = R("Mi", 1024 * c, 1024 * c + 1024)
+            i = op("g", lambda x=x, c=c, k=k, a=(pid, rid, msk): g.remote_dma(x["ap"], x["ap"], T.sem["h%d" % c], T.sem["sn%d" % k], *a),
+                   [], [R("Mi")], 500, lat=5000, sem=("sn%d" % k, bin(msk).count("1")), after=copies[:2])
+            ops[i]["own"] = True; copies.insert(2, i)
         for k, u in enumerate(LOCAL):
-            if COPY[u] != "Mi":
+            if COPY[u] != "Mi" and u != 1:
                 op(None, None, [R(COPY[u])], [], 0, lat=COPY_NS * (k + 1), sem=("c%d" % u, landed(u)), after=[j])
-    MS(R("Mf", W, GW), 0.0); MS(R("LV", 0, 64), 0.0)
+    TS(R("LO", 0, 64), R("ONE", 0, 64), 0.0, OP.mult)
+    MS(R("YX", 1024, SW // 4), 0.0); MS(R("WH"), WHOLE); MS(R("PT", 0, 256), 0.0); MS(R("Mf", W, GW), 0.0); MS(R("LV", 0, 64), 0.0)
     for c in range(8):
         ACT(R("Xs", 512 * c, 512 * c + 512), R("Xb", 512 * c, 512 * c + 512), AF.Identity, bias=HI)
         CP_(R("Mf", 512 * c, 512 * c + 512), R("Mi", 512 * c, 512 * c + 512))
@@ -268,32 +301,51 @@ def rank_program(g, core, T, topo):
     def ch(name, c, w=64):
         return R(name, w * c, w * c + w)
 
-    def follow(src, at, dst, lo, hi, by, bank):
-        n = hi - lo; pm = R(bank, 0, n)
+    def follow(t, src, at, dst, lo, hi, by, bank):
+        n = hi - lo; pm = R(bank, 0, n); top = dst == "OB" and M_BY == "s"
         if by == "s":
-            b = 16 * (lo - 64)
+            b = 0
             for x in range(lo, hi, 64):
                 y = min(x + 64, hi)
-                ACT(R("Gf", 16 * (x - 64), 16 * (y - 64)), IN("F", W, R(src, at + x, at + y)), AF.Identity, bias=-BIG - 2048)
+                ACT(R("Gf", 16 * (x - lo), 16 * (y - lo)), IN("F", W, R(src, at + x, at + y)), AF.Identity, bias=-BIG - 2048)
             part = lambda name, c0, c1, step=None: dict(R(name, c0, c1, step), ap=T[name][0:n, c0:c1:step or 1])
             for k4 in range(0, 16, 4):
                 MM([(part(bank, 128 + k, 256, 16), R("Gf", b + k, b + 16 * n, 16), R("I32", k, 128, 16), k == 0, k == 15) for k in range(k4, k4 + 4)])
-            CP_(part("T16", 0, 128), part(bank, 128, 256))
-            MM([(pm, part("T16", 0, 128), part("I16", 0, n), True, True)])
+            if T_BY == "v":
+                CP_(part("T16", 0, 128), part(bank, 128, 256))
+                MM([(pm, part("T16", 0, 128), part("I16", 0, n), True, True)])
+            else:
+                ACT(part("T32", 0, 128), part(bank, 128, 256), AF.Identity)
+                MM([(pm, part("T32", 0, 128), part("I32", 0, n), True, True)])
+        elif by == "w":
+            part = lambda name, c0, c1, step=None: dict(R(name, c0, c1, step), ap=T[name][0:n, c0:c1:step or 1])
+            for x in range(lo, hi, 64):
+                TS(R("G", 16 * (x - lo), 16 * (x - lo + 64)), IN("F", W, R(src, at + x, at + x + 64)), -BIG - 2048, OP.add)
+            MM([(part(bank, 256 + k, 384, 16), R("G", k, 16 * n, 16), R("I16", k, 128, 16), k == 0, k == 15) for k in range(16)])
+            CP_(part("T16", 0, 128), part(bank, 256, 384))
+            MM([(pm, part("T16", 0, 128), part("I16", 0, n), True, not top)] + [(R(bank, x, x + 64), R("I"), R("WH"), False, x + 64 == n) for x in range(0, n, 64)] * top)
         else:
             b = 16 * lo % 2048
             TS(R("G", b, b + 16 * n), IN("F", W, R(src, at + lo, at + hi)), -BIG - 2048, OP.add)
-            MM([(pm, ch("D16", k, 128), R("G", b + k, b + 16 * n, 16), k == 0, k == 15) for k in range(16)])
-        TS(R(dst, lo, hi), pm, 2048.0, OP.add)
+            MM([(pm, ch("D16", k, 128), R("G", b + k, b + 16 * n, 16), k == 0, k == 15 and not top) for k in range(16)]
+               + [(pm, R("I"), R("WH", 0, n), False, True)] * top)
+        TS(R(dst, lo, hi), pm, 2048.0 - WHOLE * top, OP.add)
         if dst == "OB":
-            TS(R("M2", lo, hi), pm, WHOLE + 2048, OP.add, -WHOLE, OP.add)
-            if hi % 64 == 0:
-                steps(hi // 64 - 1, bank)
+            if top:
+                ACT(R("M2", lo, hi), pm, AF.Identity, bias=2048.0 - WHOLE)
+            else:
+                TS(R("M2", lo, hi), pm, WHOLE + 2048, OP.add, -WHOLE, OP.add)
+            for x in range(lo + 64, hi + 1, 64):
+                steps(t, x // 64 - 1, bank)
 
-    def steps(c, bank):
-        pn = R(bank, 64, 128)
+    def parts(t):
+        return [(0, 64 * SPLIT), (64 * SPLIT, 256)] if t in LOCAL and VSPLIT else [(0, 256)]
+
+    def steps(t, c, bank):
+        pn = R(bank, 128, 192)
         MM([(pn, R("SH"), ch("M2", c), True, True)])
-        TR(ch("PT", c), pn)
+        z = [x[1] for x in parts(t) if x[0] <= 64 * c < x[1]][0]
+        TR(R("PT", z + 64 * c, z + 64 * c + 64), pn)
 
     def score(t, c):
         b = 1024 * (c % 2); pd = "pd%d" % (c % 2)
@@ -309,47 +361,54 @@ def rank_program(g, core, T, topo):
         j = TT(R("EQ", b, b + 1024), IN("Mi" if t == 0 else "Mf", W, ch("OB", c)), ch("VR", c, 1024), OP.is_equal)
         if t == 0 and c == 3:
             ops[j]["after"] += copies
-        bank = "k0" if c < SPLIT else "k1"
-        key = ch(bank, c); own = range(SPLIT) if c < SPLIT else range(SPLIT, 4)
+        early = SPLIT if t else 4
+        bank = "k1" if c < early else "k0"
+        key = ch(bank, c); own = range(early) if c < early else range(early, 4)
         if c == own[0]:
             MM([(ch(bank, d), R("I"), R("KC"), d == c, False) for d in own])
-        for hf in range(2):
-            MM([(key, into("SA", k), R("AB", b + 64 * k, b + 64 * k + 64), False, False) for k in range(8 * hf, 8 * hf + 8)], True)
-            MM([(key, into("SE", k), R("EQ", b + k, b + 1024, 16), False, False) for k in range(8 * hf, 8 * hf + 8)], True)
-        MM([(key, R("NI"), ch("LP", c), False, c == own[-1]) if t else (key, R("I"), ch("PEN", c), False, c == own[-1])], c != own[-1])
+        MM([(key, R("NI"), ch("LP", c), False, False) if t else (key, R("I"), ch("PEN", c), False, False)], True)
+        sa = lambda k: (into("SA", k), R("AB", b + 64 * k, b + 64 * k + 64))
+        se = lambda k: (into("SE", k), R("EQ", b + k, b + 1024, 16))
+        for n, (f, hf) in enumerate(((se, 0), (se, 1), (sa, 0), (sa, 1)) if t else ((sa, 0), (sa, 1), (se, 0), (se, 1))):
+            end = n == 3 and c == own[-1]
+            MM([(key,) + f(k) + (False, end and k == 15) for k in range(8 * hf, 8 * hf + 8)], not end)
+        if c == own[-1]:
+            lo, hi = 64 * own[0], 64 * c + 64
+            kt = R("pa", 256 + lo, 256 + hi)
+            TR(kt, R(bank, lo, hi))
+            a, z = [x for x in parts(t) if x[0] <= lo < x[1]][0]
+            SCAN(R("P", a + lo, a + hi), R("RS", lo, hi), kt, -2.0e9, OP.add, OP.max)
+            TT(R("NR", lo, hi), kt, R("P", a + lo, a + hi), OP.is_lt)
+            SCAN(R("P", z + lo, z + hi), R("PT", z + lo, z + hi), R("NR", lo, hi), 0.0, OP.add, OP.mult)
 
     def choose(t, lo, hi):
         m0 = 32 * t + lo // 8; m1 = m0 + (hi - lo) // 16; m2 = m1 + (hi - lo) // 16
-        kt = R("pa", 256 + lo, 256 + hi)
-        TR(kt, R("k1" if hi == 256 else "k0", lo, hi))
-        SCAN(R("P", lo, hi), R("RS", lo, hi), kt, -2.0e9, OP.add, OP.max)
-        TT(R("NR", lo, hi), kt, R("P", lo, hi), OP.is_lt)
-        s0, s1 = lo // 16, hi // 16
-        fx = lambda at, x, k, a, z: [(R("pd0", at + s0 + h, at + s1, 2), ch("FX32", 2 * h + q, 128), R(x, lo + k + 16 * q, hi, 32), a and h + q == 0, z and h + q == 2)
-                                     for h in range(2) for q in range(2)]
-        MM(fx(512, "PT", 0, True, False))
-        MM(fx(0, "P", 15, True, t not in LOCAL))
+        hq = [(h, q) for h in range(2) for q in range(2)]
+        n = (hi - lo) // 16; s0 = lo // 16; at = 512 if lo else 0
+        MM([(R("pd0", at + h, at + 2 * n, 2), ch("FX32", 2 * h + q, 128), R("PT", 2 * lo + 16 * q, 2 * hi, 32), h + q == 0, False) for h, q in hq])
+        MM([(R("pd0", at + h, at + 2 * n, 2), ch("FX32", 2 * h + q, 128), R("P", 2 * lo + 15 + 16 * q, 2 * hi, 32), False, h + q == 2) for h, q in hq])
         if t in LOCAL:
-            MM([(dict(m[0], **R("pb", s0 + k // 2, s1, 2)),) + m[1:] for k, m in enumerate(fx(0, "P", 15, True, True))])
-            TS(R("s1", s0, s1), R("pb", s0, s1), -1.0e6, OP.is_lt, 8192.0, OP.mult)
-        SCAN(R("U", lo, hi), R("PT", lo, hi), R("NR", lo, hi), 0.0, OP.add, OP.mult)
-        if t not in LOCAL:
-            TS(R("O1", m1, m2), R("pd0", s0, s1), -1.0 / 256, OP.mult, col(WC), OP.add)
-        MM(fx(512, "U", 15, False, True))
-        CP_(R("O1", m0, m1), R("pd0", 512 + s0, 512 + s1))
+            MM([(R("k0" if hi == 256 else "k1", s0 + h, s0 + n, 2), ch("FX32", 2 * h + q, 128), R("P", 2 * lo + 15 + 16 * q, lo + hi, 32), h + q == 0, False)
+                for h, q in hq])
+        CP_(R("O1", m0, m1), R("pd0", at + n, at + 2 * n))
+        TS(R("s1", s0, s0 + n), R("pd0", at, at + n), -1.0e6, OP.is_lt, 8192.0, OP.mult)
+        TT(R("s3", s0, s0 + n), R("pd0", at + n, at + 2 * n), R("s1", s0, s0 + n), OP.add)
         if t in LOCAL:
             return
+        TS(R("O1", m1, m2), R("pd0", 0, 16), -1.0 / 256, OP.mult, col(WC), OP.add)
         dst = T.cores[voter(t)]; rid, pid, _se = topo.addr(dst); sem = ("a%d" if lo else "e%d") % t
         o1 = R("O1", m0, m2); l1 = R("L1", m0, m2)
         s = op("g", lambda: g.remote_dma(l1["ap"], o1["ap"], T.sem[sem], T.sem.sent, pid, rid, topo.mask(core, dst)), [], [o1], 500, sem="remote")
         nsent[0] += len(topo.engines(core, dst))
+        if t == 0:
+            masks([s])
         op(None, None, [l1], [], 0, lat=HOP1, sem=(sem, len(topo.engines(T.cores[voted(t)], core))), after=[s])
 
     def vote(t, lo, hi):
         m0 = 32 * t + lo // 8; m1 = m0 + (hi - lo) // 16; m2 = m1 + (hi - lo) // 16
         s0, s1 = lo // 16, hi // 16
         if t in LOCAL:
-            co = R("O1", m0, m1); sums = R("pd0", s0, s1)
+            co = R("O1", m0, m1); sums = R("k0" if hi == 256 else "k1", s0, s1)
             TT(R("E1", lo, hi), IN(COPY[t], W, co), R("VV", lo, hi), OP.is_equal)
             ACT(R("BC", lo, hi), IN("IO", W, co), AF.Identity, bias=UP)
             MM([(sums, into("SE", k), R("E1", lo + k, hi, 16), False, k == 15) for k in range(16)])
@@ -363,14 +422,23 @@ def rank_program(g, core, T, topo):
             MM([(R("k0", s0, s1), into("SE", k), R("E1", lo + k, hi, 16), k == 0, k == 15) for k in range(16)])
             TT(R("PS", s0 + 1, s1 + 1), R("k0", s0, s1), R("NF", s0, s1), OP.is_ge)
             TT(R("NP", s0, s1), R("k0", s0, s1), R("NF", s0, s1), OP.is_lt)
-        MM([(R("k1", s0, s1), R("NL"), R("PS", s0 + 1, s1 + 1), True, False), (R("k1", s0, s1), R("NU"), R("PS", s0, s1), False, True)])
+        pre = R("k1" if hi == 256 else "pa", 32 + s0, 32 + s1)
+        MM([(pre, R("NL"), R("PS", s0 + 1, s1 + 1), True, False), (pre, R("NU"), R("PS", s0, s1), False, True)])
         TT(R("QQ", s0, s1), R("NP", s0, s1), R("Q0", s0, s1), OP.mult)
-        SCAN(R("SN", s0, s1), R("k1", s0, s1), R("Z16", s0, s1), R("SN", s0 - 1, s0) if lo else 767.0, OP.add, OP.add)
+        SCAN(R("SN", s0, s1), pre, R("Z16", s0, s1), R("SN", s0 - 1, s0) if lo else 767.0, OP.add, OP.add)
         TT(R("SL", s0, s1), R("SN", s0, s1), R("QQ", s0, s1), OP.subtract)
         j = CP_(R("SO", s0, s1), R("SL", s0, s1))
         CP_(IN("CC", 768, R("SO", s0, s1)), R("BC", lo, hi))
         ACT(IN("CV", 768, R("SO", s0, s1)), R("VU", lo, hi), AF.Silu)
         return j
+
+    def ym(t):
+        if t == 0:
+            ACT(R("YM", 0, 1024, 4), R("M2"), AF.Identity)
+        else:
+            MM([(R("pd1", 512, 768), R("NI32"), R("M2"), True, False), (R("pd1", 512, 768), R("I"), R("LP"), False, True)])
+            TT(R("NR"), R("pd1", 512, 768), lanes("Mf", t), OP.min)
+            ACT(R("YM", t, 1024, 4), R("NR"), AF.Abs)
 
     def yx(t, src, less):
         ACT(R("X2"), lanes("Xb", t), AF.Identity, bias=256.0)
@@ -378,7 +446,6 @@ def rank_program(g, core, T, topo):
         TT(R("X2"), R("pb", 256, 512), R("X2"), OP.min)
         ACT(R("YX", t, 1024, 4), R("X2"), AF.Abs, bias=-256.0)
 
-    halves = [(0, 64 * SPLIT), (64 * SPLIT, 256)] if SPLIT else [(0, 256)]
     for t in range(RO):
         rho = owner(t)
         last = t == RO - 1
@@ -386,14 +453,14 @@ def rank_program(g, core, T, topo):
             for c in range(4):
                 CP_(ch("OB", c), lanes("Mi", 0, c, c + 1))
                 CP_(ch("M2", c), lanes("Mi", 0, c, c + 1))
-                steps(c, ("pa", "pb")[c % 2])
+                steps(t, c, ("pa", "pb")[c % 2])
         else:
             alike.append([len(ops)])
             for step, lo, hi, by, bank in FOLLOW:
                 if step == 1:
-                    follow("O0", 256 * t - 256, "OA", lo, hi, by, bank)
+                    follow(t, "O0", 256 * t - 256, "OA", lo, hi, by, bank)
                 else:
-                    follow("OA", 0, "OB", lo, hi, by, bank)
+                    follow(t, "OA", 0, "OB", lo, hi, by, bank)
             alike[-1] = list(range(alike[-1][0], len(ops)))
         if t in LOCAL:
             for u in range(1, t):
@@ -406,22 +473,24 @@ def rank_program(g, core, T, topo):
         j = len(ops)
         for c in range(4):
             score(t, c)
-            if c == SPLIT - 1:
-                choose(t, *halves[0])
         if t:
             alike[-1] += list(range(j, len(ops)))
-        choose(t, *halves[-1])
+        for lo, hi in parts(t):
+            choose(t, lo, hi)
         if t:
             yx(t - 1, lanes("Xs", t - 1), 0.0)
-        for lo, hi in halves:
-            s0, s1 = lo // 16, hi // 16
-            if t not in LOCAL:
-                TS(R("s1", s0, s1), R("O1", 32 * t + s0 + s1, 32 * t + 2 * s1), 12000.0, OP.is_ge, 8192.0, OP.mult)
-            CP_(R("s3", s0, s1), R("O1", 32 * t + 2 * s0, 32 * t + s0 + s1))
-        TT(R("s3"), R("s3"), R("s1"), OP.add); TT(R("s3"), R("s3"), R("DC"), OP.min)
+        elif VSPLIT:
+            IOTA(R("PT", 128 * SPLIT, 256 + 64 * SPLIT), [[0, 256 - 64 * SPLIT]], 0)
+        TT(R("s3"), R("s3"), R("DC"), OP.min)
         smo = CP_(R("SMO"), R("s3"))
-        for lo, hi in halves:
-            ops[vote(t, lo, hi)]["after"].append(smo)
+        if last:
+            ym(t)
+            out = DMA("y", T.ym[:], T.YM[:], [], [R("YM")], "oym", 4000)
+        for lo, hi in parts(t):
+            j = vote(t, lo, hi)
+        ops[j]["after"].append(smo)
+        if last:
+            ops[j]["after"].append(out)
         for hf, nm in enumerate(("CC", "CV")):
             TT(ch("MK", hf), R(nm, 704, 768), ch("KH", 0), OP.mult)
             SCAN(ch("SC", hf), ch("RM", 0), ch("MK", hf), 0.0, OP.mult, OP.add)
@@ -450,23 +519,24 @@ def rank_program(g, core, T, topo):
                        [], [R("OB"), lz(0, 0, 32)], 500, lat=3000, sem=("s" + slot, n))
                 ops[j]["own"] = True
                 op(None, None, [R(slot)], [], 0, lat=4000, sem=(slot, len(topo.engines(T.cores[voter(u)], core))), after=[j])
+        if t == 0 and 1 in LOCAL:
+            sig0 = [RemoteDMATransfer(dst_ids=[DstId(rid=topo.addr(h)[0], pnc=topo.addr(h)[1])], dma_engine_mask=1 << topo.engines(core, h)[-1 - k],
+                                      remote_sem=T.sem.go) for k, h in enumerate(near(core, r, T, topo))]
+            j = op("g", lambda: g.remote_dma_fused(sig0, local_sem=T.sem.sent), [], [lz(0, 0, 32)], 500, sem="remote")
+            nsent[0] += len(sig0)
+            op(None, None, [R(COPY[1])], [], 0, lat=COPY_NS * 0.9, sem=("c1", landed(1)), after=[j])
         if t == 1 and COPY.get(RO - 1) == "Mi":
             ops[s]["wait"] = [o["id"] for o in ops if o["eng"] is not None and any(x[0] == "Mi" for x in o["rd"])]
             sig = [RemoteDMATransfer(dst_ids=[DstId(rid=topo.addr(h)[0], pnc=topo.addr(h)[1])], dma_engine_mask=1 << topo.engines(core, h)[-1 - k],
                                      remote_sem=T.sem.go) for k, h in enumerate(helpers(core, T, topo))]
             j = op("g", lambda: g.remote_dma_fused(sig, local_sem=T.sem.sent), [], [lz(0, 0, 32)], 500, sem="remote")
             nsent[0] += len(sig)
-            op(None, None, [R("Mi")], [], 0, lat=COPY_NS, sem=("c%d" % (RO - 1), landed(RO - 1)), after=[j])
+            op(None, None, [R("Mi")], [], 0, lat=2 * COPY_NS, sem=("c%d" % (RO - 1), landed(RO - 1)), after=[j])
         ACT(R("XC"), IN("Xs", W + 256, R("SMO")), AF.Identity, bias=-0.5)
         MM([(R("pd1", 0, 256), R("I32"), XA, True, False)]); MM([(R("pd1", 0, 256), R("I32"), R("XC"), False, True)])
         ACT(R("SY"), R("pd1", 0, 256), AF.Identity, bias=WHOLE, scale=0.5)
-        if t == 0:
-            ACT(R("YM", 0, 1024, 4), R("M2"), AF.Identity)
-        else:
-            MM([(R("pd1", 512, 768), R("NI32"), R("M2"), True, False), (R("pd1", 512, 768), R("I"), R("LP"), False, True)])
-            TT(R("NR"), R("pd1", 512, 768), lanes("Mf", t), OP.min)
-            ACT(R("YM", t, 1024, 4), R("NR"), AF.Abs)
         if not last:
+            ym(t)
             if t:
                 ACT(lanes("Mf", t), R("M2"), AF.Identity)
             ACT(lanes("Xs", t), R("SY"), AF.Identity, bias=-WHOLE)
@@ -477,7 +547,6 @@ def rank_program(g, core, T, topo):
             vrep(t + 1, [s])
         else:
             yx(t, R("SY"), WHOLE)
-            DMA("y", T.ym[:], T.YM[:], [], [R("YM")], "oym", 4000)
         add = 0.0 if last else BIG
         val = "BV" if last else "MV"
         for q in range(N - 1, -1, -1):
@@ -493,10 +562,11 @@ def rank_program(g, core, T, topo):
             ACT(ch("BC", q), IN("IO", GW, lz(q, 0, 4)), AF.Identity, bias=add)
         for q in range(1, N):
             TT(ch("LO", q), IN("F", GW, lz(q, 0, 4)), ch(val, q), OP.not_equal)
-        for bank in ("pb", "pa"):
+        for bank in ("pb", "pa")[:1 if last else 2]:
             MM([(R(bank, 4 * q, 4 * q + 4), R("I32"), R("VF", 8 * q + 4, 8 * q + 8), q == 0, bank == "pb" and q == N - 1) for q in range(N)])
         TS(R("VL"), R("pb", 0, 16), 8192.0, OP.mult)
-        MM([(R("pa", 4, 16), ch("D16", k, 128), R("LO", 64 + k, 256, 16), False, k == 15) for k in range(16)])
+        if not last:
+            MM([(R("pa", 4, 16), ch("D16", k, 128), R("LO", 64 + k, 256, 16), False, k == 15) for k in range(16)])
         vval = "BC" if last else "MC"; diff = R("k0", 64, 256)
         MM([(diff, R("NI32"), R(vval, 64, 256), True, False)])
         if last:
@@ -505,8 +575,8 @@ def rank_program(g, core, T, topo):
             MM([(diff, R("I32"), R("BV", 64, 256), False, True)])
         TT(R("LV", 64, 256), diff, R("LO", 64, 256), OP.mult)
         TT(IN("F", GW, R("VL")), R("LV"), R(vval), OP.add)
-        TT(R("VM"), R("pa", 0, 16), R("DU"), OP.min)
         if not last:
+            TT(R("VM"), R("pa", 0, 16), R("DU"), OP.min)
             TS(R("VO"), R("VM"), 8192.0, OP.mult)
             for q in range(N - 1, -1, -1):
                 ACT(IN("Xs", GW, lz(q, 0, 4)), ch("BV", q), AF.Silu)
@@ -515,23 +585,31 @@ def rank_program(g, core, T, topo):
             ACT(IN("Xs", SW, R("VO")), R("BC"), AF.Silu)
             ACT(R("CN"), R("VM"), AF.Sign, bias=(W - 0.5) / 8192, scale=-1.0, acc=col(AF_))
             MM([(R("pb", 0, 1), R("ONE32"), col(AF_), True, True)])
-            TS(R("AI", 0, 1), R("pb", 0, 1), 0.5, OP.mult, 1024.0, OP.add); TS(R("AI", 1, 2), R("AI", 0, 1), 3, OP.bitwise_and)
-            if t + 1 in LOCAL:
-                TS(col(WC), R("AI", 1, 2), col(THL), OP.add, 65536.0, OP.mult)
+            if t + 1 in LOCAL and A_BY == "s":
+                ACT(col(A1), R("pb", 0, 1), AF.Identity, bias=255.625, scale=0.125); ACT(col(A2), R("pb", 0, 1), AF.Identity, bias=col(THM), scale=32768.0)
+                ACT(col(A1), col(A1), AF.Identity, bias=WHOLE); ACT(col(A1), col(A1), AF.Identity, bias=-WHOLE)
+                ACT(col(WC), col(A1), AF.Identity, bias=col(A2), scale=-262144.0)
             else:
-                TS(col(WC), R("AI", 1, 2), col(THC), OP.add, 256.0, OP.mult)
+                TS(R("AI", 0, 1), R("pb", 0, 1), 0.5, OP.mult, 1024.0, OP.add); TS(R("AI", 1, 2), R("AI", 0, 1), 3, OP.bitwise_and)
+                if t + 1 in LOCAL:
+                    TS(col(WC), R("AI", 1, 2), col(THL), OP.add, 65536.0, OP.mult)
+                else:
+                    TS(col(WC), R("AI", 1, 2), col(THC), OP.add, 256.0, OP.mult)
         else:
             TS(R("s4"), lz(r, 4, 8), float(W - 1), OP.min)
-            ACT(R("XO"), IN("Xb", W, R("s4")), AF.Identity)
-            TS(R("UO"), R("VM", 4 * r, 4 * r + 4), 2048.0, OP.mult, 0.1 - r / 4.0, OP.add)
-            CP_(IN("YX", SW // 4, R("UO")), R("XO"))
+            ACT(R("XO", 0, 64), IN("Xb", W, R("s4")), AF.Identity)
+            TS(R("UO"), lz(r, 4, 8), 0.25, OP.mult, 0.1 - r / 4.0, OP.add)
+            ACT(R("XO", 64, 128), IN("YX", SW // 4, R("UO")), AF.Identity)
+            TT(R("XO", 64, 128), R("XO", 64, 128), R("XO", 0, 64), OP.subtract)
+            TT(R("XO", 64, 128), R("XO", 64, 128), R("LO", 64 * r, 256 if r == 0 else 64 * r + 64) if r else dict(R("LO"), ap=T.LO[:, 0:64], n=64), OP.mult)
+            TT(IN("YX", SW // 4, R("UO")), R("XO", 64, 128), R("XO", 0, 64), OP.add)
             DMA("y", T.yp[:], T.F[0:128:16, 0:W], [], [R("F", 0, W)], "oyp", 2800)
             DMA("s", T.yx[:], T.YX[:, 0:1024], [], [R("YX", 0, 1024)], "oyx", 3400)
 
-    emit(g, T, Q, ops, nsent[0], marks, alike)
+    return Q, ops, nsent[0], marks, alike
 
 
-def emit(g, T, Q, ops, nsent, marks, alike):
+def emit(g, T, Q, ops, nsent, marks, alike, timed):
     def meet(a, b, banks):
         for (n, lo, hi) in a:
             for (m, l2, h2) in b:
@@ -571,8 +649,8 @@ def emit(g, T, Q, ops, nsent, marks, alike):
         for j in o["dep"]:
             succ[j].append(o["id"])
 
-    def gap(j, o):
-        return ops[j]["lat"] + LAT if o["dep"][j] or o["eng"] is None else 0.0
+    def gap(j, o, m=0):
+        return timed[m][j]["lat"] + COSTS[m][2] if o["dep"][j] or o["eng"] is None else 0.0
     anc = [0] * n; gp = []; nxt = [[] for _ in range(n)]
     for o in ops:
         far = 0
@@ -626,8 +704,15 @@ def emit(g, T, Q, ops, nsent, marks, alike):
         return sorted(range(n), key=lambda i: (kk[i], i))
     cost = [o["cost"] for o in ops]; tail = [o["cost"] + o["lat"] for o in ops]; eng = [o["eng"] for o in ops]
 
+    models = [([[(j, timed[m][j]["cost"] + gap(j, o, m)) for j, w in gp[o["id"]]] for o in ops], [o["cost"] for o in timed[m]],
+               [o["cost"] + o["lat"] for o in timed[m]]) for m in range(len(timed))]
+
     def run(seq, base=None, last=None):
-        st, prev = ([0.0] * n, {}) if base is None else (list(base[0]), dict(base[1]))
+        res = [once(seq, base and base[m], last, *models[m]) for m in range(len(models))]
+        return sum(x[0] for x in res) / len(res), res[0][1], res
+
+    def once(seq, base, last, gp, cost, tail):
+        st, prev = ([0.0] * n, {}) if base is None else (list(base[1]), dict(base[4]))
         by = {}
         for i in seq:
             t0 = 0.0; b = -1
@@ -647,7 +732,7 @@ def emit(g, T, Q, ops, nsent, marks, alike):
     def better(seq, tries, slack, base=None, last=None):
         now = run(seq, base, last); best = (now, seq); m = len(seq)
         for it in range(tries):
-            span, st, by, z = now[:4]
+            span = now[0]; by, z = now[2][it % len(models)][2:4]
             pairs = []
             while z in by:
                 b = by[z]
@@ -698,8 +783,8 @@ def emit(g, T, Q, ops, nsent, marks, alike):
             for k in range(len(marks)):
                 a = seq.index(marks[k - 1]) + 1 if k else 0; z = seq.index(marks[k]) + 1
                 head = run(seq[:a]) if a else None
-                mid = better(seq[a:z], TRIES // 8, SLACK / (1 + 2 * turn), head and (head[1], head[4]), marks[k])
-                seq = tight(seq[:a] + mid + seq[z:])
+                mid = better(seq[a:z], TRIES // 8, SLACK / (1 + 2 * turn), head and head[2], marks[k])
+                seq = min(tight(seq[:a] + mid + seq[z:]), seq[:a] + mid + seq[z:], key=lambda x: run(x)[0])
             st = run(seq)[1]
             b = min(alike, key=lambda x: st[x[-1]] - st[x[0]])
             for x in alike:

from concourse.bass import DstId, RemoteDMATransfer
from concourse.mybir import AluOpType as OP, AxisListType, ActivationFunctionType as AF

W, RO, BIG, GW, SW = 4096, 4, 65536.0, 4624, 4880
HI, UP = 8192.0, 32.0
WHOLE = 12582912.0
F32, BF, F16, I32, U16 = "float32", "bfloat16", "float16", "int32", "uint16"
FOLLOW = [(1, 0, 64, "v", "pa"), (1, 64, 128, "v", "pb"), (2, 0, 64, "v", "pa"), (1, 128, 256, "s", "k0"),
          (2, 64, 128, "v", "pb"), (2, 128, 192, "v", "pa"), (2, 192, 256, "v", "pb")]
WAIT_W = True
SPLIT = 3
VSPLIT = False
T_BY, A_BY, M_BY = "s", "s", "s"
LOCAL = (1, 2, 3)
COPY = {1: "T1", 2: "T2", 3: "Mi"}
COPY_NS = 25000.0
LOAD = (5000.0, 1900.0)
TRIES, SLACK = 190000, 2500.0
PLAN = {}


def _sb(n, d):
    return ("sbuf", [128, n], d)


SCRATCH = {
    "Mi": _sb(W, I32), "Xb": _sb(W, BF), "Mf": _sb(GW, F32), "F": _sb(GW, F32), "Xs": _sb(SW, F32), "IO": _sb(GW, F32),
    "VR": _sb(W, I32), "G": _sb(2048, F16), "Gf": _sb(2048, F32), "EQ": _sb(2048, BF), "XG": _sb(2048, BF), "AB": _sb(2048, BF),
    "D16": _sb(2048, BF), "T16": _sb(128, F16), "T32": _sb(128, F32), "I16": _sb(128, F16), "SE": _sb(144, BF), "SA": _sb(144, BF), "YX": _sb(SW // 4, BF), "YM": _sb(1024, F32),
    "s4": _sb(4, U16), "UO": _sb(4, U16), "XO": _sb(128, BF),
    "FX32": _sb(512, F32), "I": _sb(128, BF), "NI": _sb(128, BF), "NL": _sb(128, BF), "NU": _sb(128, BF),
    "ONE": _sb(128, BF), "I32": _sb(128, F32), "NI32": _sb(128, F32), "ONE32": _sb(128, F32), "SH": _sb(128, F32), "IR": _sb(256, F32),
    "KH": _sb(128, F32), "KC": _sb(64, BF), "RS": _sb(256, F32), "RM": _sb(128, F32), "DM": _sb(256, F32),
    "pidx": _sb(8, I32), "col": _sb(16, F32), "IOF": _sb(16, F32), "Q0": _sb(16, F32), "C2": _sb(4, F32), "Z16": _sb(16, F32), "DC": _sb(16, F32),
    "TH1": _sb(8, I32), "TH8": _sb(8, I32), "THF": _sb(8, F32),
    "O0": _sb(768, U16), "OA": _sb(256, U16), "OB": _sb(256, U16), "M2": _sb(256, F32), "PEN": _sb(256, BF),
    "LP": _sb(256, BF), "PT": _sb(512, F32), "P": _sb(512, F32), "NR": _sb(256, F32), "U": _sb(128, F32),
    "O1": _sb(128, U16), "L1": _sb(128, U16), "LZ": _sb(128, U16),
    "VV": _sb(256, F32), "VU": _sb(256, F32), "E1": _sb(256, BF), "NF": _sb(16, F32), "PS": _sb(18, BF), "NP": _sb(16, F32), "QQ": _sb(16, F32),
    "SN": _sb(16, F32), "SL": _sb(16, F32), "SO": _sb(16, U16), "CC": _sb(768, F32), "CV": _sb(768, F32), "MK": _sb(128, F32),
    "SC": _sb(128, F32), "OF": _sb(8, F32), "N2": _sb(256, F32), "P2": _sb(256, F32),
    "BV": _sb(256, F32), "BC": _sb(256, F32), "MV": _sb(256, F32), "MC": _sb(256, F32), "VF": _sb(32, F32), "LO": _sb(256, F16),
    "VO": _sb(16, U16), "CN": _sb(16, F32), "AI": _sb(4, I32),
    "s1": _sb(16, F32), "s3": _sb(16, F32), "SMO": _sb(16, U16), "CL": _sb(256, I32), "XC": _sb(256, F32), "SY": _sb(256, F32),
    "X2": _sb(256, F32), "PB": _sb(256, F32), "DU": _sb(16, F32), "VM": _sb(16, F32), "WH": _sb(64, BF), "VL": _sb(16, U16), "LV": _sb(256, F32),
    "T1": _sb(W, I32), "T2": _sb(W, I32), "N12": _sb(256, U16), "N13": _sb(256, U16), "N23": _sb(256, U16),
    "pd0": ("psum", [128, 1024], F32), "pd1": ("psum", [128, 1024], F32), "pa": ("psum", [128, 512], F32),
    "pb": ("psum", [128, 512], F32), "k0": ("psum", [128, 512], F32), "k1": ("psum", [128, 512], F32),
}
ALIAS = {"D0": ("U", 128), "B": ("NR", 128), "J16": ("P", 256)}
SEMAPHORES = (["cv", "cs", "cp", "cg", "sent", "lth", "lx", "oym", "oyx", "oyp", "pi0", "pi1"] + ["lm%d" % i for i in range(4)]
              + ["go", "sn0", "sn1", "c1", "c2", "c3", "N12", "N13", "N23", "sN12", "sN13", "sN23"] + ["h%d" % i for i in range(4)] + ["sh%d" % i for i in range(4)]
              + ["a%d" % i for i in range(RO)] + ["e%d" % i for i in range(RO)] + ["b%d" % i for i in range(RO)])
COSTS = [(1.0, 0.5, 90.0, 1500.0, 1900.0, 50.0, 80.0, 1.56, 3.8), (0.83, 0.45, 120.0, 1200.0, 1600.0, 60.0, 110.0, 1.56, 3.8)]


def helpers(core, T, topo):
    return [h for h in topo.cores_of(core) if topo.die(h) != topo.die(core) and all(topo.may_write(h, x) for x in T.cores)][:2]


def near(core, q, T, topo):
    dst = T.cores[(q - 2) % len(T.cores)]
    return [h for h in topo.cores_of(core) if h != core and topo.die(h) == topo.die(core) and topo.may_write(h, dst)][:2]


def quarter_mask(core, helper, c, T, topo):
    other = [x for x in T.cores if x != core][0]
    return topo.mask(core, helper) & ~(topo.mask(core, other) if c % 2 else 0)


def helper_program(g, core, T, topo):
    N = len(T.cores)
    for q, own in enumerate(T.cores):
        if LOCAL and core in helpers(own, T, topo):
            half = helpers(own, T, topo).index(core); sent = 0
            for t in LOCAL:
                dst = T.cores[(q - 1 - t % (N - 1)) % N]; rid, pid, _se = topo.addr(dst)
                if COPY[t] == "Mi":
                    g.wait_ge(T.sem.go, 1)
                for c in (2 * half, 2 * half + 1)[:1 if t == 1 else 2]:
                    g.wait_ge(T.sem["h%d" % c], bin(quarter_mask(own, core, c, T, topo)).count("1"))
                    g.remote_dma(T[COPY[t]][:, 1024 * c:1024 * c + 1024], T.Mi[:, 1024 * c:1024 * c + 1024], T.sem["c%d" % t], T.sem.sent,
                                 pid, rid, topo.mask(core, dst))
                    sent += len(topo.engines(core, dst))
            g.wait_ge(T.sem.sent, sent)
        if 1 in LOCAL and core in near(own, q, T, topo):
            c = 2 * near(own, q, T, topo).index(core) + 1; dst = T.cores[(q - 2) % N]; rid, pid, _se = topo.addr(dst)
            g.wait_ge(T.sem["h%d" % c], bin(quarter_mask(own, core, c, T, topo)).count("1")); g.wait_ge(T.sem.go, 1)
            g.remote_dma(T[COPY[1]][:, 1024 * c:1024 * c + 1024], T.Mi[:, 1024 * c:1024 * c + 1024], T.sem.c1, T.sem.sent, pid, rid, topo.mask(core, dst))
            g.wait_ge(T.sem.sent, len(topo.engines(core, dst)))


def rank_program(g, core, T, topo):
    r = T.rank_of(core)
    if r is None:
        return helper_program(g, core, T, topo)
    plans = [calls(g, core, T, topo, r, costs) for costs in COSTS]
    emit(g, T, *plans[0], [p[1] for p in plans])


def calls(g, core, T, topo, r, costs):
    CYC, PEC, LAT, HOP1, HOP2, VFIX, SFIX, GATH, SCAT = costs
    N = len(T.cores)
    ops = []
    Q = {"v": g.vector, "s": g.scalar, "p": g.tensor, "g": g, "y": g.sync}
    size = {F32: 4, I32: 4, BF: 2, F16: 2, U16: 2}

    def R(name, lo=0, hi=None, step=None):
        if name in ALIAS:
            name, full = ALIAS[name]
            hi = full if hi is None else hi
        if hi is None:
            hi = SCRATCH[name][1][1]
        ap = T[name][:, lo:hi] if step is None else T[name][:, lo:hi:step]
        n = hi - lo if step is None else (hi - lo + step - 1) // step
        return {"ap": ap, "use": [(name, lo, hi)], "n": n, "ind": False, "name": name}

    def IN(name, hi, off):
        return {"ap": T[name][:, 0:hi].indirect(off["ap"]), "use": [(name, 0, hi)], "off": off["use"], "n": 16 * off["n"], "ind": True, "name": name}

    def psum(x):
        return SCRATCH[x["name"]][0] == "psum"

    def op(eng, fn, outs, ins, cost, lat=0.0, sem=None, after=()):
        wr, rd = [], []
        for x in outs:
            wr += x["use"]; rd += x.get("off", [])
        for x in ins:
            if isinstance(x, dict):
                rd += x["use"] + x.get("off", [])
        ops.append({"eng": eng, "fn": fn, "wr": wr, "rd": rd, "cost": cost, "lat": lat, "sem": sem, "after": list(after), "id": len(ops)})
        return len(ops) - 1

    def vcost(o, ins, two=False):
        if o["ind"]:
            return 50 + SCAT * CYC * o["n"]
        if ins[0]["ind"]:
            return 50 + GATH * CYC * o["n"]
        f = 0.5 if all(size[SCRATCH[x["name"]][2]] == 2 for x in [o] + ins) else 1.0
        if two and not any(psum(x) for x in ins):
            f *= 2
        return VFIX + CYC * max(64, f * o["n"])

    def ap(x):
        return x["ap"] if isinstance(x, dict) else x

    def CP_(o, a):
        return op("v", lambda: g.vector.tensor_copy(o["ap"], a["ap"]), [o], [a], vcost(o, [a]))

    def TT(o, a, b, f):
        return op("v", lambda: g.vector.tensor_tensor(o["ap"], a["ap"], b["ap"], f), [o], [a, b], vcost(o, [a, b], True))

    def TS(o, a, s1, f1, s2=None, f2=None):
        if f2 is None:
            return op("v", lambda: g.vector.tensor_scalar(o["ap"], a["ap"], ap(s1), None, f1), [o], [a, s1], vcost(o, [a]))
        return op("v", lambda: g.vector.tensor_scalar(o["ap"], a["ap"], ap(s1), ap(s2), f1, f2), [o], [a, s1, s2], vcost(o, [a]))

    def SCAN(o, a, b, init, f0, f1):
        return op("v", lambda: g.vector.tensor_tensor_scan(o["ap"], a["ap"], b["ap"], ap(init), f0, f1), [o], [a, b, init], vcost(o, [a, b]))

    def TR(o, a):
        return op("v", lambda: g.vector.transpose(o["ap"], a["ap"]), [o], [a], vcost(o, [a]))

    def MS(o, val):
        return op("v", lambda: g.vector.memset(o["ap"], val), [o], [], VFIX + CYC * max(64, o["n"] * size[SCRATCH[o["name"]][2]] / 4))

    def RED(o, a):
        return op("v", lambda: g.vector.tensor_reduce(o["ap"], a["ap"], AxisListType.X, OP.add), [o], [a], 100)

    def ACT(o, a, f, bias=0.0, scale=1.0, acc=None):
        c = 65 + GATH * CYC * o["n"] if a["ind"] else SFIX + CYC * max(64, o["n"])
        if o["ind"]:
            return op("s", lambda: g.scalar.activation(o["ap"], a["ap"], f), [o], [a], 65 + SCAT * CYC * o["n"])
        if acc is not None:
            return op("s", lambda: g.scalar.activation(o["ap"], a["ap"], f, bias=bias, scale=scale, accum_out=acc["ap"]), [o, acc], [a], c + 20)
        return op("s", lambda: g.scalar.activation(o["ap"], a["ap"], f, bias=ap(bias), scale=ap(scale)), [o], [a, bias, scale], c)

    def MM(lst, free=False):
        def fn():
            for (o, l, x, s0, s1) in lst:
                h = g.tensor.matmul(o["ap"], l["ap"], x["ap"], s0, s1)
            return h
        c = sum(PEC * max(64, x["n"]) * (4 if SCRATCH[x["name"]][2] == F32 else 1) for (o, l, x, s0, s1) in lst)
        j = op("p", fn, [m[0] for m in lst], [m[1] for m in lst] + [m[2] for m in lst], c + 40, lat=60)
        ops[j]["free"] = free
        return j

    def IOTA(o, pat, base, cm=0):
        if SCRATCH[o["name"]][2] == I32:
            return op("g", lambda: g.iota(o["ap"], pat, base, cm), [o], [], 130 + 2 * CYC * o["n"])
        return op("g", lambda: g.iota(o["ap"], pat, base, cm, allow_small_or_imprecise_dtypes=True), [o], [], 130 + 2 * CYC * o["n"])

    def DMA(q, out, in_, outs, ins, sem, lat):
        return op(q, lambda: Q[q].dma_start(out, in_), outs, ins, 60, lat=lat, sem=(sem, 16))

    def col(i):
        return R("col", i, i + 1)

    PM, PG, H0, H1, K15, THC, WC, AF_, THL, THM, A1, A2 = range(12)
    lanes = lambda name, t, c0=0, c1=4: R(name, 1024 * c0 + 4 * t + r, 1024 * c1, 16)
    voted = lambda t: (r - 1 - t % (N - 1)) % N
    voter = lambda t: (r + 1 + t % (N - 1)) % N
    owner = lambda t: r if t in LOCAL else voted(t)
    landed = lambda t: sum(2 * len(topo.engines(h, core)) for h in helpers(T.cores[voter(t)], T, topo))

    j = DMA("y", T.Xb[:], T.xv[:], [R("Xb")], [], "lx", LOAD[0])
    for c in range(4):
        k = DMA("y", T.Mi[:, 1024 * c:1024 * c + 1024], T.mt[:, 1024 * c:1024 * c + 1024], [R("Mi", 1024 * c, 1024 * c + 1024)], [], "lm%d" % c, LOAD[0] + LOAD[1] * (c + 1))
        ops[k]["after"].append(j); j = k
    IOTA(R("D0"), [[1, 128]], 0, -1)
    IOTA(R("B"), [[1, 8], [0, 16]], 0)
    IOTA(R("pidx", 0, 1), [[0, 1]], 0, 1)
    IOTA(R("J16"), [[0, 16], [1, 16]], 0)
    IOTA(R("IR"), [[1, 256]], 0)
    op("g", lambda: g.dma_start(T.TH1[0:1, 0:8], T.th[:], allow_slow_non_contiguous=True), [R("TH1")], [], 1000, lat=3000, sem=("lth", 16))

    void = W + 260 + r

    def vrep(t, after=()):
        js = [IOTA(R("VR", 1024 * c, 1024 * c + 1024), [[16, 64], [0, 16]], 1024 * c + 4 * t + r) for c in range(4)]
        js.append(IOTA(R("VV"), [[16, 256]], 4 * t + owner(t)))
        js.append(IOTA(R("VU"), [[16, 256]], 4 * t + owner(t) + int(UP)))
        js += [IOTA(R(nm, 704, 768), [[4, 64]], void + int(UP)) for nm in ("CC", "CV")]
        for j in js:
            ops[j]["after"] += list(after)
    IOTA(R("IO", 0, GW // 8), [[1, GW // 8]], 0)
    vrep(0, [o["id"] for o in ops if o["eng"] == "g"])
    op("g", lambda: g.partition_broadcast(T.TH8[:], T.TH1[0:1, 0:8], 128), [R("TH8")], [R("TH1")], 200)
    for c in range(8):
        ACT(R("F", GW // 8 * c, GW // 8 * (c + 1)), R("IO", 0, GW // 8), AF.Identity, bias=BIG + GW // 8 * c)
        if c:
            ACT(R("IO", GW // 8 * c, GW // 8 * (c + 1)), R("IO", 0, GW // 8), AF.Identity, bias=float(GW // 8 * c))
    TS(R("pidx", 1, 2), R("pidx", 0, 1), 15, OP.bitwise_and); CP_(col(PM), R("pidx", 1, 2))
    TS(R("pidx", 2, 3), R("pidx", 0, 1), 4, OP.arith_shift_right); CP_(col(PG), R("pidx", 2, 3))
    TS(R("pidx", 3, 4), R("pidx", 0, 1), 16, OP.bitwise_and)
    TS(col(H0), R("pidx", 3, 4), 0.0, OP.is_equal); TS(col(H1), R("pidx", 3, 4), 16.0, OP.is_equal)
    TS(col(K15), col(PM), -1.0, OP.mult, 15.0, OP.add)
    TS(R("I"), R("D0"), 0.0, OP.is_equal); TS(R("NI"), R("D0"), 0.0, OP.is_equal, -1.0, OP.mult); TS(R("I32"), R("D0"), 0.0, OP.is_equal)
    TS(R("B"), R("B"), col(PG), OP.is_equal)
    MS(R("ONE"), 1.0); MS(R("SE"), 0.0); MS(R("SA"), 0.0); MS(R("Z16"), 0.0); MS(R("PS"), 0.0)
    TS(R("SE", 15, 143, 16), R("B", 0, 128, 16), 65536.0, OP.mult); TS(R("SA", 15, 143, 16), R("B", 0, 128, 16), -16.0, OP.mult)
    into = lambda name, k: R(name, 15 - k, 143 - k)
    TS(R("KC"), R("ONE", 0, 64), col(K15), OP.mult)
    TS(R("MK"), R("D0"), 0.0, OP.is_gt, -1.0, OP.mult); TT(R("NL"), R("MK"), R("B"), OP.mult)
    TS(R("SC"), R("D0"), 0.0, OP.is_le, -1.0, OP.mult); TT(R("NU"), R("SC"), R("B"), OP.mult)
    TS(R("KH"), R("J16", 0, 128), col(PM), OP.is_equal)
    TS(R("RS"), R("J16"), 0.0, OP.is_equal, -1.0e9, OP.mult); TS(R("RM"), R("J16", 0, 128), 0.0, OP.not_equal)
    TS(R("IOF"), R("IR", 0, 16), 16.0, OP.mult, col(PM), OP.add); TS(R("Q0"), R("IOF"), 256.0, OP.add)
    TS(R("C2"), R("IOF", 0, 4), 4.0, OP.mult, void + UP, OP.add); TS(R("DC"), R("IOF"), float(W), OP.add)
    for s in range(4):
        TS(R("DM", 64 * s, 64 * s + 64), R("IR", 0, 64), R("IOF", s, s + 1), OP.is_gt, R("C2", s, s + 1), OP.mult)
    for h in range(2):
        for q in range(2):
            TS(R("FX32", 256 * h + 128 * q, 256 * h + 128 * q + 128), R("D0"), 16.0 * (q - h), OP.is_equal, col(H0 + h), OP.mult)
    TS(R("NI32"), R("I32"), -1.0, OP.mult); MS(R("ONE32"), 1.0)
    TS(R("N2", 0, 128), R("D0"), 1.0, OP.is_equal); TS(R("N2", 128, 256), R("D0"), -15.0, OP.is_equal)
    TT(R("P2", 0, 128), R("N2", 0, 128), R("I32"), OP.subtract); TT(R("P2", 0, 128), R("P2", 0, 128), R("N2", 128, 256), OP.subtract)
    TT(R("P2", 0, 128), R("P2", 0, 128), R("RM"), OP.mult); TT(R("SH"), R("P2", 0, 128), R("N2", 128, 256), OP.add)
    MS(R("D16"), 1.0)

    def masks(after):
        for c in range(2):
            x = R("D16", 1024 * c, 1024 * c + 1024)
            op("g", lambda x=x, c=c: g.affine_select(x["ap"], x["ap"], [[-1024, 8], [16, 8], [1025, 16]], OP.is_equal, 0.0, -8192 * c, -1),
               [x], [x], 170 + 2 * CYC * 1024, after=after)
    CP_(R("I16"), R("I32"))
    TT(R("THF"), R("TH8"), R("B", 0, 128, 16), OP.mult); RED(col(THC), R("THF"))
    TS(col(THM), col(THC), 1024 - 255.0 / 256, OP.add, 65536.0, OP.mult)
    TS(col(THL), col(THC), -255.0 / 256, OP.add); TS(col(THC), col(THC), 1.0 / 1024, OP.add); TS(col(WC), col(THC), 256.0, OP.mult)
    for q in range(N):
        TS(R("DU", 4 * q, 4 * q + 4), R("IOF", 0, 4), 4.0 / 8192, OP.mult, (GW + q) / 8192.0, OP.add)
    copies = []
    if LOCAL:
        for c in (0, 2, 1, 3):
            h = helpers(core, T, topo)[c // 2]; rid, pid, _se = topo.addr(h)
            msk = quarter_mask(core, h, c, T, topo); x = R("Mi", 1024 * c, 1024 * c + 1024)
            j = op("g", lambda x=x, c=c, a=(pid, rid, msk): g.remote_dma(x["ap"], x["ap"], T.sem["h%d" % c], T.sem["sh%d" % c], *a),
                   [], [R("Mi")], 500, lat=5000, sem=("sh%d" % c, bin(msk).count("1")))
            ops[j]["own"] = True; copies.append(j)
        for k, h in enumerate(near(core, r, T, topo) if 1 in LOCAL else []):
            c = 2 * k + 1; rid, pid, _se = topo.addr(h); msk = quarter_mask(core, h, c, T, topo); x = R("Mi", 1024 * c, 1024 * c + 1024)
            i = op("g", lambda x=x, c=c, k=k, a=(pid, rid, msk): g.remote_dma(x["ap"], x["ap"], T.sem["h%d" % c], T.sem["sn%d" % k], *a),
                   [], [R("Mi")], 500, lat=5000, sem=("sn%d" % k, bin(msk).count("1")), after=copies[:2])
            ops[i]["own"] = True; copies.insert(2, i)
        for k, u in enumerate(LOCAL):
            if COPY[u] != "Mi" and u != 1:
                op(None, None, [R(COPY[u])], [], 0, lat=COPY_NS * (k + 1), sem=("c%d" % u, landed(u)), after=[j])
    TS(R("LO", 0, 64), R("ONE", 0, 64), 0.0, OP.mult)
    MS(R("YX", 1024, SW // 4), 0.0); MS(R("WH"), WHOLE); MS(R("PT", 0, 256), 0.0); MS(R("Mf", W, GW), 0.0); MS(R("LV", 0, 64), 0.0)
    for c in range(8):
        ACT(R("Xs", 512 * c, 512 * c + 512), R("Xb", 512 * c, 512 * c + 512), AF.Identity, bias=HI)
        CP_(R("Mf", 512 * c, 512 * c + 512), R("Mi", 512 * c, 512 * c + 512))
    for t in range(1, RO):
        CP_(R("O0", 256 * t - 256, 256 * t), lanes("Mi", t))
    XA = R("Xs", W, W + 256)
    ACT(XA, lanes("Xb", 0), AF.Identity, bias=HI)

    nsent = [0]
    marks = []; alike = []

    def ch(name, c, w=64):
        return R(name, w * c, w * c + w)

    def follow(t, src, at, dst, lo, hi, by, bank):
        n = hi - lo; pm = R(bank, 0, n); top = dst == "OB" and M_BY == "s"
        if by == "s":
            b = 0
            for x in range(lo, hi, 64):
                y = min(x + 64, hi)
                ACT(R("Gf", 16 * (x - lo), 16 * (y - lo)), IN("F", W, R(src, at + x, at + y)), AF.Identity, bias=-BIG - 2048)
            part = lambda name, c0, c1, step=None: dict(R(name, c0, c1, step), ap=T[name][0:n, c0:c1:step or 1])
            for k4 in range(0, 16, 4):
                MM([(part(bank, 128 + k, 256, 16), R("Gf", b + k, b + 16 * n, 16), R("I32", k, 128, 16), k == 0, k == 15) for k in range(k4, k4 + 4)])
            if T_BY == "v":
                CP_(part("T16", 0, 128), part(bank, 128, 256))
                MM([(pm, part("T16", 0, 128), part("I16", 0, n), True, True)])
            else:
                ACT(part("T32", 0, 128), part(bank, 128, 256), AF.Identity)
                MM([(pm, part("T32", 0, 128), part("I32", 0, n), True, True)])
        elif by == "w":
            part = lambda name, c0, c1, step=None: dict(R(name, c0, c1, step), ap=T[name][0:n, c0:c1:step or 1])
            for x in range(lo, hi, 64):
                TS(R("G", 16 * (x - lo), 16 * (x - lo + 64)), IN("F", W, R(src, at + x, at + x + 64)), -BIG - 2048, OP.add)
            MM([(part(bank, 256 + k, 384, 16), R("G", k, 16 * n, 16), R("I16", k, 128, 16), k == 0, k == 15) for k in range(16)])
            CP_(part("T16", 0, 128), part(bank, 256, 384))
            MM([(pm, part("T16", 0, 128), part("I16", 0, n), True, not top)] + [(R(bank, x, x + 64), R("I"), R("WH"), False, x + 64 == n) for x in range(0, n, 64)] * top)
        else:
            b = 16 * lo % 2048
            TS(R("G", b, b + 16 * n), IN("F", W, R(src, at + lo, at + hi)), -BIG - 2048, OP.add)
            MM([(pm, ch("D16", k, 128), R("G", b + k, b + 16 * n, 16), k == 0, k == 15 and not top) for k in range(16)]
               + [(pm, R("I"), R("WH", 0, n), False, True)] * top)
        TS(R(dst, lo, hi), pm, 2048.0 - WHOLE * top, OP.add)
        if dst == "OB":
            if top:
                ACT(R("M2", lo, hi), pm, AF.Identity, bias=2048.0 - WHOLE)
            else:
                TS(R("M2", lo, hi), pm, WHOLE + 2048, OP.add, -WHOLE, OP.add)
            for x in range(lo + 64, hi + 1, 64):
                steps(t, x // 64 - 1, bank)

    def parts(t):
        return [(0, 64 * SPLIT), (64 * SPLIT, 256)] if t in LOCAL and VSPLIT else [(0, 256)]

    def steps(t, c, bank):
        pn = R(bank, 128, 192)
        MM([(pn, R("SH"), ch("M2", c), True, True)])
        z = [x[1] for x in parts(t) if x[0] <= 64 * c < x[1]][0]
        TR(R("PT", z + 64 * c, z + 64 * c + 64), pn)

    def score(t, c):
        b = 1024 * (c % 2); pd = "pd%d" % (c % 2)
        if t == 0:
            TS(ch("CL", c), lanes("Mi", 0, c, c + 1), 12, OP.bitwise_and)
            TS(ch("PEN", c), ch("CL", c), 0.0, OP.is_equal, -8388608.0, OP.mult)
        ACT(R("XG", b, b + 1024), IN("Xs" if t else "Xb", W, ch("OB", c)), AF.Identity, bias=-HI if t else 0.0)
        for hf in range(2):
            ks = range(8 * hf, 8 * hf + 8)
            MM([(ch(pd, k), R("NI"), lanes("Xb", t, c, c + 1), k == ks[0], False) for k in ks])
            MM([(ch(pd, k), R("I"), R("XG", b + k, b + 1024, 16), False, k == ks[-1]) for k in ks])
            ACT(R("AB", b + 512 * hf, b + 512 * hf + 512), ch(pd, hf, 512), AF.Abs)
        j = TT(R("EQ", b, b + 1024), IN("Mi" if t == 0 else "Mf", W, ch("OB", c)), ch("VR", c, 1024), OP.is_equal)
        if t == 0 and c == 3:
            ops[j]["after"] += copies
        early = SPLIT if t else 4
        bank = "k1" if c < early else "k0"
        key = ch(bank, c); own = range(early) if c < early else range(early, 4)
        if c == own[0]:
            MM([(ch(bank, d), R("I"), R("KC"), d == c, False) for d in own])
        MM([(key, R("NI"), ch("LP", c), False, False) if t else (key, R("I"), ch("PEN", c), False, False)], True)
        sa = lambda k: (into("SA", k), R("AB", b + 64 * k, b + 64 * k + 64))
        se = lambda k: (into("SE", k), R("EQ", b + k, b + 1024, 16))
        for n, (f, hf) in enumerate(((se, 0), (se, 1), (sa, 0), (sa, 1)) if t else ((sa, 0), (sa, 1), (se, 0), (se, 1))):
            end = n == 3 and c == own[-1]
            MM([(key,) + f(k) + (False, end and k == 15) for k in range(8 * hf, 8 * hf + 8)], not end)
        if c == own[-1]:
            lo, hi = 64 * own[0], 64 * c + 64
            kt = R("pa", 256 + lo, 256 + hi)
            TR(kt, R(bank, lo, hi))
            a, z = [x for x in parts(t) if x[0] <= lo < x[1]][0]
            SCAN(R("P", a + lo, a + hi), R("RS", lo, hi), kt, -2.0e9, OP.add, OP.max)
            TT(R("NR", lo, hi), kt, R("P", a + lo, a + hi), OP.is_lt)
            SCAN(R("P", z + lo, z + hi), R("PT", z + lo, z + hi), R("NR", lo, hi), 0.0, OP.add, OP.mult)

    def choose(t, lo, hi):
        m0 = 32 * t + lo // 8; m1 = m0 + (hi - lo) // 16; m2 = m1 + (hi - lo) // 16
        hq = [(h, q) for h in range(2) for q in range(2)]
        n = (hi - lo) // 16; s0 = lo // 16; at = 512 if lo else 0
        MM([(R("pd0", at + h, at + 2 * n, 2), ch("FX32", 2 * h + q, 128), R("PT", 2 * lo + 16 * q, 2 * hi, 32), h + q == 0, False) for h, q in hq])
        MM([(R("pd0", at + h, at + 2 * n, 2), ch("FX32", 2 * h + q, 128), R("P", 2 * lo + 15 + 16 * q, 2 * hi, 32), False, h + q == 2) for h, q in hq])
        if t in LOCAL:
            MM([(R("k0" if hi == 256 else "k1", s0 + h, s0 + n, 2), ch("FX32", 2 * h + q, 128), R("P", 2 * lo + 15 + 16 * q, lo + hi, 32), h + q == 0, False)
                for h, q in hq])
        CP_(R("O1", m0, m1), R("pd0", at + n, at + 2 * n))
        TS(R("s1", s0, s0 + n), R("pd0", at, at + n), -1.0e6, OP.is_lt, 8192.0, OP.mult)
        TT(R("s3", s0, s0 + n), R("pd0", at + n, at + 2 * n), R("s1", s0, s0 + n), OP.add)
        if t in LOCAL:
            return
        TS(R("O1", m1, m2), R("pd0", 0, 16), -1.0 / 256, OP.mult, col(WC), OP.add)
        dst = T.cores[voter(t)]; rid, pid, _se = topo.addr(dst); sem = ("a%d" if lo else "e%d") % t
        o1 = R("O1", m0, m2); l1 = R("L1", m0, m2)
        s = op("g", lambda: g.remote_dma(l1["ap"], o1["ap"], T.sem[sem], T.sem.sent, pid, rid, topo.mask(core, dst)), [], [o1], 500, sem="remote")
        nsent[0] += len(topo.engines(core, dst))
        if t == 0:
            masks([s])
        op(None, None, [l1], [], 0, lat=HOP1, sem=(sem, len(topo.engines(T.cores[voted(t)], core))), after=[s])

    def vote(t, lo, hi):
        m0 = 32 * t + lo // 8; m1 = m0 + (hi - lo) // 16; m2 = m1 + (hi - lo) // 16
        s0, s1 = lo // 16, hi // 16
        if t in LOCAL:
            co = R("O1", m0, m1); sums = R("k0" if hi == 256 else "k1", s0, s1)
            TT(R("E1", lo, hi), IN(COPY[t], W, co), R("VV", lo, hi), OP.is_equal)
            ACT(R("BC", lo, hi), IN("IO", W, co), AF.Identity, bias=UP)
            MM([(sums, into("SE", k), R("E1", lo + k, hi, 16), False, k == 15) for k in range(16)])
            TS(R("PS", s0 + 1, s1 + 1), sums, col(WC), OP.is_ge)
            TS(R("NP", s0, s1), sums, col(WC), OP.is_lt)
        else:
            co = R("L1", m0, m1)
            TT(R("E1", lo, hi), IN("Mi" if t == 0 else "Mf", W, co), R("VV", lo, hi), OP.is_equal)
            TS(R("NF", s0, s1), R("L1", m1, m2), -255.0, OP.add, 256.0, OP.mult)
            ACT(R("BC", lo, hi), IN("IO", W, co), AF.Identity, bias=UP)
            MM([(R("k0", s0, s1), into("SE", k), R("E1", lo + k, hi, 16), k == 0, k == 15) for k in range(16)])
            TT(R("PS", s0 + 1, s1 + 1), R("k0", s0, s1), R("NF", s0, s1), OP.is_ge)
            TT(R("NP", s0, s1), R("k0", s0, s1), R("NF", s0, s1), OP.is_lt)
        pre = R("k1" if hi == 256 else "pa", 32 + s0, 32 + s1)
        MM([(pre, R("NL"), R("PS", s0 + 1, s1 + 1), True, False), (pre, R("NU"), R("PS", s0, s1), False, True)])
        TT(R("QQ", s0, s1), R("NP", s0, s1), R("Q0", s0, s1), OP.mult)
        SCAN(R("SN", s0, s1), pre, R("Z16", s0, s1), R("SN", s0 - 1, s0) if lo else 767.0, OP.add, OP.add)
        TT(R("SL", s0, s1), R("SN", s0, s1), R("QQ", s0, s1), OP.subtract)
        j = CP_(R("SO", s0, s1), R("SL", s0, s1))
        CP_(IN("CC", 768, R("SO", s0, s1)), R("BC", lo, hi))
        ACT(IN("CV", 768, R("SO", s0, s1)), R("VU", lo, hi), AF.Silu)
        return j

    def ym(t):
        if t == 0:
            ACT(R("YM", 0, 1024, 4), R("M2"), AF.Identity)
        else:
            MM([(R("pd1", 512, 768), R("NI32"), R("M2"), True, False), (R("pd1", 512, 768), R("I"), R("LP"), False, True)])
            TT(R("NR"), R("pd1", 512, 768), lanes("Mf", t), OP.min)
            ACT(R("YM", t, 1024, 4), R("NR"), AF.Abs)

    def yx(t, src, less):
        ACT(R("X2"), lanes("Xb", t), AF.Identity, bias=256.0)
        ACT(R("pb", 256, 512), src, AF.Abs, bias=-(less + HI + 256))
        TT(R("X2"), R("pb", 256, 512), R("X2"), OP.min)
        ACT(R("YX", t, 1024, 4), R("X2"), AF.Abs, bias=-256.0)

    for t in range(RO):
        rho = owner(t)
        last = t == RO - 1
        if t == 0:
            for c in range(4):
                CP_(ch("OB", c), lanes("Mi", 0, c, c + 1))
                CP_(ch("M2", c), lanes("Mi", 0, c, c + 1))
                steps(t, c, ("pa", "pb")[c % 2])
        else:
            alike.append([len(ops)])
            for step, lo, hi, by, bank in FOLLOW:
                if step == 1:
                    follow(t, "O0", 256 * t - 256, "OA", lo, hi, by, bank)
                else:
                    follow(t, "OA", 0, "OB", lo, hi, by, bank)
            alike[-1] = list(range(alike[-1][0], len(ops)))
        if t in LOCAL:
            for u in range(1, t):
                CP_(R(COPY[t], 4 * u + voter(t), W, 16), R("N%d%d" % (u, t)))
        if last:
            DMA("y", T.PB[:], T.Xs[0:128:16, 0:W], [R("PB")], [R("Xs", 0, W)], "pi0", 2500)
            ACT(R("PB"), R("PB"), AF.Abs); ACT(R("PB"), R("PB"), AF.Identity, bias=WHOLE - BIG)
            ACT(R("PB"), R("PB"), AF.Relu, bias=1.0 - WHOLE); ACT(R("PB"), R("PB"), AF.Identity, bias=-1.0)
            DMA("y", T.F[0:128:16, 0:W], T.PB[:], [R("F", 0, W)], [R("PB")], "pi1", 2500)
        j = len(ops)
        for c in range(4):
            score(t, c)
        if t:
            alike[-1] += list(range(j, len(ops)))
        for lo, hi in parts(t):
            choose(t, lo, hi)
        if t:
            yx(t - 1, lanes("Xs", t - 1), 0.0)
        elif VSPLIT:
            IOTA(R("PT", 128 * SPLIT, 256 + 64 * SPLIT), [[0, 256 - 64 * SPLIT]], 0)
        TT(R("s3"), R("s3"), R("DC"), OP.min)
        smo = CP_(R("SMO"), R("s3"))
        if last:
            ym(t)
            out = DMA("y", T.ym[:], T.YM[:], [], [R("YM")], "oym", 4000)
        for lo, hi in parts(t):
            j = vote(t, lo, hi)
        ops[j]["after"].append(smo)
        if last:
            ops[j]["after"].append(out)
        for hf, nm in enumerate(("CC", "CV")):
            TT(ch("MK", hf), R(nm, 704, 768), ch("KH", 0), OP.mult)
            SCAN(ch("SC", hf), ch("RM", 0), ch("MK", hf), 0.0, OP.mult, OP.add)
        for s4 in range(4):
            TS(ch("N2", s4), R("CC", 704, 768), R("SC", 16 * s4 + 15, 16 * s4 + 16), OP.is_equal, 8192.0, OP.mult)
        SCAN(R("P2"), R("N2"), R("DM"), 0.0, OP.max, OP.min)
        TT(R("OF", 0, 4), R("SC", 15, 64, 16), R("P2", 63, 256, 64), OP.max)
        TT(R("OF", 4, 8), R("SC", 79, 128, 16), R("P2", 63, 256, 64), OP.max)
        lz = lambda q, lo, hi, t=t: R("LZ", 32 * t + 8 * q + lo, 32 * t + 8 * q + hi)
        TS(lz(rho, 0, 8), R("OF"), -UP, OP.add)
        others = [T.cores[(r + d) % N] for d in range(1, N)]
        others.sort(key=lambda x: topo.same_plane(topo.chip(core), topo.chip(x)))
        msk = topo.mask(core, others[0])
        for x in others:
            msk &= topo.mask(core, x)
        ne = bin(msk).count("1")
        tr = RemoteDMATransfer(dst_ids=[DstId(rid=topo.addr(x)[0], pnc=topo.addr(x)[1]) for x in others], dma_engine_mask=msk,
                               remote_sem=T.sem["b%d" % t], src=lz(rho, 0, 8)["ap"], dsts=[lz(rho, 0, 8)["ap"] for x in others])
        s = op("g", lambda tr=tr: g.remote_dma_fused([tr], local_sem=T.sem.sent), [], [lz(rho, 0, 8)], 500, sem="remote")
        nsent[0] += ne; marks.append(s)
        op(None, None, [lz(q, 0, 8) for q in range(N) if q != rho], [], 0, lat=HOP2, sem=("b%d" % t, ne * (N - 1)), after=[s])
        for u in LOCAL:
            if 0 < t < u:
                slot = "N%d%d" % (t, u); dst = T.cores[voted(u)]; rid, pid, _se = topo.addr(dst); n = len(topo.engines(core, dst))
                j = op("g", lambda slot=slot, a=(pid, rid, topo.mask(core, dst)): g.remote_dma(T[slot][:], T.OB[:], T.sem[slot], T.sem["s" + slot], *a),
                       [], [R("OB"), lz(0, 0, 32)], 500, lat=3000, sem=("s" + slot, n))
                ops[j]["own"] = True
                op(None, None, [R(slot)], [], 0, lat=4000, sem=(slot, len(topo.engines(T.cores[voter(u)], core))), after=[j])
        if t == 0 and 1 in LOCAL:
            sig0 = [RemoteDMATransfer(dst_ids=[DstId(rid=topo.addr(h)[0], pnc=topo.addr(h)[1])], dma_engine_mask=1 << topo.engines(core, h)[-1 - k],
                                      remote_sem=T.sem.go) for k, h in enumerate(near(core, r, T, topo))]
            j = op("g", lambda: g.remote_dma_fused(sig0, local_sem=T.sem.sent), [], [lz(0, 0, 32)], 500, sem="remote")
            nsent[0] += len(sig0)
            op(None, None, [R(COPY[1])], [], 0, lat=COPY_NS * 0.9, sem=("c1", landed(1)), after=[j])
        if t == 1 and COPY.get(RO - 1) == "Mi":
            ops[s]["wait"] = [o["id"] for o in ops if o["eng"] is not None and any(x[0] == "Mi" for x in o["rd"])]
            sig = [RemoteDMATransfer(dst_ids=[DstId(rid=topo.addr(h)[0], pnc=topo.addr(h)[1])], dma_engine_mask=1 << topo.engines(core, h)[-1 - k],
                                     remote_sem=T.sem.go) for k, h in enumerate(helpers(core, T, topo))]
            j = op("g", lambda: g.remote_dma_fused(sig, local_sem=T.sem.sent), [], [lz(0, 0, 32)], 500, sem="remote")
            nsent[0] += len(sig)
            op(None, None, [R("Mi")], [], 0, lat=2 * COPY_NS, sem=("c%d" % (RO - 1), landed(RO - 1)), after=[j])
        ACT(R("XC"), IN("Xs", W + 256, R("SMO")), AF.Identity, bias=-0.5)
        MM([(R("pd1", 0, 256), R("I32"), XA, True, False)]); MM([(R("pd1", 0, 256), R("I32"), R("XC"), False, True)])
        ACT(R("SY"), R("pd1", 0, 256), AF.Identity, bias=WHOLE, scale=0.5)
        if not last:
            ym(t)
            if t:
                ACT(lanes("Mf", t), R("M2"), AF.Identity)
            ACT(lanes("Xs", t), R("SY"), AF.Identity, bias=-WHOLE)
            for x in range(N):
                if t and x != r:
                    ACT(R("Xs", 4 * t + x, W, 16), R("Xs", 4 * t + x, W, 16), AF.Abs)
                ACT(R("Xs", 4 * t + 4 + x, W, 16), R("Xs", 4 * t + 4 + x, W, 16), AF.Identity, scale=-1.0)
            vrep(t + 1, [s])
        else:
            yx(t, R("SY"), WHOLE)
        add = 0.0 if last else BIG
        val = "BV" if last else "MV"
        for q in range(N - 1, -1, -1):
            if not last:
                ACT(ch("MV", q), IN("Mf", GW, lz(q, 4, 8)), AF.Identity, bias=BIG + q / 16.0)
            ACT(ch("BV", q), IN("IO", GW, lz(q, 4, 8)), AF.Identity, bias=add)
        TS(R("VF"), lz(0, 0, 32), 1.0 / 8192, OP.mult)
        for q in range(N - 1, -1, -1):
            CP_(IN("F", GW, lz(q, 0, 4)), ch(val, q))
        for q in range(N):
            if not last:
                ACT(ch("MC", q), IN("Mf", GW, lz(q, 0, 4)), AF.Identity, bias=BIG)
            ACT(ch("BC", q), IN("IO", GW, lz(q, 0, 4)), AF.Identity, bias=add)
        for q in range(1, N):
            TT(ch("LO", q), IN("F", GW, lz(q, 0, 4)), ch(val, q), OP.not_equal)
        for bank in ("pb", "pa")[:1 if last else 2]:
            MM([(R(bank, 4 * q, 4 * q + 4), R("I32"), R("VF", 8 * q + 4, 8 * q + 8), q == 0, bank == "pb" and q == N - 1) for q in range(N)])
        TS(R("VL"), R("pb", 0, 16), 8192.0, OP.mult)
        if not last:
            MM([(R("pa", 4, 16), ch("D16", k, 128), R("LO", 64 + k, 256, 16), False, k == 15) for k in range(16)])
        vval = "BC" if last else "MC"; diff = R("k0", 64, 256)
        MM([(diff, R("NI32"), R(vval, 64, 256), True, False)])
        if last:
            MM([(R("k0", 64, 192), R("NI"), R("ONE"), False, False), (R("k0", 192, 256), R("NI"), R("ONE", 0, 64), False, True)])
        else:
            MM([(diff, R("I32"), R("BV", 64, 256), False, True)])
        TT(R("LV", 64, 256), diff, R("LO", 64, 256), OP.mult)
        TT(IN("F", GW, R("VL")), R("LV"), R(vval), OP.add)
        if not last:
            TT(R("VM"), R("pa", 0, 16), R("DU"), OP.min)
            TS(R("VO"), R("VM"), 8192.0, OP.mult)
            for q in range(N - 1, -1, -1):
                ACT(IN("Xs", GW, lz(q, 0, 4)), ch("BV", q), AF.Silu)
            ACT(XA, lanes("Xs", t + 1), AF.Abs)
            ACT(R("LP"), XA, AF.Relu, bias=-(HI + 255) * 128, scale=128.0)
            ACT(IN("Xs", SW, R("VO")), R("BC"), AF.Silu)
            ACT(R("CN"), R("VM"), AF.Sign, bias=(W - 0.5) / 8192, scale=-1.0, acc=col(AF_))
            MM([(R("pb", 0, 1), R("ONE32"), col(AF_), True, True)])
            if t + 1 in LOCAL and A_BY == "s":
                ACT(col(A1), R("pb", 0, 1), AF.Identity, bias=255.625, scale=0.125); ACT(col(A2), R("pb", 0, 1), AF.Identity, bias=col(THM), scale=32768.0)
                ACT(col(A1), col(A1), AF.Identity, bias=WHOLE); ACT(col(A1), col(A1), AF.Identity, bias=-WHOLE)
                ACT(col(WC), col(A1), AF.Identity, bias=col(A2), scale=-262144.0)
            else:
                TS(R("AI", 0, 1), R("pb", 0, 1), 0.5, OP.mult, 1024.0, OP.add); TS(R("AI", 1, 2), R("AI", 0, 1), 3, OP.bitwise_and)
                if t + 1 in LOCAL:
                    TS(col(WC), R("AI", 1, 2), col(THL), OP.add, 65536.0, OP.mult)
                else:
                    TS(col(WC), R("AI", 1, 2), col(THC), OP.add, 256.0, OP.mult)
        else:
            TS(R("s4"), lz(r, 4, 8), float(W - 1), OP.min)
            ACT(R("XO", 0, 64), IN("Xb", W, R("s4")), AF.Identity)
            TS(R("UO"), lz(r, 4, 8), 0.25, OP.mult, 0.1 - r / 4.0, OP.add)
            ACT(R("XO", 64, 128), IN("YX", SW // 4, R("UO")), AF.Identity)
            TT(R("XO", 64, 128), R("XO", 64, 128), R("XO", 0, 64), OP.subtract)
            TT(R("XO", 64, 128), R("XO", 64, 128), R("LO", 64 * r, 256 if r == 0 else 64 * r + 64) if r else dict(R("LO"), ap=T.LO[:, 0:64], n=64), OP.mult)
            TT(IN("YX", SW // 4, R("UO")), R("XO", 64, 128), R("XO", 0, 64), OP.add)
            DMA("y", T.yp[:], T.F[0:128:16, 0:W], [], [R("F", 0, W)], "oyp", 2800)
            DMA("s", T.yx[:], T.YX[:, 0:1024], [], [R("YX", 0, 1024)], "oyx", 3400)

    return Q, ops, nsent[0], marks, alike


def emit(g, T, Q, ops, nsent, marks, alike, timed):
    def meet(a, b, banks):
        for (n, lo, hi) in a:
            for (m, l2, h2) in b:
                if n == m:
                    if banks and SCRATCH[n][0] == "psum":
                        if lo // 512 <= (h2 - 1) // 512 and l2 // 512 <= (hi - 1) // 512:
                            return True
                    elif not banks and lo < h2 and l2 < hi:
                        return True
        return False
    by = {}
    for o in ops:
        o["dep"] = {}
        names = set(x[0] for x in o["wr"] + o["rd"])
        seen = set()
        for nm in names:
            seen.update(by.get(nm, []))
            by.setdefault(nm, []).append(o["id"])
        for j in seen:
            e = ops[j]; same = e["eng"] == o["eng"] and e["sem"] is None and o["sem"] is None
            raw = meet(e["wr"], o["rd"], False)
            war = meet(e["rd"], o["wr"], False) or meet(e["wr"], o["wr"], False)
            if same:
                if e.get("free") and o.get("free"):
                    continue
                if raw or war or (o["eng"] == "p" and meet(e["wr"], o["wr"], True)):
                    o["dep"][j] = o["eng"] != "p" and (raw or WAIT_W)
            elif raw or war or meet(e["wr"] + e["rd"], o["wr"] + o["rd"], True):
                o["dep"][j] = True
        for j in o["after"]:
            o["dep"][j] = False
        for j in o.get("wait", []):
            o["dep"][j] = True
    n = len(ops)
    succ = [[] for _ in range(n)]
    for o in ops:
        for j in o["dep"]:
            succ[j].append(o["id"])

    def gap(j, o, m=0):
        return timed[m][j]["lat"] + COSTS[m][2] if o["dep"][j] or o["eng"] is None else 0.0
    anc = [0] * n; gp = []; nxt = [[] for _ in range(n)]
    for o in ops:
        far = 0
        for j in o["dep"]:
            far |= anc[j]
        gp.append([(j, ops[j]["cost"] + gap(j, o)) for j in o["dep"] if not far >> j & 1])
        for j in o["dep"]:
            far |= 1 << j
        anc[o["id"]] = far
        for j, w in gp[-1]:
            nxt[j].append((o["id"], o["cost"] + gap(j, o)))

    def place(seq, back):
        busy = {}
        st = [0.0] * n
        for i in seq:
            o = ops[i]
            t0 = o["lat"] if back else 0.0
            for j, w in (nxt[i] if back else gp[i]):
                if st[j] + w > t0:
                    t0 = st[j] + w
            if o["eng"] is not None:
                lst = busy.setdefault(o["eng"], [])
                lo, hi = 0, len(lst)
                while lo < hi:
                    mid = (lo + hi) // 2
                    if lst[mid][1] <= t0:
                        lo = mid + 1
                    else:
                        hi = mid
                while lo < len(lst) and t0 + o["cost"] > lst[lo][0]:
                    t0 = max(t0, lst[lo][1]); lo += 1
                lst.insert(lo, (t0, t0 + o["cost"]))
            st[i] = t0
        return st
    up = [0.0] * n
    for i in range(n - 1, -1, -1):
        up[i] = ops[i]["cost"] + max([w - ops[k]["cost"] + up[k] for k, w in nxt[i]] + [ops[i]["lat"]]) + 1e-3
    rnd = [12345]

    def rand():
        rnd[0] = (rnd[0] * 1103515245 + 12345) % 2147483648
        return rnd[0] / 2147483648

    def by_key(key):
        kk = list(key)
        for i in range(n):
            for j, w in gp[i]:
                if kk[j] >= kk[i]:
                    kk[i] = kk[j] + 1e-3
        return sorted(range(n), key=lambda i: (kk[i], i))
    cost = [o["cost"] for o in ops]; tail = [o["cost"] + o["lat"] for o in ops]; eng = [o["eng"] for o in ops]

    models = [([[(j, timed[m][j]["cost"] + gap(j, o, m)) for j, w in gp[o["id"]]] for o in ops], [o["cost"] for o in timed[m]],
               [o["cost"] + o["lat"] for o in timed[m]]) for m in range(len(timed))]

    def run(seq, base=None, last=None):
        res = [once(seq, base and base[m], last, *models[m]) for m in range(len(models))]
        return sum(x[0] for x in res) / len(res), res[0][1], res

    def once(seq, base, last, gp, cost, tail):
        st, prev = ([0.0] * n, {}) if base is None else (list(base[1]), dict(base[4]))
        by = {}
        for i in seq:
            t0 = 0.0; b = -1
            for j, w in gp[i]:
                if st[j] + w > t0:
                    t0 = st[j] + w; b = j
            e = eng[i]
            if e is not None:
                p = prev.get(e)
                if p is not None and st[p] + cost[p] > t0:
                    t0 = st[p] + cost[p]; b = -2 - p
                prev[e] = i
            st[i] = t0; by[i] = b
        z = max(seq, key=lambda i: st[i] + tail[i]) if last is None else last
        return st[z] + tail[z], st, by, z, prev

    def better(seq, tries, slack, base=None, last=None):
        now = run(seq, base, last); best = (now, seq); m = len(seq)
        for it in range(tries):
            span = now[0]; by, z = now[2][it % len(models)][2:4]
            pairs = []
            while z in by:
                b = by[z]
                if b <= -2:
                    b = -2 - b
                    if b in by:
                        pairs.append((b, z))
                z = b
            if not pairs:
                break
            u, v = pairs[int(rand() * len(pairs))]
            if anc[v] >> u & 1:
                continue
            a, z = seq.index(u), seq.index(v)
            ahead = rand() < 0.5
            for more in range(int(rand() * rand() * 6)):
                k = a - 1 if ahead else z + 1
                while 0 <= k < m and eng[seq[k]] != eng[v]:
                    k += -1 if ahead else 1
                if not 0 <= k < m or (anc[v] >> seq[k] & 1 if ahead else anc[seq[k]] >> u & 1):
                    break
                a, z = (k, z) if ahead else (a, k)
            mid = seq[a:z + 1]
            if ahead:
                mid = [i for i in mid if i == v or anc[v] >> i & 1] + [i for i in mid if not (i == v or anc[v] >> i & 1)]
            else:
                mid = [i for i in mid if not (i == u or anc[i] >> u & 1)] + [i for i in mid if i == u or anc[i] >> u & 1]
            new = seq[:a] + mid + seq[z + 1:]
            res = run(new, base, last)
            if res[0] <= span + slack * (1.0 - it / tries) * rand():
                now = res; seq = new
                if it % 8 == 0:
                    seq = sorted(seq, key=lambda i: res[1][i])
                if res[0] < best[0][0]:
                    best = (res, seq)
        return best[1]

    def tight(seq):
        st = place(seq, False)
        return sorted(seq, key=lambda i: st[i])
    if "key" not in PLAN:
        cur = place(sorted(range(n), key=lambda i: (-up[i], i)), False)
        for it in range(6):
            bk = place(sorted(range(n), key=lambda i: (-(cur[i] + cost[i]), -i)), True)
            cur = place(by_key([-bk[i] - cost[i] for i in range(n)]), False)
        seq = by_key(cur)
        for turn in range(2):
            for k in range(len(marks)):
                a = seq.index(marks[k - 1]) + 1 if k else 0; z = seq.index(marks[k]) + 1
                head = run(seq[:a]) if a else None
                mid = better(seq[a:z], TRIES // 8, SLACK / (1 + 2 * turn), head and head[2], marks[k])
                seq = min(tight(seq[:a] + mid + seq[z:]), seq[:a] + mid + seq[z:], key=lambda x: run(x)[0])
            st = run(seq)[1]
            b = min(alike, key=lambda x: st[x[-1]] - st[x[0]])
            for x in alike:
                key = list(st)
                for i, j in zip(x, b):
                    key[i] = st[x[0]] + st[j] - st[b[0]]
                new = better(tight(by_key(key)), TRIES // 100, SLACK / 10)
                if run(new)[0] < run(seq)[0]:
                    seq = new; st = run(seq)[1]
    else:
        seq = by_key(PLAN["key"])
    best = run(better(seq, TRIES // 20, SLACK / 10))
    PLAN["key"] = best[1]; PLAN["span"] = best[0]
    start = best[1]
    end = [start[i] + ops[i]["cost"] for i in range(n)]
    order = sorted(range(n), key=lambda i: (start[i], i))
    cnt = {"v": 0, "s": 0, "p": 0, "g": 0}
    for i in order:
        o = ops[i]
        o["inc"] = o["sem"] is None and any(ops[k]["dep"][i] for k in succ[i])
        if o["sem"] is None:
            cnt[o["eng"]] += o["inc"]
            o["sig"] = ("c" + o["eng"], cnt[o["eng"]])
        else:
            o["sig"] = o["sem"]
    known = {e: {} for e in Q}
    for i in order:
        o = ops[i]
        if o["eng"] is None:
            o["kn"] = {}
            continue
        kn = known[o["eng"]]
        need = sorted((j for j, w in o["dep"].items() if w), key=lambda j: -end[j])
        for j in need:
            sm, val = ops[j]["sig"]
            if kn.get(sm, 0) < val:
                Q[o["eng"]].wait_ge(T.sem[sm], int(val)); kn[sm] = val
                for s2, v2 in ops[j]["kn"].items():
                    kn[s2] = max(kn.get(s2, 0), v2)
        o["kn"] = dict(kn)
        h = o["fn"]()
        if o["sem"] is None:
            if o["inc"]:
                h.then_inc(T.sem[o["sig"][0]], 1)
        elif o["sem"] != "remote" and not o.get("own"):
            h.then_inc(T.sem[o["sem"][0]], 16)
    for e in cnt:
        if cnt[e]:
            g.wait_ge(T.sem["c" + e], int(cnt[e]))
    for o in ops:
        if o["sem"] not in (None, "remote"):
            g.wait_ge(T.sem[o["sem"][0]], int(o["sem"][1]))
    g.wait_ge(T.sem.sent, int(nsent))
    return max(end[i] + ops[i]["lat"] for i in range(n))
